import numpy as np
import ml_dtypes


def mxq(x, axis, fmt="e4m3"):
    dtype, down = {"e4m3": (ml_dtypes.float8_e4m3fn, 7), "e5m2": (ml_dtypes.float8_e5m2, 14)}[fmt]
    v = np.moveaxis(np.asarray(x, np.float32).astype(ml_dtypes.bfloat16).astype(np.float64), axis, -1)
    blocks = v.reshape(v.shape[:-1] + (-1, 32))
    amax = np.abs(blocks).max(-1, keepdims=True)
    byte = np.maximum(np.where(amax > 0, np.frexp(amax)[1] - 1 + 127, 0) - down, 1)
    scale = np.exp2(byte - 127.0)
    codes = (blocks / scale).astype(np.float32).astype(dtype).astype(np.float64)
    return np.moveaxis((codes * scale).reshape(v.shape), -1, axis)


WIDE = False


def mx_kscale(k):
    if not WIDE:
        return np.ones(k)
    levels = np.array([10, -10, 5, -5, 0])
    if k % 512:
        return np.exp2(np.random.permutation(np.resize(levels, k // 32))).repeat(32)
    a = np.empty((k // 512, 16))
    for p in range(k // 512):
        a[p, :8] = np.random.permutation(np.resize(levels, 8))
        for g in range(8):
            far = levels[np.abs(levels - a[p, g]) >= 10]
            a[p, g + 8] = far[np.random.randint(len(far))]
    return np.exp2(a.ravel()).repeat(32)


def f64(x):
    return np.asarray(x).astype(np.float64)


def striped(idx):
    return np.tile(idx.reshape(-1, 16).T, (8, 1)).astype(np.uint16)


def unstriped(offs):
    return offs[:16].T.reshape(-1).astype(np.int64)


E2M1 = np.array([0.0, 0.5, 1.0, 1.5, 2.0, 3.0, 4.0, 6.0, -0.0, -0.5, -1.0, -1.5, -2.0, -3.0, -4.0, -6.0])


def pack_weight(w, fmt):
    k, n = w.shape
    w = f64(np.asarray(w, np.float32).astype(ml_dtypes.bfloat16)).reshape(k // 32, 32, n)
    amax = np.abs(w).max(1)
    if fmt == "e4m3":
        byte = np.frexp(amax)[1] - 1 + 127 - 7
    else:
        mant, ex = np.frexp(amax / 6.0)
        byte = np.where(mant > 0.5, ex, ex - 1) + 127
    byte = np.clip(np.where(amax > 0, byte, 1), 1, 254)
    scaled = (w * np.exp2(127.0 - byte)[:, None, :]).reshape(k, n).astype(np.float32)
    by_word = np.ascontiguousarray(scaled.reshape(k // 512, 128, 4, n).transpose(0, 1, 3, 2))
    if fmt == "e4m3":
        words = by_word.astype(ml_dtypes.float8_e4m3fn).view(np.uint8)
    else:
        c = by_word.astype(ml_dtypes.float4_e2m1fn).view(np.uint8) & 0xF
        words = (c[..., 0::2] | (c[..., 1::2] << 4)).reshape(k // 512, 128, 2 * n)
    return np.ascontiguousarray(words), np.ascontiguousarray(byte.astype(np.uint8).reshape(k // 512, 16, n))


def unpack_weight(words, scales, fmt):
    g, _, n = scales.shape
    words = np.ascontiguousarray(words).reshape(g, 128, n, -1)
    if fmt == "e4m3":
        vals = words.view(ml_dtypes.float8_e4m3fn).astype(np.float64)
    else:
        nib = np.empty((g, 128, n, 4), np.uint8)
        nib[..., 0::2] = words & 0xF
        nib[..., 1::2] = words >> 4
        vals = E2M1[nib]
    vals = vals * np.repeat(np.exp2(scales.astype(np.float64) - 127.0), 8, axis=1)[..., None]
    return vals.transpose(0, 1, 3, 2).reshape(g * 512, n)


def gelu(v):
    return 0.5 * v * (1.0 + np.tanh(np.sqrt(2.0 / np.pi) * (v + 0.044715 * v**3)))


K, T, S, P, H, N = 1024, 2048, 1024, 512, 1024, 512

def setup_inputs():
    n = np.random.standard_normal
    s = mx_kscale(K)[:, None]
    u = mx_kscale(H)[:, None]
    tab_words, tab_scales = pack_weight(n((K, T)) * s, "e4m3")
    w4_words, w4_scales = pack_weight(2.0 * n((H, N)) / np.sqrt(H) / u, "e2m1")
    pairs = np.random.permutation(S)
    return {
        "tab_words": tab_words,
        "tab_scales": tab_scales,
        "offs": striped(np.random.permutation(T)[:S]),
        "pos1": striped(pairs[:P]),
        "pos2": striped(pairs[P:]),
        "w1": (n((K, H)) / np.sqrt(K) / s).astype(np.float32),
        "gain": (np.exp(0.3 * n(H)) * u[:, 0]).astype(np.float32),
        "w4_words": w4_words,
        "w4_scales": w4_scales,
    }

def reference(tab_words, tab_scales, offs, pos1, pos2, w1, gain, w4_words, w4_scales):
    v = unpack_weight(tab_words, tab_scales, "e4m3")[:, unstriped(offs)]
    q1 = mxq(f64(w1), 0, "e4m3")
    h = q1.T @ v
    a = h[:, unstriped(pos1)]
    b = h[:, unstriped(pos2)]
    d = a - b
    z = f64(gain)[:, None] * (d / (1.0 + d * d))
    zq = mxq(z, 0, "e4m3")
    w4 = unpack_weight(w4_words, w4_scales, "e2m1")
    return w4.T @ zq

@@ -1,0 +1,295 @@
+from contextlib import ExitStack
+
+import concourse.mybir as mybir
+
+K, T, S, NP, H, N = 1024, 2048, 1024, 512, 1024, 512
+FLOPS = 2 * K * H * S + 2 * H * N * NP
+
+F32 = mybir.dt.float32
+BF16 = mybir.dt.bfloat16
+I32 = mybir.dt.int32
+U32 = mybir.dt.uint32
+U16 = mybir.dt.uint16
+U8 = mybir.dt.uint8
+FP8X4 = mybir.dt.float8_e4m3fn_x4
+FP4X4 = mybir.dt.float4_e2m1fn_x4
+ALU = mybir.AluOpType
+ACT = mybir.ActivationFunctionType
+
+P = 128
+TINY = 2.0 ** -126
+SUB_ON_GPSIMD = True
+CAST_B1_ON_GPSIMD = True
+
+
+def tile_list_robust_station_increments_kernel(
+    tc, tab_words, tab_scales, offs, pos1, pos2, w1, gain, w4_words, w4_scales, out
+):
+    nc = tc.nc
+    with ExitStack() as ctx:
+        keep = ctx.enter_context(tc.tile_pool(name="keep", bufs=1))
+        ring = ctx.enter_context(tc.tile_pool(name="ring", bufs=4))
+        psum = ctx.enter_context(tc.psum_pool(name="psum", bufs=8))
+
+        offs_t = keep.tile([P, S // 16], U16, name="offs_t")
+        pos1_t = keep.tile([P, NP // 16], U16, name="pos1_t")
+        pos2_t = keep.tile([P, NP // 16], U16, name="pos2_t")
+        tabw = [keep.tile([P, T], I32, name=f"tabw{a}", align_bytes=64) for a in range(2)]
+        tabs = keep.tile([P, T // 4], I32, name="tabs", align_bytes=64)
+        vw = [keep.tile([P, S], U32, name=f"vw{a}", align_bytes=64) for a in range(2)]
+        vs = keep.tile([P, S], U8, name="vs", align_bytes=64)
+        w4w = keep.tile([P, 2, 2 * N // 4], I32, name="w4w", align_bytes=64)
+        w4s = keep.tile([P, 2, N // 4], I32, name="w4s", align_bytes=64)
+        g = keep.tile([P, 2, 4], F32, name="g")
+        gabs = keep.tile([P, 8], F32, name="gabs")
+        gsign = keep.tile([P, 8], F32, name="gsign")
+        gclamp = keep.tile([P, 8], F32, name="gclamp")
+        ginv = keep.tile([P, 8], F32, name="ginv")
+        warm_in = keep.tile([P, 1], F32, name="warm_in")
+        warm_out = keep.tile([P, 1], F32, name="warm_out")
+
+        nc.vector.memset(tabs[:], 0)
+        nc.gpsimd.memset(warm_in[:], 1.0)
+        nc.scalar.activation(warm_out[:], warm_in[:], ACT.Abs_reciprocal_sqrt)
+        nc.vector.memset(w4s[:], 0)
+
+        raw = {}
+        for b in range(2):
+            for a in range(2):
+                for hf in range(2):
+                    raw[b, a, hf] = keep.tile([P, 4, 256], F32, name=f"raw{b}{a}{hf}")
+
+        def load_w1(b, a, hf):
+            c0 = 512 * b + 256 * hf
+            nc.sync.dma_start(
+                out=raw[b, a, hf][:],
+                in_=w1[512 * a : 512 * (a + 1), c0 : c0 + 256].rearrange("(p j) c -> p j c", j=4),
+            )
+
+        def load_tab(a):
+            nc.sync.dma_start(out=tabw[a][:], in_=tab_words[a].rearrange("p t i -> p (t i)").bitcast(I32))
+
+        nc.sync.dma_start(offs_t[:], offs)
+        load_tab(0)
+        ts32 = tab_scales.bitcast(I32)
+        for q in range(4):
+            nc.scalar.dma_start(out=tabs[32 * q : 32 * q + 8, :], in_=ts32[:, 4 * q : 4 * q + 4, :])
+        nc.scalar.dma_start(out=g[:], in_=gain.rearrange("(b p t) -> p b t", b=2, t=4))
+        load_w1(0, 0, 0)
+        load_w1(0, 0, 1)
+        load_tab(1)
+        load_w1(0, 1, 0)
+        load_w1(0, 1, 1)
+        nc.sync.dma_start(pos1_t[:], pos1)
+        nc.sync.dma_start(pos2_t[:], pos2)
+        for a in range(2):
+            for hf in range(2):
+                load_w1(1, a, hf)
+        nc.sync.dma_start(out=w4w[:], in_=w4_words.bitcast(I32).rearrange("a p c -> p a c"))
+        w4s32 = w4_scales.bitcast(I32)
+        for q in range(4):
+            nc.sync.dma_start(
+                out=w4s[32 * q : 32 * q + 4, :, :],
+                in_=w4s32[:, 4 * q : 4 * q + 4, :].rearrange("a i c -> i a c"),
+            )
+
+        gflat = g[:].rearrange("p b t -> p (b t)")
+        nc.scalar.activation(gabs[:], gflat, ACT.Abs)
+        nc.scalar.activation(gsign[:], gflat, ACT.Sign)
+        nc.vector.tensor_scalar(gclamp[:], gabs[:], TINY, None, ALU.max)
+        nc.vector.reciprocal(ginv[:], gclamp[:])
+
+        grouped = {}
+        codes = {}
+        scales = {}
+        for b in range(2):
+            for a in range(2):
+                grouped[b, a] = keep.tile([P, 2048], BF16, name=f"grp{b}{a}", align_bytes=64)
+                codes[b, a] = keep.tile([P, 512], U32, name=f"wc{b}{a}", align_bytes=64)
+                scales[b, a] = keep.tile([P, 512], U8, name=f"ws{b}{a}", align_bytes=64)
+
+        def cast(b, a, hf, eng):
+            dst = grouped[b, a][:].rearrange("p (t m j) -> p m t j", t=4, j=4)[:, 64 * hf : 64 * (hf + 1), :, :]
+            src = raw[b, a, hf][:].rearrange("p j (m t) -> p m t j", t=4)
+            if eng == "v":
+                nc.vector.tensor_copy(out=dst, in_=src)
+            elif eng == "s":
+                nc.scalar.copy(out=dst, in_=src)
+            else:
+                nc.gpsimd.tensor_scalar(dst, src, 1.0, 0.0, ALU.mult, ALU.add)
+
+        def quant_w(b, a, t0, t1):
+            nc.vector.quantize_mx(
+                out=codes[b, a][:, 128 * t0 : 128 * t1].bitcast(FP8X4),
+                scales=scales[b, a][:, 128 * t0 : 128 * t1],
+                in_=grouped[b, a][:, 512 * t0 : 512 * t1],
+            )
+
+        nc.vector.tensor_copy(out=vw[0][:], in_=tabw[0][:].bitcast(U32).indirect(offs_t[:]))
+        nc.vector.tensor_copy(out=vs[:], in_=tabs[:].bitcast(U8).indirect(offs_t[:]))
+        cast(0, 0, 0, "s")
+        cast(0, 0, 1, "s")
+        quant_w(0, 0, 0, 4)
+        nc.vector.tensor_copy(out=vw[1][:], in_=tabw[1][:].bitcast(U32).indirect(offs_t[:]))
+        cast(0, 1, 0, "s")
+        cast(0, 1, 1, "v")
+        quant_w(0, 1, 0, 1)
+
+        h = {}
+        accs = {}
+
+        def h_pass(b, t, hf, a):
+            if a == 0:
+                accs[b, t, hf] = psum.tile([P, 512], F32, name="acc")
+            cols = slice(512 * hf, 512 * (hf + 1))
+            nc.tensor.matmul_mx(
+                out=accs[b, t, hf][:],
+                lhsT=codes[b, a][:, 128 * t : 128 * (t + 1)].bitcast(FP8X4),
+                lhsT_scale=scales[b, a][:, 128 * t : 128 * (t + 1)],
+                rhs=vw[a][:, cols].bitcast(FP8X4),
+                rhs_scale=vs[4 * a :, cols],
+                start=(a == 0),
+                stop=(a == 1),
+            )
+
+        def make_h(b, t):
+            h[b, t] = keep.tile([P, S], F32, name=f"h{b}{t}")
+            i = 4 * b + t
+            for hf in range(2):
+                cols = slice(512 * hf, 512 * (hf + 1))
+                if b == 1:
+                    h_pass(b, t, hf, 0)
+                h_pass(b, t, hf, 1)
+                acc = accs[b, t, hf]
+                if i == 0 and hf == 1:
+                    nc.vector.tensor_scalar(h[b, t][:, cols], acc[:], gsign[:, i : i + 1], None, ALU.mult)
+                else:
+                    nc.scalar.activation(h[b, t][:, cols], acc[:], ACT.Copy, scale=gsign[:, i : i + 1])
+
+        for t in range(4):
+            for hf in range(2):
+                h_pass(0, t, hf, 0)
+        make_h(0, 0)
+        quant_w(0, 1, 1, 2)
+        quant_w(0, 1, 2, 4)
+        for t in range(1, 4):
+            make_h(0, t)
+        eng = "g" if CAST_B1_ON_GPSIMD else "s"
+        for a in range(2):
+            for hf in range(2):
+                cast(1, a, hf, eng)
+
+        chunks = [(0, 0, 512), (1, 0, 256), (1, 256, 128), (1, 384, 128)]
+        dt = {}
+        wt = {}
+        for ci, (b, c0, n) in enumerate(chunks):
+            dt[ci] = keep.tile([P, 4, n], F32, name=f"d{ci}")
+            wt[ci] = keep.tile([P, 4, n], F32, name=f"w{ci}")
+        zb = [keep.tile([P, 4 * NP], BF16, name=f"zb{b}", align_bytes=64) for b in range(2)]
+        zc = [keep.tile([P, NP], U32, name=f"zc{b}", align_bytes=64) for b in range(2)]
+        zs = [keep.tile([P, NP], U8, name=f"zs{b}", align_bytes=64) for b in range(2)]
+
+        def unit(ci, t):
+            b, c0, n = chunks[ci]
+            i = 4 * b + t
+            ga = ring.tile([P, 512], F32, name="ga", bufs=6)
+            gb = ring.tile([P, 512], F32, name="gb", bufs=6)
+            lc = slice(c0 // 16, (c0 + n) // 16)
+            nc.vector.tensor_copy(out=ga[:, :n], in_=h[b, t][:].indirect(pos1_t[:, lc]))
+            nc.vector.tensor_copy(out=gb[:, :n], in_=h[b, t][:].indirect(pos2_t[:, lc]))
+            d = dt[ci][:, t, :]
+            if SUB_ON_GPSIMD and ci < 3:
+                nc.gpsimd.tensor_tensor(d, ga[:, :n], gb[:, :n], ALU.subtract)
+            else:
+                nc.vector.tensor_tensor(d, ga[:, :n], gb[:, :n], ALU.subtract)
+            sq = ring.tile([P, 512], F32, name="sq")
+            rs = ring.tile([P, 512], F32, name="rs")
+            nc.scalar.activation(sq[:, :n], d, ACT.Square)
+            nc.scalar.activation(
+                rs[:, :n], sq[:, :n], ACT.Abs_reciprocal_sqrt, bias=ginv[:, i : i + 1], scale=ginv[:, i : i + 1]
+            )
+            nc.scalar.activation(wt[ci][:, t, :], rs[:, :n], ACT.Square)
+
+        def mult(ci, lo, hi):
+            b, c0, n = chunks[ci]
+            dst = zb[b][:, 4 * (c0 + lo) : 4 * (c0 + hi)].rearrange("p (c i t) -> p c t i", i=4, t=4)
+            d = dt[ci][:, :, lo:hi].rearrange("p t (c i) -> p c t i", i=4)
+            w = wt[ci][:, :, lo:hi].rearrange("p t (c i) -> p c t i", i=4)
+            nc.vector.tensor_tensor(dst, d, w, ALU.mult)
+
+        def quant_z(b, lo, hi):
+            nc.vector.quantize_mx(
+                out=zc[b][:, lo:hi].bitcast(FP8X4), scales=zs[b][:, lo:hi], in_=zb[b][:, 4 * lo : 4 * hi]
+            )
+
+        w4u = w4w[:].bitcast(U8)
+        w4su = w4s[:].bitcast(U8)
+        out_v = out.rearrange("(i q) p -> q i p", q=P)
+
+        def out_pass(acc, i, c, b):
+            cols = slice(128 * c, 128 * (c + 1))
+            nc.tensor.matmul_mx(
+                out=acc,
+                lhsT=w4u[:, b, 256 * i : 256 * (i + 1)].bitcast(FP4X4),
+                lhsT_scale=w4su[:, b, 128 * i : 128 * (i + 1)],
+                rhs=zc[b][:, cols].bitcast(FP8X4),
+                rhs_scale=zs[b][:, cols],
+                start=(b == 0),
+                stop=(b == 1),
+            )
+
+        def product(c, res, lo):
+            acc = psum.tile([P, 4, 128], F32, name="acc")
+            for i in range(4):
+                for b in range(2):
+                    out_pass(acc[:, i, :], i, c, b)
+            nc.scalar.copy(out=res[:, :, lo : lo + 128], in_=acc[:])
+
+        res0 = keep.tile([P, 4, 256], F32, name="res0")
+        res1 = keep.tile([P, 4, 128], F32, name="res1")
+        res2 = keep.tile([P, 4, 128], F32, name="res2")
+
+        unit(0, 0)
+        unit(0, 1)
+        quant_w(1, 0, 0, 4)
+        quant_w(1, 1, 0, 4)
+        for t in range(4):
+            make_h(1, t)
+        unit(0, 2)
+        unit(0, 3)
+        unit(1, 0)
+        unit(1, 1)
+        unit(1, 2)
+        mult(0, 0, 256)
+        unit(1, 3)
+        mult(0, 256, 512)
+        unit(2, 0)
+        quant_z(0, 0, 512)
+        unit(2, 1)
+        unit(2, 2)
+        mult(1, 0, 256)
+        unit(2, 3)
+        quant_z(1, 0, 256)
+        product(0, res0, 0)
+        product(1, res0, 128)
+        nc.sync.dma_start(out=out_v[:, :, 0:256], in_=res0[:])
+        unit(3, 0)
+        unit(3, 1)
+        mult(2, 0, 128)
+        unit(3, 2)
+        quant_z(1, 256, 384)
+        product(2, res1, 0)
+        nc.sync.dma_start(out=out_v[:, :, 256:384], in_=res1[:])
+        last = [psum.tile([P, 128], F32, name="acc") for i in range(4)]
+        for i in range(4):
+            out_pass(last[i][:], i, 3, 0)
+        unit(3, 3)
+        mult(3, 0, 128)
+        quant_z(1, 384, 512)
+        for i in range(4):
+            out_pass(last[i][:], i, 3, 1)
+            if i % 2 == 0:
+                nc.scalar.copy(out=res2[:, i, :], in_=last[i][:])
+            else:
+                nc.vector.tensor_copy(out=res2[:, i, :], in_=last[i][:])
+                nc.sync.dma_start(out=out_v[:, i - 1 : i + 1, 384:512], in_=res2[:, i - 1 : i + 1, :])

@@ -18,8 +18,10 @@ ACT = mybir.ActivationFunctionType
 
 P = 128
 TINY = 2.0 ** -126
-SUB_ON_GPSIMD = True
-CAST_B1_ON_GPSIMD = True
+RA = [1, 2, 3]
+HB = 3
+CHUNKS = [(0, 0, 256), (0, 256, 256), (1, 0, 256), (1, 256, 128), (1, 384, 128)]
+SLOT = [0, 1024]
 
 
 def tile_list_robust_station_increments_kernel(
@@ -28,8 +30,9 @@ def tile_list_robust_station_increments_kernel(
     nc = tc.nc
     with ExitStack() as ctx:
         keep = ctx.enter_context(tc.tile_pool(name="keep", bufs=1))
-        ring = ctx.enter_context(tc.tile_pool(name="ring", bufs=4))
-        psum = ctx.enter_context(tc.psum_pool(name="psum", bufs=8))
+        reuse = ctx.enter_context(tc.tile_pool(name="reuse", bufs=1))
+        hps = ctx.enter_context(tc.psum_pool(name="hps", bufs=HB))
+        psum = ctx.enter_context(tc.psum_pool(name="psum", bufs=8 - HB))
 
         offs_t = keep.tile([P, S // 16], U16, name="offs_t")
         pos1_t = keep.tile([P, NP // 16], U16, name="pos1_t")
@@ -73,11 +76,11 @@ def tile_list_robust_station_increments_kernel(
         load_tab(0)
         ts32 = tab_scales.bitcast(I32)
         for q in range(4):
-            nc.scalar.dma_start(out=tabs[32 * q : 32 * q + 8, :], in_=ts32[:, 4 * q : 4 * q + 4, :])
-        nc.scalar.dma_start(out=g[:], in_=gain.rearrange("(b p t) -> p b t", b=2, t=4))
+            nc.sync.dma_start(out=tabs[32 * q : 32 * q + 8, :], in_=ts32[:, 4 * q : 4 * q + 4, :])
+        load_tab(1)
+        nc.sync.dma_start(out=g[:], in_=gain.rearrange("(b p t) -> p b t", b=2, t=4))
         load_w1(0, 0, 0)
         load_w1(0, 0, 1)
-        load_tab(1)
         load_w1(0, 1, 0)
         load_w1(0, 1, 1)
         nc.sync.dma_start(pos1_t[:], pos1)
@@ -104,11 +107,14 @@ def tile_list_robust_station_increments_kernel(
         scales = {}
         for b in range(2):
             for a in range(2):
-                grouped[b, a] = keep.tile([P, 2048], BF16, name=f"grp{b}{a}", align_bytes=64)
                 codes[b, a] = keep.tile([P, 512], U32, name=f"wc{b}{a}", align_bytes=64)
                 scales[b, a] = keep.tile([P, 512], U8, name=f"ws{b}{a}", align_bytes=64)
 
         def cast(b, a, hf, eng):
+            if hf == 0:
+                grouped[b, a] = reuse.tile(
+                    [P, 2048], BF16, name=f"grp{b}{a}", align_bytes=64, offset=4096 * ((a + b + 1) % 2)
+                )
             dst = grouped[b, a][:].rearrange("p (t m j) -> p m t j", t=4, j=4)[:, 64 * hf : 64 * (hf + 1), :, :]
             src = raw[b, a, hf][:].rearrange("p j (m t) -> p m t j", t=4)
             if eng == "v":
@@ -127,20 +133,14 @@ def tile_list_robust_station_increments_kernel(
 
         nc.vector.tensor_copy(out=vw[0][:], in_=tabw[0][:].bitcast(U32).indirect(offs_t[:]))
         nc.vector.tensor_copy(out=vs[:], in_=tabs[:].bitcast(U8).indirect(offs_t[:]))
-        cast(0, 0, 0, "s")
-        cast(0, 0, 1, "s")
-        quant_w(0, 0, 0, 4)
         nc.vector.tensor_copy(out=vw[1][:], in_=tabw[1][:].bitcast(U32).indirect(offs_t[:]))
-        cast(0, 1, 0, "s")
-        cast(0, 1, 1, "v")
-        quant_w(0, 1, 0, 1)
 
         h = {}
         accs = {}
 
         def h_pass(b, t, hf, a):
             if a == 0:
-                accs[b, t, hf] = psum.tile([P, 512], F32, name="acc")
+                accs[b, t, hf] = hps.tile([P, 512], F32, name="hacc")
             cols = slice(512 * hf, 512 * (hf + 1))
             nc.tensor.matmul_mx(
                 out=accs[b, t, hf][:],
@@ -157,8 +157,7 @@ def tile_list_robust_station_increments_kernel(
             i = 4 * b + t
             for hf in range(2):
                 cols = slice(512 * hf, 512 * (hf + 1))
-                if b == 1:
-                    h_pass(b, t, hf, 0)
+                h_pass(b, t, hf, 0)
                 h_pass(b, t, hf, 1)
                 acc = accs[b, t, hf]
                 if i == 0 and hf == 1:
@@ -166,56 +165,54 @@ def tile_list_robust_station_increments_kernel(
                 else:
                     nc.scalar.activation(h[b, t][:, cols], acc[:], ACT.Copy, scale=gsign[:, i : i + 1])
 
-        for t in range(4):
-            for hf in range(2):
-                h_pass(0, t, hf, 0)
-        make_h(0, 0)
-        quant_w(0, 1, 1, 2)
-        quant_w(0, 1, 2, 4)
-        for t in range(1, 4):
-            make_h(0, t)
-        eng = "g" if CAST_B1_ON_GPSIMD else "s"
-        for a in range(2):
-            for hf in range(2):
-                cast(1, a, hf, eng)
-
-        chunks = [(0, 0, 512), (1, 0, 256), (1, 256, 128), (1, 384, 128)]
+        engs = {"v": nc.vector, "g": nc.gpsimd}
+        chunks = CHUNKS
+        pairs = {}
         dt = {}
         wt = {}
-        for ci, (b, c0, n) in enumerate(chunks):
-            dt[ci] = keep.tile([P, 4, n], F32, name=f"d{ci}")
-            wt[ci] = keep.tile([P, 4, n], F32, name=f"w{ci}")
         zb = [keep.tile([P, 4 * NP], BF16, name=f"zb{b}", align_bytes=64) for b in range(2)]
         zc = [keep.tile([P, NP], U32, name=f"zc{b}", align_bytes=64) for b in range(2)]
         zs = [keep.tile([P, NP], U8, name=f"zs{b}", align_bytes=64) for b in range(2)]
 
-        def unit(ci, t):
+        def gath(ci, t):
             b, c0, n = chunks[ci]
-            i = 4 * b + t
-            ga = ring.tile([P, 512], F32, name="ga", bufs=6)
-            gb = ring.tile([P, 512], F32, name="gb", bufs=6)
-            lc = slice(c0 // 16, (c0 + n) // 16)
-            nc.vector.tensor_copy(out=ga[:, :n], in_=h[b, t][:].indirect(pos1_t[:, lc]))
-            nc.vector.tensor_copy(out=gb[:, :n], in_=h[b, t][:].indirect(pos2_t[:, lc]))
-            d = dt[ci][:, t, :]
-            if SUB_ON_GPSIMD and ci < 3:
-                nc.gpsimd.tensor_tensor(d, ga[:, :n], gb[:, :n], ALU.subtract)
+            if t == 0:
+                dt[ci] = keep.tile([P, 4, n], F32, name=f"d{ci}")
+                wt[ci] = keep.tile([P, 4, n], F32, name=f"w{ci}")
+            if n == 256:
+                base = 8192 * ((ci + 1) % 2) + 2048 * t
             else:
-                nc.vector.tensor_tensor(d, ga[:, :n], gb[:, :n], ALU.subtract)
-            sq = ring.tile([P, 512], F32, name="sq")
-            rs = ring.tile([P, 512], F32, name="rs")
-            nc.scalar.activation(sq[:, :n], d, ACT.Square)
-            nc.scalar.activation(
-                rs[:, :n], sq[:, :n], ACT.Abs_reciprocal_sqrt, bias=ginv[:, i : i + 1], scale=ginv[:, i : i + 1]
-            )
-            nc.scalar.activation(wt[ci][:, t, :], rs[:, :n], ACT.Square)
+                base = SLOT[ci - 3] + 2048 * t
+            pair = [
+                reuse.tile([P, n], F32, name=f"pick{ci}{t}{s}", align_bytes=64, offset=base + 4 * n * s)
+                for s in range(2)
+            ]
+            pairs[ci, t] = pair
+            lc = slice(c0 // 16, (c0 + n) // 16)
+            nc.vector.tensor_copy(out=pair[0][:], in_=h[b, t][:].indirect(pos1_t[:, lc]))
+            nc.vector.tensor_copy(out=pair[1][:], in_=h[b, t][:].indirect(pos2_t[:, lc]))
 
-        def mult(ci, lo, hi):
+        def sub(ci, t, eng):
+            pair = pairs[ci, t]
+            engs[eng].tensor_tensor(dt[ci][:, t, :], pair[0][:], pair[1][:], ALU.subtract)
+
+        def weight(ci, t):
+            pair = pairs[ci, t]
+            d = dt[ci][:, t, :]
+            i = 4 * chunks[ci][0] + t
+            nc.scalar.activation(pair[0][:], d, ACT.Square)
+            nc.scalar.activation(
+                pair[1][:], pair[0][:], ACT.Abs_reciprocal_sqrt,
+                bias=ginv[:, i : i + 1], scale=ginv[:, i : i + 1],
+            )
+            nc.scalar.activation(wt[ci][:, t, :], pair[1][:], ACT.Square)
+
+        def mult(ci, lo, hi, eng):
             b, c0, n = chunks[ci]
             dst = zb[b][:, 4 * (c0 + lo) : 4 * (c0 + hi)].rearrange("p (c i t) -> p c t i", i=4, t=4)
             d = dt[ci][:, :, lo:hi].rearrange("p t (c i) -> p c t i", i=4)
             w = wt[ci][:, :, lo:hi].rearrange("p t (c i) -> p c t i", i=4)
-            nc.vector.tensor_tensor(dst, d, w, ALU.mult)
+            engs[eng].tensor_tensor(dst, d, w, ALU.mult)
 
         def quant_z(b, lo, hi):
             nc.vector.quantize_mx(
@@ -238,58 +235,135 @@ def tile_list_robust_station_increments_kernel(
                 stop=(b == 1),
             )
 
-        def product(c, res, lo):
+        res = {3: keep.tile([P, 4, 128], F32, name="res3")}
+        last = []
+
+        def evacuate(dst, src, eng):
+            if eng == "s":
+                nc.scalar.copy(out=dst, in_=src)
+            else:
+                nc.vector.tensor_copy(out=dst, in_=src)
+
+        def product(c, eng):
+            if RA[c] < 0:
+                res[c] = keep.tile([P, 4, 128], F32, name=f"res{c}")
+            else:
+                res[c] = reuse.tile([P, 4, 128], F32, name=f"res{c}", align_bytes=64, offset=2048 * RA[c])
             acc = psum.tile([P, 4, 128], F32, name="acc")
             for i in range(4):
                 for b in range(2):
                     out_pass(acc[:, i, :], i, c, b)
-            nc.scalar.copy(out=res[:, :, lo : lo + 128], in_=acc[:])
+            evacuate(res[c][:], acc[:], eng)
+            nc.sync.dma_start(out=out_v[:, :, 128 * c : 128 * (c + 1)], in_=res[c][:])
 
-        res0 = keep.tile([P, 4, 256], F32, name="res0")
-        res1 = keep.tile([P, 4, 128], F32, name="res1")
-        res2 = keep.tile([P, 4, 128], F32, name="res2")
+        def last_first():
+            for i in range(4):
+                last.append(psum.tile([P, 128], F32, name="acc"))
+                out_pass(last[i][:], i, 3, 0)
 
-        unit(0, 0)
-        unit(0, 1)
+        def last_second():
+            for i in range(4):
+                out_pass(last[i][:], i, 3, 1)
+                evacuate(res[3][:, i, :], last[i][:], "sv"[i % 2])
+                if i % 2 == 1:
+                    nc.sync.dma_start(out=out_v[:, i - 1 : i + 1, 384:512], in_=res[3][:, i - 1 : i + 1, :])
+
+        cast(0, 0, 0, "s")
+        cast(0, 0, 1, "g")
+        quant_w(0, 0, 0, 1)
+        cast(0, 1, 0, "s")
+        cast(0, 1, 1, "v")
+        quant_w(0, 1, 0, 1)
+        make_h(0, 0)
+        quant_w(0, 0, 1, 2)
+        quant_w(0, 1, 1, 2)
+        quant_w(0, 0, 2, 4)
+        quant_w(0, 1, 2, 4)
+        make_h(0, 1)
+        make_h(0, 2)
+        make_h(0, 3)
+        cast(1, 0, 0, "g")
+        cast(1, 0, 1, "g")
+        cast(1, 1, 0, "s")
+        cast(1, 1, 1, "s")
         quant_w(1, 0, 0, 4)
         quant_w(1, 1, 0, 4)
-        for t in range(4):
-            make_h(1, t)
-        unit(0, 2)
-        unit(0, 3)
-        unit(1, 0)
-        unit(1, 1)
-        unit(1, 2)
-        mult(0, 0, 256)
-        unit(1, 3)
-        mult(0, 256, 512)
-        unit(2, 0)
+        gath(0, 0)
+        sub(0, 0, "g")
+        weight(0, 0)
+        gath(0, 1)
+        sub(0, 1, "g")
+        weight(0, 1)
+        gath(0, 2)
+        sub(0, 2, "g")
+        weight(0, 2)
+        gath(0, 3)
+        sub(0, 3, "g")
+        weight(0, 3)
+        make_h(1, 0)
+        make_h(1, 1)
+        make_h(1, 2)
+        make_h(1, 3)
+        gath(1, 0)
+        sub(1, 0, "g")
+        weight(1, 0)
+        gath(1, 1)
+        sub(1, 1, "g")
+        weight(1, 1)
+        gath(1, 2)
+        sub(1, 2, "g")
+        weight(1, 2)
+        gath(1, 3)
+        sub(1, 3, "g")
+        weight(1, 3)
+        mult(0, 0, 128, "g")
+        mult(0, 128, 256, "g")
+        gath(2, 0)
+        sub(2, 0, "g")
+        weight(2, 0)
+        gath(2, 1)
+        sub(2, 1, "g")
+        weight(2, 1)
+        gath(2, 2)
+        sub(2, 2, "g")
+        weight(2, 2)
+        gath(2, 3)
+        sub(2, 3, "g")
+        weight(2, 3)
+        mult(1, 0, 256, "v")
         quant_z(0, 0, 512)
-        unit(2, 1)
-        unit(2, 2)
-        mult(1, 0, 256)
-        unit(2, 3)
+        gath(3, 0)
+        sub(3, 0, "g")
+        weight(3, 0)
+        gath(3, 1)
+        sub(3, 1, "g")
+        weight(3, 1)
+        gath(3, 2)
+        sub(3, 2, "g")
+        weight(3, 2)
+        gath(3, 3)
+        sub(3, 3, "g")
+        weight(3, 3)
+        gath(4, 0)
+        sub(4, 0, "g")
+        weight(4, 0)
+        gath(4, 1)
+        sub(4, 1, "g")
+        weight(4, 1)
+        gath(4, 2)
+        sub(4, 2, "g")
+        weight(4, 2)
+        gath(4, 3)
+        sub(4, 3, "v")
+        weight(4, 3)
+        mult(2, 0, 256, "v")
         quant_z(1, 0, 256)
-        product(0, res0, 0)
-        product(1, res0, 128)
-        nc.sync.dma_start(out=out_v[:, :, 0:256], in_=res0[:])
-        unit(3, 0)
-        unit(3, 1)
-        mult(2, 0, 128)
-        unit(3, 2)
+        mult(3, 0, 128, "v")
         quant_z(1, 256, 384)
-        product(2, res1, 0)
-        nc.sync.dma_start(out=out_v[:, :, 256:384], in_=res1[:])
-        last = [psum.tile([P, 128], F32, name="acc") for i in range(4)]
-        for i in range(4):
-            out_pass(last[i][:], i, 3, 0)
-        unit(3, 3)
-        mult(3, 0, 128)
+        product(0, "s")
+        product(1, "v")
+        product(2, "s")
+        last_first()
+        mult(4, 0, 128, "v")
         quant_z(1, 384, 512)
-        for i in range(4):
-            out_pass(last[i][:], i, 3, 1)
-            if i % 2 == 0:
-                nc.scalar.copy(out=res2[:, i, :], in_=last[i][:])
-            else:
-                nc.vector.tensor_copy(out=res2[:, i, :], in_=last[i][:])
-                nc.sync.dma_start(out=out_v[:, i - 1 : i + 1, 384:512], in_=res2[:, i - 1 : i + 1, :])
+        last_second()

@@ -18,10 +18,10 @@ ACT = mybir.ActivationFunctionType
 
 P = 128
 TINY = 2.0 ** -126
-RA = [1, 2, 3]
-HB = 3
-CHUNKS = [(0, 0, 256), (0, 256, 256), (1, 0, 256), (1, 256, 128), (1, 384, 128)]
-SLOT = [0, 1024]
+RA = [-1, -1, -1]
+HB = 2
+GATE = 2
+CHUNKS = [(0, 0, 256), (0, 256, 256), (1, 0, 256), (1, 256, 256)]
 
 
 def tile_list_robust_station_increments_kernel(
@@ -83,11 +83,12 @@ def tile_list_robust_station_increments_kernel(
         load_w1(0, 0, 1)
         load_w1(0, 1, 0)
         load_w1(0, 1, 1)
+        load_w1(1, 0, 0)
+        load_w1(1, 0, 1)
         nc.sync.dma_start(pos1_t[:], pos1)
         nc.sync.dma_start(pos2_t[:], pos2)
-        for a in range(2):
-            for hf in range(2):
-                load_w1(1, a, hf)
+        load_w1(1, 1, 0)
+        load_w1(1, 1, 1)
         nc.sync.dma_start(out=w4w[:], in_=w4_words.bitcast(I32).rearrange("a p c -> p a c"))
         w4s32 = w4_scales.bitcast(I32)
         for q in range(4):
@@ -160,7 +161,7 @@ def tile_list_robust_station_increments_kernel(
                 h_pass(b, t, hf, 0)
                 h_pass(b, t, hf, 1)
                 acc = accs[b, t, hf]
-                if i == 0 and hf == 1:
+                if False:
                     nc.vector.tensor_scalar(h[b, t][:, cols], acc[:], gsign[:, i : i + 1], None, ALU.mult)
                 else:
                     nc.scalar.activation(h[b, t][:, cols], acc[:], ACT.Copy, scale=gsign[:, i : i + 1])
@@ -170,7 +171,8 @@ def tile_list_robust_station_increments_kernel(
         pairs = {}
         dt = {}
         wt = {}
-        zb = [keep.tile([P, 4 * NP], BF16, name=f"zb{b}", align_bytes=64) for b in range(2)]
+        zb0 = keep.tile([P, 4 * NP], BF16, name="zb0", align_bytes=64)
+        zb1 = {}
         zc = [keep.tile([P, NP], U32, name=f"zc{b}", align_bytes=64) for b in range(2)]
         zs = [keep.tile([P, NP], U8, name=f"zs{b}", align_bytes=64) for b in range(2)]
 
@@ -179,14 +181,16 @@ def tile_list_robust_station_increments_kernel(
             if t == 0:
                 dt[ci] = keep.tile([P, 4, n], F32, name=f"d{ci}")
                 wt[ci] = keep.tile([P, 4, n], F32, name=f"w{ci}")
-            if n == 256:
-                base = 8192 * ((ci + 1) % 2) + 2048 * t
+            if ci < 2 and t >= GATE:
+                pair = [
+                    reuse.tile(
+                        [P, n], F32, name=f"pick{ci}{t}{s}", align_bytes=64,
+                        offset=4096 * (t - 2) * (3 - GATE) + 4096 * (GATE - 2) + 2048 * ci + 1024 * s,
+                    )
+                    for s in range(2)
+                ]
             else:
-                base = SLOT[ci - 3] + 2048 * t
-            pair = [
-                reuse.tile([P, n], F32, name=f"pick{ci}{t}{s}", align_bytes=64, offset=base + 4 * n * s)
-                for s in range(2)
-            ]
+                pair = [keep.tile([P, n], F32, name=f"pick{ci}{t}{s}") for s in range(2)]
             pairs[ci, t] = pair
             lc = slice(c0 // 16, (c0 + n) // 16)
             nc.vector.tensor_copy(out=pair[0][:], in_=h[b, t][:].indirect(pos1_t[:, lc]))
@@ -209,14 +213,19 @@ def tile_list_robust_station_increments_kernel(
 
         def mult(ci, lo, hi, eng):
             b, c0, n = chunks[ci]
-            dst = zb[b][:, 4 * (c0 + lo) : 4 * (c0 + hi)].rearrange("p (c i t) -> p c t i", i=4, t=4)
+            if b == 0:
+                flat = zb0[:, 4 * (c0 + lo) : 4 * (c0 + hi)]
+            else:
+                zb1[c0 + lo] = keep.tile([P, 512], BF16, name="zb1", align_bytes=64, bufs=2)
+                flat = zb1[c0 + lo][:]
+            dst = flat.rearrange("p (c i t) -> p c t i", i=4, t=4)
             d = dt[ci][:, :, lo:hi].rearrange("p t (c i) -> p c t i", i=4)
             w = wt[ci][:, :, lo:hi].rearrange("p t (c i) -> p c t i", i=4)
             engs[eng].tensor_tensor(dst, d, w, ALU.mult)
 
         def quant_z(b, lo, hi):
             nc.vector.quantize_mx(
-                out=zc[b][:, lo:hi].bitcast(FP8X4), scales=zs[b][:, lo:hi], in_=zb[b][:, 4 * lo : 4 * hi]
+                out=zc[b][:, lo:hi].bitcast(FP8X4), scales=zs[b][:, lo:hi], in_=zb0[:] if b == 0 else zb1[lo][:]
             )
 
         w4u = w4w[:].bitcast(U8)
@@ -264,12 +273,12 @@ def tile_list_robust_station_increments_kernel(
         def last_second():
             for i in range(4):
                 out_pass(last[i][:], i, 3, 1)
-                evacuate(res[3][:, i, :], last[i][:], "sv"[i % 2])
+                evacuate(res[3][:, i, :], last[i][:], "v")
                 if i % 2 == 1:
                     nc.sync.dma_start(out=out_v[:, i - 1 : i + 1, 384:512], in_=res[3][:, i - 1 : i + 1, :])
 
         cast(0, 0, 0, "s")
-        cast(0, 0, 1, "g")
+        cast(0, 0, 1, "s")
         quant_w(0, 0, 0, 1)
         cast(0, 1, 0, "s")
         cast(0, 1, 1, "v")
@@ -281,89 +290,78 @@ def tile_list_robust_station_increments_kernel(
         quant_w(0, 1, 2, 4)
         make_h(0, 1)
         make_h(0, 2)
-        make_h(0, 3)
-        cast(1, 0, 0, "g")
-        cast(1, 0, 1, "g")
+        cast(1, 0, 0, "v")
+        cast(1, 0, 1, "s")
         cast(1, 1, 0, "s")
         cast(1, 1, 1, "s")
+        make_h(0, 3)
         quant_w(1, 0, 0, 4)
         quant_w(1, 1, 0, 4)
-        gath(0, 0)
-        sub(0, 0, "g")
-        weight(0, 0)
-        gath(0, 1)
-        sub(0, 1, "g")
-        weight(0, 1)
-        gath(0, 2)
-        sub(0, 2, "g")
-        weight(0, 2)
-        gath(0, 3)
-        sub(0, 3, "g")
-        weight(0, 3)
         make_h(1, 0)
         make_h(1, 1)
         make_h(1, 2)
         make_h(1, 3)
+        gath(0, 0)
         gath(1, 0)
-        sub(1, 0, "g")
+        sub(0, 0, "v")
+        sub(1, 0, "v")
+        weight(0, 0)
         weight(1, 0)
+        gath(0, 1)
         gath(1, 1)
-        sub(1, 1, "g")
+        sub(0, 1, "v")
+        sub(1, 1, "v")
+        weight(0, 1)
         weight(1, 1)
+        gath(0, 2)
         gath(1, 2)
-        sub(1, 2, "g")
+        sub(0, 2, "v")
+        sub(1, 2, "v")
+        weight(0, 2)
         weight(1, 2)
+        gath(0, 3)
         gath(1, 3)
-        sub(1, 3, "g")
+        sub(0, 3, "v")
+        sub(1, 3, "v")
+        weight(0, 3)
         weight(1, 3)
-        mult(0, 0, 128, "g")
-        mult(0, 128, 256, "g")
         gath(2, 0)
-        sub(2, 0, "g")
+        gath(3, 0)
+        sub(2, 0, "v")
+        sub(3, 0, "v")
         weight(2, 0)
+        weight(3, 0)
         gath(2, 1)
-        sub(2, 1, "g")
+        gath(3, 1)
+        sub(2, 1, "v")
+        sub(3, 1, "v")
         weight(2, 1)
+        weight(3, 1)
         gath(2, 2)
-        sub(2, 2, "g")
+        gath(3, 2)
+        sub(2, 2, "v")
+        sub(3, 2, "v")
         weight(2, 2)
+        weight(3, 2)
         gath(2, 3)
-        sub(2, 3, "g")
+        gath(3, 3)
+        sub(2, 3, "v")
+        sub(3, 3, "v")
         weight(2, 3)
+        weight(3, 3)
+        mult(0, 0, 256, "v")
         mult(1, 0, 256, "v")
         quant_z(0, 0, 512)
-        gath(3, 0)
-        sub(3, 0, "g")
-        weight(3, 0)
-        gath(3, 1)
-        sub(3, 1, "g")
-        weight(3, 1)
-        gath(3, 2)
-        sub(3, 2, "g")
-        weight(3, 2)
-        gath(3, 3)
-        sub(3, 3, "g")
-        weight(3, 3)
-        gath(4, 0)
-        sub(4, 0, "g")
-        weight(4, 0)
-        gath(4, 1)
-        sub(4, 1, "g")
-        weight(4, 1)
-        gath(4, 2)
-        sub(4, 2, "g")
-        weight(4, 2)
-        gath(4, 3)
-        sub(4, 3, "v")
-        weight(4, 3)
-        mult(2, 0, 256, "v")
-        quant_z(1, 0, 256)
+        last_first()
+        mult(2, 0, 128, "v")
+        quant_z(1, 0, 128)
+        product(0, "s")
+        mult(2, 128, 256, "v")
+        quant_z(1, 128, 256)
+        product(1, "s")
         mult(3, 0, 128, "v")
         quant_z(1, 256, 384)
-        product(0, "s")
-        product(1, "v")
         product(2, "s")
-        last_first()
-        mult(4, 0, 128, "v")
+        mult(3, 128, 256, "v")
         quant_z(1, 384, 512)
         last_second()

@@ -2,8 +2,8 @@ from contextlib import ExitStack
 
 import concourse.mybir as mybir
 
-K, T, S, NP, H, N = 1024, 2048, 1024, 512, 1024, 512
-FLOPS = 2 * K * H * S + 2 * H * N * NP
+K, T, S, PAIRS, H, N = 1024, 2048, 1024, 512, 1024, 512
+FLOPS = 2 * K * H * S + 2 * H * N * PAIRS
 
 F32 = mybir.dt.float32
 BF16 = mybir.dt.bfloat16
@@ -17,11 +17,15 @@ ALU = mybir.AluOpType
 ACT = mybir.ActivationFunctionType
 
 P = 128
-TINY = 2.0 ** -126
-RA = [-1, -1, -1]
-HB = 2
-GATE = 2
-CHUNKS = [(0, 0, 256), (0, 256, 256), (1, 0, 256), (1, 256, 256)]
+PACK = 4
+PASS = P * PACK
+BANK = 512
+HALF = PASS // 2
+CHUNK = 128
+CHUNKS = PAIRS // CHUNK
+H_BANKS = 2
+SMALLEST = 2.0**-126
+STAGE_BYTES = 2 * PACK * PASS
 
 
 def tile_list_robust_station_increments_kernel(
@@ -30,338 +34,240 @@ def tile_list_robust_station_increments_kernel(
     nc = tc.nc
     with ExitStack() as ctx:
         keep = ctx.enter_context(tc.tile_pool(name="keep", bufs=1))
-        reuse = ctx.enter_context(tc.tile_pool(name="reuse", bufs=1))
-        hps = ctx.enter_context(tc.psum_pool(name="hps", bufs=HB))
-        psum = ctx.enter_context(tc.psum_pool(name="psum", bufs=8 - HB))
+        stage = ctx.enter_context(tc.tile_pool(name="stage", bufs=1))
+        h_psum = ctx.enter_context(tc.psum_pool(name="h_psum", bufs=H_BANKS))
+        out_psum = ctx.enter_context(tc.psum_pool(name="out_psum", bufs=8 - H_BANKS))
 
-        offs_t = keep.tile([P, S // 16], U16, name="offs_t")
-        pos1_t = keep.tile([P, NP // 16], U16, name="pos1_t")
-        pos2_t = keep.tile([P, NP // 16], U16, name="pos2_t")
-        tabw = [keep.tile([P, T], I32, name=f"tabw{a}", align_bytes=64) for a in range(2)]
-        tabs = keep.tile([P, T // 4], I32, name="tabs", align_bytes=64)
-        vw = [keep.tile([P, S], U32, name=f"vw{a}", align_bytes=64) for a in range(2)]
-        vs = keep.tile([P, S], U8, name="vs", align_bytes=64)
-        w4w = keep.tile([P, 2, 2 * N // 4], I32, name="w4w", align_bytes=64)
-        w4s = keep.tile([P, 2, N // 4], I32, name="w4s", align_bytes=64)
-        g = keep.tile([P, 2, 4], F32, name="g")
-        gabs = keep.tile([P, 8], F32, name="gabs")
-        gsign = keep.tile([P, 8], F32, name="gsign")
-        gclamp = keep.tile([P, 8], F32, name="gclamp")
-        ginv = keep.tile([P, 8], F32, name="ginv")
-        warm_in = keep.tile([P, 1], F32, name="warm_in")
-        warm_out = keep.tile([P, 1], F32, name="warm_out")
+        idx_list = keep.tile([P, S // 16], U16, name="idx_list")
+        p1_list = keep.tile([P, PAIRS // 16], U16, name="p1_list")
+        p2_list = keep.tile([P, PAIRS // 16], U16, name="p2_list")
+        table_words = [keep.tile([P, T], I32, name=f"table_words{a}", align_bytes=64) for a in range(2)]
+        table_scales = keep.tile([P, T // 4], I32, name="table_scales", align_bytes=64)
+        v_words = [keep.tile([P, S], U32, name=f"v_words{a}", align_bytes=64) for a in range(2)]
+        v_scales = keep.tile([P, S], U8, name="v_scales", align_bytes=64)
+        w4_word_tile = keep.tile([P, 2, 2 * N // 4], I32, name="w4_word_tile", align_bytes=64)
+        w4_scale_tile = keep.tile([P, 2, N // 4], I32, name="w4_scale_tile", align_bytes=64)
+        gain_tile = keep.tile([P, 2, PACK], F32, name="gain_tile")
 
-        nc.vector.memset(tabs[:], 0)
-        nc.gpsimd.memset(warm_in[:], 1.0)
-        nc.scalar.activation(warm_out[:], warm_in[:], ACT.Abs_reciprocal_sqrt)
-        nc.vector.memset(w4s[:], 0)
+        nc.vector.memset(table_scales[:], 0)
+        nc.vector.memset(w4_scale_tile[:], 0)
 
-        raw = {}
-        for b in range(2):
-            for a in range(2):
-                for hf in range(2):
-                    raw[b, a, hf] = keep.tile([P, 4, 256], F32, name=f"raw{b}{a}{hf}")
+        w1_raw = {}
 
-        def load_w1(b, a, hf):
-            c0 = 512 * b + 256 * hf
+        def load_w1(b, a, half):
+            w1_raw[b, a, half] = keep.tile([P, PACK, HALF], F32, name=f"w1_raw{b}{a}{half}")
+            first = PASS * b + HALF * half
+            rows = w1[PASS * a : PASS * (a + 1), first : first + HALF]
+            nc.sync.dma_start(out=w1_raw[b, a, half][:], in_=rows.rearrange("(p j) c -> p j c", j=PACK))
+
+        def load_table_words(a):
+            nc.sync.dma_start(out=table_words[a][:], in_=tab_words[a].rearrange("p t i -> p (t i)").bitcast(I32))
+
+        nc.sync.dma_start(idx_list[:], offs)
+        nc.sync.dma_start(out=gain_tile[:], in_=gain.rearrange("(b p t) -> p b t", b=2, t=PACK))
+        load_table_words(0)
+        for quad in range(4):
             nc.sync.dma_start(
-                out=raw[b, a, hf][:],
-                in_=w1[512 * a : 512 * (a + 1), c0 : c0 + 256].rearrange("(p j) c -> p j c", j=4),
+                out=table_scales[32 * quad : 32 * quad + 8, :],
+                in_=tab_scales.bitcast(I32)[:, 4 * quad : 4 * quad + 4, :],
+            )
+        load_table_words(1)
+        for b, a in ((0, 0), (0, 1), (1, 0)):
+            for half in range(2):
+                load_w1(b, a, half)
+        nc.sync.dma_start(p1_list[:], pos1)
+        nc.sync.dma_start(p2_list[:], pos2)
+        for half in range(2):
+            load_w1(1, 1, half)
+        nc.sync.dma_start(out=w4_word_tile[:], in_=w4_words.bitcast(I32).rearrange("b p c -> p b c"))
+        for quad in range(4):
+            nc.sync.dma_start(
+                out=w4_scale_tile[32 * quad : 32 * quad + 4, :, :],
+                in_=w4_scales.bitcast(I32)[:, 4 * quad : 4 * quad + 4, :].rearrange("b i c -> i b c"),
             )
 
-        def load_tab(a):
-            nc.sync.dma_start(out=tabw[a][:], in_=tab_words[a].rearrange("p t i -> p (t i)").bitcast(I32))
+        gains = gain_tile[:].rearrange("p b t -> p (b t)")
+        size, floored, inverse, invroot, root, root_squared, fix, twice_positive, sign = (
+            keep.tile([P, 2 * PACK], F32, name=f"gain_{name}")
+            for name in ("size", "floored", "inverse", "invroot", "root", "root_squared", "fix", "twice", "sign")
+        )
+        nc.vector.scalar_tensor_tensor(size[:], gains, -1.0, gains, ALU.mult, ALU.max)
+        nc.vector.tensor_scalar(floored[:], size[:], SMALLEST, None, ALU.max)
+        nc.vector.reciprocal(inverse[:], floored[:])
+        nc.scalar.activation(invroot[:], floored[:], ACT.Abs_reciprocal_sqrt)
+        nc.vector.reciprocal(root[:], invroot[:])
+        nc.gpsimd.tensor_tensor(root_squared[:], root[:], root[:], ALU.mult)
+        nc.gpsimd.tensor_tensor(fix[:], root_squared[:], inverse[:], ALU.mult)
+        nc.gpsimd.tensor_scalar(twice_positive[:], gains, 0.0, 2.0, ALU.is_ge, ALU.mult)
+        nc.gpsimd.tensor_scalar(sign[:], twice_positive[:], 1.0, -1.0, ALU.mult, ALU.add)
 
-        nc.sync.dma_start(offs_t[:], offs)
-        load_tab(0)
-        ts32 = tab_scales.bitcast(I32)
-        for q in range(4):
-            nc.sync.dma_start(out=tabs[32 * q : 32 * q + 8, :], in_=ts32[:, 4 * q : 4 * q + 4, :])
-        load_tab(1)
-        nc.sync.dma_start(out=g[:], in_=gain.rearrange("(b p t) -> p b t", b=2, t=4))
-        load_w1(0, 0, 0)
-        load_w1(0, 0, 1)
-        load_w1(0, 1, 0)
-        load_w1(0, 1, 1)
-        load_w1(1, 0, 0)
-        load_w1(1, 0, 1)
-        nc.sync.dma_start(pos1_t[:], pos1)
-        nc.sync.dma_start(pos2_t[:], pos2)
-        load_w1(1, 1, 0)
-        load_w1(1, 1, 1)
-        nc.sync.dma_start(out=w4w[:], in_=w4_words.bitcast(I32).rearrange("a p c -> p a c"))
-        w4s32 = w4_scales.bitcast(I32)
-        for q in range(4):
-            nc.sync.dma_start(
-                out=w4s[32 * q : 32 * q + 4, :, :],
-                in_=w4s32[:, 4 * q : 4 * q + 4, :].rearrange("a i c -> i a c"),
-            )
+        nc.vector.tensor_copy(out=v_words[0][:], in_=table_words[0][:].bitcast(U32).indirect(idx_list[:]))
+        nc.vector.tensor_copy(out=v_scales[:], in_=table_scales[:].bitcast(U8).indirect(idx_list[:]))
+        nc.vector.tensor_copy(out=v_words[1][:], in_=table_words[1][:].bitcast(U32).indirect(idx_list[:]))
 
-        gflat = g[:].rearrange("p b t -> p (b t)")
-        nc.scalar.activation(gabs[:], gflat, ACT.Abs)
-        nc.scalar.activation(gsign[:], gflat, ACT.Sign)
-        nc.vector.tensor_scalar(gclamp[:], gabs[:], TINY, None, ALU.max)
-        nc.vector.reciprocal(ginv[:], gclamp[:])
-
-        grouped = {}
-        codes = {}
-        scales = {}
+        w1_rounded = {}
+        w1_words = {}
+        w1_scales = {}
         for b in range(2):
             for a in range(2):
-                codes[b, a] = keep.tile([P, 512], U32, name=f"wc{b}{a}", align_bytes=64)
-                scales[b, a] = keep.tile([P, 512], U8, name=f"ws{b}{a}", align_bytes=64)
+                w1_words[b, a] = keep.tile([P, PASS], U32, name=f"w1_words{b}{a}", align_bytes=64)
+                w1_scales[b, a] = keep.tile([P, PASS], U8, name=f"w1_scales{b}{a}", align_bytes=64)
 
-        def cast(b, a, hf, eng):
-            if hf == 0:
-                grouped[b, a] = reuse.tile(
-                    [P, 2048], BF16, name=f"grp{b}{a}", align_bytes=64, offset=4096 * ((a + b + 1) % 2)
+        def copy_on_gpsimd(dst, src):
+            nc.gpsimd.tensor_scalar(dst, src, 1.0, 0.0, ALU.mult, ALU.add)
+
+        def round_w1(b, a, half, copy):
+            if half == 0:
+                area = (a + b + 1) % 2
+                w1_rounded[b, a] = stage.tile(
+                    [P, PACK * PASS], BF16, name=f"w1_rounded{b}{a}", align_bytes=64, offset=STAGE_BYTES * area
                 )
-            dst = grouped[b, a][:].rearrange("p (t m j) -> p m t j", t=4, j=4)[:, 64 * hf : 64 * (hf + 1), :, :]
-            src = raw[b, a, hf][:].rearrange("p j (m t) -> p m t j", t=4)
-            if eng == "v":
-                nc.vector.tensor_copy(out=dst, in_=src)
-            elif eng == "s":
-                nc.scalar.copy(out=dst, in_=src)
-            else:
-                nc.gpsimd.tensor_scalar(dst, src, 1.0, 0.0, ALU.mult, ALU.add)
-
-        def quant_w(b, a, t0, t1):
-            nc.vector.quantize_mx(
-                out=codes[b, a][:, 128 * t0 : 128 * t1].bitcast(FP8X4),
-                scales=scales[b, a][:, 128 * t0 : 128 * t1],
-                in_=grouped[b, a][:, 512 * t0 : 512 * t1],
+            by_column = w1_rounded[b, a][:].rearrange("p (t m j) -> p m t j", t=PACK, j=PACK)
+            per_half = HALF // PACK
+            copy(
+                by_column[:, per_half * half : per_half * (half + 1), :, :],
+                w1_raw[b, a, half][:].rearrange("p j (m t) -> p m t j", t=PACK),
             )
 
-        nc.vector.tensor_copy(out=vw[0][:], in_=tabw[0][:].bitcast(U32).indirect(offs_t[:]))
-        nc.vector.tensor_copy(out=vs[:], in_=tabs[:].bitcast(U8).indirect(offs_t[:]))
-        nc.vector.tensor_copy(out=vw[1][:], in_=tabw[1][:].bitcast(U32).indirect(offs_t[:]))
+        def quantise_w1(b, a, first_slot, end_slot):
+            cols = slice(P * first_slot, P * end_slot)
+            nc.vector.quantize_mx(
+                out=w1_words[b, a][:, cols].bitcast(FP8X4),
+                scales=w1_scales[b, a][:, cols],
+                in_=w1_rounded[b, a][:, PASS * first_slot : PASS * end_slot],
+            )
 
         h = {}
-        accs = {}
-
-        def h_pass(b, t, hf, a):
-            if a == 0:
-                accs[b, t, hf] = hps.tile([P, 512], F32, name="hacc")
-            cols = slice(512 * hf, 512 * (hf + 1))
-            nc.tensor.matmul_mx(
-                out=accs[b, t, hf][:],
-                lhsT=codes[b, a][:, 128 * t : 128 * (t + 1)].bitcast(FP8X4),
-                lhsT_scale=scales[b, a][:, 128 * t : 128 * (t + 1)],
-                rhs=vw[a][:, cols].bitcast(FP8X4),
-                rhs_scale=vs[4 * a :, cols],
-                start=(a == 0),
-                stop=(a == 1),
-            )
 
         def make_h(b, t):
             h[b, t] = keep.tile([P, S], F32, name=f"h{b}{t}")
-            i = 4 * b + t
-            for hf in range(2):
-                cols = slice(512 * hf, 512 * (hf + 1))
-                h_pass(b, t, hf, 0)
-                h_pass(b, t, hf, 1)
-                acc = accs[b, t, hf]
-                if False:
-                    nc.vector.tensor_scalar(h[b, t][:, cols], acc[:], gsign[:, i : i + 1], None, ALU.mult)
-                else:
-                    nc.scalar.activation(h[b, t][:, cols], acc[:], ACT.Copy, scale=gsign[:, i : i + 1])
-
-        engs = {"v": nc.vector, "g": nc.gpsimd}
-        chunks = CHUNKS
-        pairs = {}
-        dt = {}
-        wt = {}
-        zb0 = keep.tile([P, 4 * NP], BF16, name="zb0", align_bytes=64)
-        zb1 = {}
-        zc = [keep.tile([P, NP], U32, name=f"zc{b}", align_bytes=64) for b in range(2)]
-        zs = [keep.tile([P, NP], U8, name=f"zs{b}", align_bytes=64) for b in range(2)]
-
-        def gath(ci, t):
-            b, c0, n = chunks[ci]
-            if t == 0:
-                dt[ci] = keep.tile([P, 4, n], F32, name=f"d{ci}")
-                wt[ci] = keep.tile([P, 4, n], F32, name=f"w{ci}")
-            if ci < 2 and t >= GATE:
-                pair = [
-                    reuse.tile(
-                        [P, n], F32, name=f"pick{ci}{t}{s}", align_bytes=64,
-                        offset=4096 * (t - 2) * (3 - GATE) + 4096 * (GATE - 2) + 2048 * ci + 1024 * s,
+            row_sign = sign[:, PACK * b + t : PACK * b + t + 1]
+            slot_cols = slice(P * t, P * (t + 1))
+            for bank in range(S // BANK):
+                cols = slice(BANK * bank, BANK * (bank + 1))
+                acc = h_psum.tile([P, BANK], F32, name="h_acc")
+                for a in range(2):
+                    nc.tensor.matmul_mx(
+                        out=acc[:],
+                        lhsT=w1_words[b, a][:, slot_cols].bitcast(FP8X4),
+                        lhsT_scale=w1_scales[b, a][:, slot_cols],
+                        rhs=v_words[a][:, cols].bitcast(FP8X4),
+                        rhs_scale=v_scales[4 * a :, cols],
+                        start=(a == 0),
+                        stop=(a == 1),
                     )
-                    for s in range(2)
-                ]
-            else:
-                pair = [keep.tile([P, n], F32, name=f"pick{ci}{t}{s}") for s in range(2)]
-            pairs[ci, t] = pair
-            lc = slice(c0 // 16, (c0 + n) // 16)
-            nc.vector.tensor_copy(out=pair[0][:], in_=h[b, t][:].indirect(pos1_t[:, lc]))
-            nc.vector.tensor_copy(out=pair[1][:], in_=h[b, t][:].indirect(pos2_t[:, lc]))
+                if (b, t, bank) == (0, 0, 1):
+                    nc.vector.tensor_scalar(h[b, t][:, cols], acc[:], row_sign, None, ALU.mult)
+                else:
+                    nc.scalar.activation(h[b, t][:, cols], acc[:], ACT.Copy, scale=row_sign)
 
-        def sub(ci, t, eng):
-            pair = pairs[ci, t]
-            engs[eng].tensor_tensor(dt[ci][:, t, :], pair[0][:], pair[1][:], ALU.subtract)
+        departure = {}
+        weight = {}
 
-        def weight(ci, t):
-            pair = pairs[ci, t]
-            d = dt[ci][:, t, :]
-            i = 4 * chunks[ci][0] + t
-            nc.scalar.activation(pair[0][:], d, ACT.Square)
-            nc.scalar.activation(
-                pair[1][:], pair[0][:], ACT.Abs_reciprocal_sqrt,
-                bias=ginv[:, i : i + 1], scale=ginv[:, i : i + 1],
+        def influence(b, t):
+            if t == 0:
+                departure[b] = keep.tile([P, PACK, PAIRS], F32, name=f"departure{b}")
+                weight[b] = keep.tile([P, PACK, PAIRS], F32, name=f"weight{b}")
+            picks = []
+            for side in range(2):
+                name = f"pick{b}{t}{side}"
+                if b == 0 and t >= 2:
+                    offset = STAGE_BYTES * (t - 2) + STAGE_BYTES // 2 * side
+                    picks.append(stage.tile([P, PAIRS], F32, name=name, align_bytes=64, offset=offset))
+                else:
+                    picks.append(keep.tile([P, PAIRS], F32, name=name))
+            nc.vector.tensor_copy(out=picks[0][:], in_=h[b, t][:].indirect(p1_list[:]))
+            nc.vector.tensor_copy(out=picks[1][:], in_=h[b, t][:].indirect(p2_list[:]))
+            d = departure[b][:, t, :]
+            subtractor = nc.vector if (b, t) == (1, PACK - 1) else nc.gpsimd
+            subtractor.tensor_tensor(d, picks[0][:], picks[1][:], ALU.subtract)
+            squared, shrink = picks
+            col = slice(PACK * b + t, PACK * b + t + 1)
+            nc.scalar.activation(squared[:], d, ACT.Square)
+            nc.scalar.activation(shrink[:], squared[:], ACT.Abs_reciprocal_sqrt, bias=fix[:, col], scale=fix[:, col])
+            nc.scalar.activation(weight[b][:, t, :], shrink[:], ACT.Square, scale=root[:, col])
+
+        z_words = [keep.tile([P, PAIRS], U32, name=f"z_words{b}", align_bytes=64) for b in range(2)]
+        z_scales = [keep.tile([P, PAIRS], U8, name=f"z_scales{b}", align_bytes=64) for b in range(2)]
+
+        def multiply(b, cols, rounded):
+            nc.vector.tensor_tensor(
+                rounded.rearrange("p (c i t) -> p c t i", i=4, t=PACK),
+                departure[b][:, :, cols].rearrange("p t (c i) -> p c t i", i=4),
+                weight[b][:, :, cols].rearrange("p t (c i) -> p c t i", i=4),
+                ALU.mult,
             )
-            nc.scalar.activation(wt[ci][:, t, :], pair[1][:], ACT.Square)
 
-        def mult(ci, lo, hi, eng):
-            b, c0, n = chunks[ci]
-            if b == 0:
-                flat = zb0[:, 4 * (c0 + lo) : 4 * (c0 + hi)]
-            else:
-                zb1[c0 + lo] = keep.tile([P, 512], BF16, name="zb1", align_bytes=64, bufs=2)
-                flat = zb1[c0 + lo][:]
-            dst = flat.rearrange("p (c i t) -> p c t i", i=4, t=4)
-            d = dt[ci][:, :, lo:hi].rearrange("p t (c i) -> p c t i", i=4)
-            w = wt[ci][:, :, lo:hi].rearrange("p t (c i) -> p c t i", i=4)
-            engs[eng].tensor_tensor(dst, d, w, ALU.mult)
+        def quantise_z(b, cols, rounded):
+            nc.vector.quantize_mx(out=z_words[b][:, cols].bitcast(FP8X4), scales=z_scales[b][:, cols], in_=rounded)
 
-        def quant_z(b, lo, hi):
-            nc.vector.quantize_mx(
-                out=zc[b][:, lo:hi].bitcast(FP8X4), scales=zs[b][:, lo:hi], in_=zb0[:] if b == 0 else zb1[lo][:]
-            )
+        w4_word_bytes = w4_word_tile[:].bitcast(U8)
+        w4_scale_bytes = w4_scale_tile[:].bitcast(U8)
+        out_by_tile = out.rearrange("(i q) c -> q i c", q=P)
+        out_tiles = N // P
 
-        w4u = w4w[:].bitcast(U8)
-        w4su = w4s[:].bitcast(U8)
-        out_v = out.rearrange("(i q) p -> q i p", q=P)
-
-        def out_pass(acc, i, c, b):
-            cols = slice(128 * c, 128 * (c + 1))
+        def out_pass(acc, i, cols, b):
             nc.tensor.matmul_mx(
                 out=acc,
-                lhsT=w4u[:, b, 256 * i : 256 * (i + 1)].bitcast(FP4X4),
-                lhsT_scale=w4su[:, b, 128 * i : 128 * (i + 1)],
-                rhs=zc[b][:, cols].bitcast(FP8X4),
-                rhs_scale=zs[b][:, cols],
+                lhsT=w4_word_bytes[:, b, 2 * P * i : 2 * P * (i + 1)].bitcast(FP4X4),
+                lhsT_scale=w4_scale_bytes[:, b, P * i : P * (i + 1)],
+                rhs=z_words[b][:, cols].bitcast(FP8X4),
+                rhs_scale=z_scales[b][:, cols],
                 start=(b == 0),
                 stop=(b == 1),
             )
 
-        res = {3: keep.tile([P, 4, 128], F32, name="res3")}
-        last = []
-
-        def evacuate(dst, src, eng):
-            if eng == "s":
-                nc.scalar.copy(out=dst, in_=src)
-            else:
-                nc.vector.tensor_copy(out=dst, in_=src)
-
-        def product(c, eng):
-            if RA[c] < 0:
-                res[c] = keep.tile([P, 4, 128], F32, name=f"res{c}")
-            else:
-                res[c] = reuse.tile([P, 4, 128], F32, name=f"res{c}", align_bytes=64, offset=2048 * RA[c])
-            acc = psum.tile([P, 4, 128], F32, name="acc")
-            for i in range(4):
-                for b in range(2):
-                    out_pass(acc[:, i, :], i, c, b)
-            evacuate(res[c][:], acc[:], eng)
-            nc.sync.dma_start(out=out_v[:, :, 128 * c : 128 * (c + 1)], in_=res[c][:])
-
-        def last_first():
-            for i in range(4):
-                last.append(psum.tile([P, 128], F32, name="acc"))
-                out_pass(last[i][:], i, 3, 0)
-
-        def last_second():
-            for i in range(4):
-                out_pass(last[i][:], i, 3, 1)
-                evacuate(res[3][:, i, :], last[i][:], "v")
-                if i % 2 == 1:
-                    nc.sync.dma_start(out=out_v[:, i - 1 : i + 1, 384:512], in_=res[3][:, i - 1 : i + 1, :])
-
-        cast(0, 0, 0, "s")
-        cast(0, 0, 1, "s")
-        quant_w(0, 0, 0, 1)
-        cast(0, 1, 0, "s")
-        cast(0, 1, 1, "v")
-        quant_w(0, 1, 0, 1)
+        round_w1(0, 0, 0, nc.scalar.copy)
+        round_w1(0, 0, 1, copy_on_gpsimd)
+        quantise_w1(0, 0, 0, PACK)
+        round_w1(0, 1, 0, nc.scalar.copy)
+        round_w1(0, 1, 1, nc.vector.tensor_copy)
+        quantise_w1(0, 1, 0, 1)
         make_h(0, 0)
-        quant_w(0, 0, 1, 2)
-        quant_w(0, 1, 1, 2)
-        quant_w(0, 0, 2, 4)
-        quant_w(0, 1, 2, 4)
+        quantise_w1(0, 1, 1, 2)
+        quantise_w1(0, 1, 2, PACK)
         make_h(0, 1)
         make_h(0, 2)
-        cast(1, 0, 0, "v")
-        cast(1, 0, 1, "s")
-        cast(1, 1, 0, "s")
-        cast(1, 1, 1, "s")
+        round_w1(1, 0, 0, copy_on_gpsimd)
+        round_w1(1, 0, 1, copy_on_gpsimd)
         make_h(0, 3)
-        quant_w(1, 0, 0, 4)
-        quant_w(1, 1, 0, 4)
-        make_h(1, 0)
-        make_h(1, 1)
-        make_h(1, 2)
-        make_h(1, 3)
-        gath(0, 0)
-        gath(1, 0)
-        sub(0, 0, "v")
-        sub(1, 0, "v")
-        weight(0, 0)
-        weight(1, 0)
-        gath(0, 1)
-        gath(1, 1)
-        sub(0, 1, "v")
-        sub(1, 1, "v")
-        weight(0, 1)
-        weight(1, 1)
-        gath(0, 2)
-        gath(1, 2)
-        sub(0, 2, "v")
-        sub(1, 2, "v")
-        weight(0, 2)
-        weight(1, 2)
-        gath(0, 3)
-        gath(1, 3)
-        sub(0, 3, "v")
-        sub(1, 3, "v")
-        weight(0, 3)
-        weight(1, 3)
-        gath(2, 0)
-        gath(3, 0)
-        sub(2, 0, "v")
-        sub(3, 0, "v")
-        weight(2, 0)
-        weight(3, 0)
-        gath(2, 1)
-        gath(3, 1)
-        sub(2, 1, "v")
-        sub(3, 1, "v")
-        weight(2, 1)
-        weight(3, 1)
-        gath(2, 2)
-        gath(3, 2)
-        sub(2, 2, "v")
-        sub(3, 2, "v")
-        weight(2, 2)
-        weight(3, 2)
-        gath(2, 3)
-        gath(3, 3)
-        sub(2, 3, "v")
-        sub(3, 3, "v")
-        weight(2, 3)
-        weight(3, 3)
-        mult(0, 0, 256, "v")
-        mult(1, 0, 256, "v")
-        quant_z(0, 0, 512)
-        last_first()
-        mult(2, 0, 128, "v")
-        quant_z(1, 0, 128)
-        product(0, "s")
-        mult(2, 128, 256, "v")
-        quant_z(1, 128, 256)
-        product(1, "s")
-        mult(3, 0, 128, "v")
-        quant_z(1, 256, 384)
-        product(2, "s")
-        mult(3, 128, 256, "v")
-        quant_z(1, 384, 512)
-        last_second()
+        influence(0, 0)
+        round_w1(1, 1, 0, copy_on_gpsimd)
+        round_w1(1, 1, 1, nc.scalar.copy)
+        for a in range(2):
+            quantise_w1(1, a, 0, PACK)
+        for t in range(PACK):
+            make_h(1, t)
+        for slot in range(1, 2 * PACK):
+            influence(*divmod(slot, PACK))
+
+        z0_rounded = keep.tile([P, PACK * PAIRS], BF16, name="z0_rounded", align_bytes=64)
+        all_pairs = slice(0, PAIRS)
+        multiply(0, all_pairs, z0_rounded[:])
+        quantise_z(0, all_pairs, z0_rounded[:])
+
+        last_cols = slice(PAIRS - CHUNK, PAIRS)
+        last_accs = []
+        for i in range(out_tiles):
+            last_accs.append(out_psum.tile([P, CHUNK], F32, name="out_acc"))
+            out_pass(last_accs[i][:], i, last_cols, 0)
+
+        for chunk in range(CHUNKS):
+            cols = slice(CHUNK * chunk, CHUNK * (chunk + 1))
+            z1_rounded = keep.tile([P, PACK * CHUNK], BF16, name="z1_rounded", align_bytes=64, bufs=2)
+            multiply(1, cols, z1_rounded[:])
+            quantise_z(1, cols, z1_rounded[:])
+            result = keep.tile([P, out_tiles, CHUNK], F32, name=f"result{chunk}")
+            if chunk < CHUNKS - 1:
+                acc = out_psum.tile([P, out_tiles, CHUNK], F32, name="out_acc")
+                for i in range(out_tiles):
+                    for b in range(2):
+                        out_pass(acc[:, i, :], i, cols, b)
+                nc.scalar.copy(out=result[:], in_=acc[:])
+                nc.sync.dma_start(out=out_by_tile[:, :, cols], in_=result[:])
+            else:
+                for i in range(out_tiles):
+                    out_pass(last_accs[i][:], i, cols, 1)
+                    nc.vector.tensor_copy(out=result[:, i, :], in_=last_accs[i][:])
+                    if i % 2 == 1:
+                        nc.sync.dma_start(out=out_by_tile[:, i - 1 : i + 1, cols], in_=result[:, i - 1 : i + 1, :])

@@ -23,9 +23,9 @@ BANK = 512
 HALF = PASS // 2
 CHUNK = 128
 CHUNKS = PAIRS // CHUNK
-H_BANKS = 2
 SMALLEST = 2.0**-126
 STAGE_BYTES = 2 * PACK * PASS
+GROUP1_RANGES = ((0, 512),)
 
 
 def tile_list_robust_station_increments_kernel(
@@ -35,8 +35,7 @@ def tile_list_robust_station_increments_kernel(
     with ExitStack() as ctx:
         keep = ctx.enter_context(tc.tile_pool(name="keep", bufs=1))
         stage = ctx.enter_context(tc.tile_pool(name="stage", bufs=1))
-        h_psum = ctx.enter_context(tc.psum_pool(name="h_psum", bufs=H_BANKS))
-        out_psum = ctx.enter_context(tc.psum_pool(name="out_psum", bufs=8 - H_BANKS))
+        psum = ctx.enter_context(tc.psum_pool(name="psum", bufs=8))
 
         idx_list = keep.tile([P, S // 16], U16, name="idx_list")
         p1_list = keep.tile([P, PAIRS // 16], U16, name="p1_list")
@@ -54,31 +53,32 @@ def tile_list_robust_station_increments_kernel(
 
         w1_raw = {}
 
-        def load_w1(b, a, half):
-            w1_raw[b, a, half] = keep.tile([P, PACK, HALF], F32, name=f"w1_raw{b}{a}{half}")
-            first = PASS * b + HALF * half
-            rows = w1[PASS * a : PASS * (a + 1), first : first + HALF]
-            nc.sync.dma_start(out=w1_raw[b, a, half][:], in_=rows.rearrange("(p j) c -> p j c", j=PACK))
+        def load_w1(b, a, first, width):
+            raw = keep.tile([P, PACK, width], F32, name=f"w1_raw{b}{a}{first}")
+            rows = w1[PASS * a : PASS * (a + 1), PASS * b + first : PASS * b + first + width]
+            nc.sync.dma_start(out=raw[:], in_=rows.rearrange("(p j) c -> p j c", j=PACK))
+            for start in range(0, width, HALF):
+                w1_raw[b, a, (first + start) // HALF] = raw[:, :, start : start + HALF]
 
         def load_table_words(a):
             nc.sync.dma_start(out=table_words[a][:], in_=tab_words[a].rearrange("p t i -> p (t i)").bitcast(I32))
 
         nc.sync.dma_start(idx_list[:], offs)
-        nc.sync.dma_start(out=gain_tile[:], in_=gain.rearrange("(b p t) -> p b t", b=2, t=PACK))
         load_table_words(0)
         for quad in range(4):
             nc.sync.dma_start(
                 out=table_scales[32 * quad : 32 * quad + 8, :],
                 in_=tab_scales.bitcast(I32)[:, 4 * quad : 4 * quad + 4, :],
             )
+        nc.sync.dma_start(out=gain_tile[:], in_=gain.rearrange("(b p t) -> p b t", b=2, t=PACK))
+        load_w1(0, 0, 0, PASS)
         load_table_words(1)
-        for b, a in ((0, 0), (0, 1), (1, 0)):
-            for half in range(2):
-                load_w1(b, a, half)
+        load_w1(0, 1, 0, HALF)
+        load_w1(0, 1, HALF, HALF)
+        load_w1(1, 0, 0, PASS)
         nc.sync.dma_start(p1_list[:], pos1)
         nc.sync.dma_start(p2_list[:], pos2)
-        for half in range(2):
-            load_w1(1, 1, half)
+        load_w1(1, 1, 0, PASS)
         nc.sync.dma_start(out=w4_word_tile[:], in_=w4_words.bitcast(I32).rearrange("b p c -> p b c"))
         for quad in range(4):
             nc.sync.dma_start(
@@ -86,24 +86,22 @@ def tile_list_robust_station_increments_kernel(
                 in_=w4_scales.bitcast(I32)[:, 4 * quad : 4 * quad + 4, :].rearrange("b i c -> i b c"),
             )
 
+        slots = 2 * PACK
         gains = gain_tile[:].rearrange("p b t -> p (b t)")
-        size, floored, inverse, invroot, root, root_squared, fix, twice_positive, sign = (
-            keep.tile([P, 2 * PACK], F32, name=f"gain_{name}")
-            for name in ("size", "floored", "inverse", "invroot", "root", "root_squared", "fix", "twice", "sign")
+        twice_positive, sign, size, root_squared, fix = (
+            keep.tile([P, slots], F32, name=f"gain_{name}") for name in ("twice", "sign", "size", "root_squared", "fix")
         )
-        nc.vector.scalar_tensor_tensor(size[:], gains, -1.0, gains, ALU.mult, ALU.max)
-        nc.vector.tensor_scalar(floored[:], size[:], SMALLEST, None, ALU.max)
-        nc.vector.reciprocal(inverse[:], floored[:])
-        nc.scalar.activation(invroot[:], floored[:], ACT.Abs_reciprocal_sqrt)
-        nc.vector.reciprocal(root[:], invroot[:])
-        nc.gpsimd.tensor_tensor(root_squared[:], root[:], root[:], ALU.mult)
-        nc.gpsimd.tensor_tensor(fix[:], root_squared[:], inverse[:], ALU.mult)
+        to_invert = keep.tile([P, 2, slots], F32, name="gain_to_invert")
+        inverted = keep.tile([P, 2, slots], F32, name="gain_inverted")
+        floored, inverse, root = to_invert[:, 0, :], inverted[:, 0, :], inverted[:, 1, :]
         nc.gpsimd.tensor_scalar(twice_positive[:], gains, 0.0, 2.0, ALU.is_ge, ALU.mult)
         nc.gpsimd.tensor_scalar(sign[:], twice_positive[:], 1.0, -1.0, ALU.mult, ALU.add)
-
-        nc.vector.tensor_copy(out=v_words[0][:], in_=table_words[0][:].bitcast(U32).indirect(idx_list[:]))
-        nc.vector.tensor_copy(out=v_scales[:], in_=table_scales[:].bitcast(U8).indirect(idx_list[:]))
-        nc.vector.tensor_copy(out=v_words[1][:], in_=table_words[1][:].bitcast(U32).indirect(idx_list[:]))
+        nc.gpsimd.tensor_tensor(size[:], gains, sign[:], ALU.mult)
+        nc.gpsimd.tensor_scalar(floored, size[:], SMALLEST, None, ALU.max)
+        nc.scalar.activation(to_invert[:, 1, :], floored, ACT.Abs_reciprocal_sqrt)
+        nc.vector.reciprocal(inverted[:], to_invert[:])
+        nc.gpsimd.tensor_tensor(root_squared[:], root, root, ALU.mult)
+        nc.gpsimd.tensor_tensor(fix[:], root_squared[:], inverse, ALU.mult)
 
         w1_rounded = {}
         w1_words = {}
@@ -116,17 +114,17 @@ def tile_list_robust_station_increments_kernel(
         def copy_on_gpsimd(dst, src):
             nc.gpsimd.tensor_scalar(dst, src, 1.0, 0.0, ALU.mult, ALU.add)
 
-        def round_w1(b, a, half, copy):
-            if half == 0:
+        def round_w1(b, a, half, copy, first=0, end=HALF // PACK):
+            if (b, a) not in w1_rounded:
                 area = (a + b + 1) % 2
                 w1_rounded[b, a] = stage.tile(
                     [P, PACK * PASS], BF16, name=f"w1_rounded{b}{a}", align_bytes=64, offset=STAGE_BYTES * area
                 )
             by_column = w1_rounded[b, a][:].rearrange("p (t m j) -> p m t j", t=PACK, j=PACK)
-            per_half = HALF // PACK
+            base = HALF // PACK * half
             copy(
-                by_column[:, per_half * half : per_half * (half + 1), :, :],
-                w1_raw[b, a, half][:].rearrange("p j (m t) -> p m t j", t=PACK),
+                by_column[:, base + first : base + end, :, :],
+                w1_raw[b, a, half].rearrange("p j (m t) -> p m t j", t=PACK)[:, first:end, :, :],
             )
 
         def quantise_w1(b, a, first_slot, end_slot):
@@ -138,136 +136,169 @@ def tile_list_robust_station_increments_kernel(
             )
 
         h = {}
+        h_acc = {}
 
-        def make_h(b, t):
-            h[b, t] = keep.tile([P, S], F32, name=f"h{b}{t}")
-            row_sign = sign[:, PACK * b + t : PACK * b + t + 1]
+        def h_pass(b, t, a):
             slot_cols = slice(P * t, P * (t + 1))
             for bank in range(S // BANK):
                 cols = slice(BANK * bank, BANK * (bank + 1))
-                acc = h_psum.tile([P, BANK], F32, name="h_acc")
-                for a in range(2):
-                    nc.tensor.matmul_mx(
-                        out=acc[:],
-                        lhsT=w1_words[b, a][:, slot_cols].bitcast(FP8X4),
-                        lhsT_scale=w1_scales[b, a][:, slot_cols],
-                        rhs=v_words[a][:, cols].bitcast(FP8X4),
-                        rhs_scale=v_scales[4 * a :, cols],
-                        start=(a == 0),
-                        stop=(a == 1),
-                    )
+                if a == 0:
+                    h_acc[b, t, bank] = psum.tile([P, BANK], F32, name="acc")
+                nc.tensor.matmul_mx(
+                    out=h_acc[b, t, bank][:],
+                    lhsT=w1_words[b, a][:, slot_cols].bitcast(FP8X4),
+                    lhsT_scale=w1_scales[b, a][:, slot_cols],
+                    rhs=v_words[a][:, cols].bitcast(FP8X4),
+                    rhs_scale=v_scales[4 * a :, cols],
+                    start=(a == 0),
+                    stop=(a == 1),
+                )
+
+        def fetch_h(b, t):
+            if (b, t) == (1, PACK - 1):
+                h[b, t] = stage.tile([P, S], F32, name=f"h{b}{t}", align_bytes=64, offset=2 * STAGE_BYTES)
+            else:
+                h[b, t] = keep.tile([P, S], F32, name=f"h{b}{t}")
+            row_sign = sign[:, PACK * b + t : PACK * b + t + 1]
+            for bank in range(S // BANK):
+                cols = slice(BANK * bank, BANK * (bank + 1))
                 if (b, t, bank) == (0, 0, 1):
-                    nc.vector.tensor_scalar(h[b, t][:, cols], acc[:], row_sign, None, ALU.mult)
+                    nc.vector.tensor_scalar(h[b, t][:, cols], h_acc[b, t, bank][:], row_sign, None, ALU.mult)
                 else:
-                    nc.scalar.activation(h[b, t][:, cols], acc[:], ACT.Copy, scale=row_sign)
+                    nc.scalar.activation(h[b, t][:, cols], h_acc[b, t, bank][:], ACT.Copy, scale=row_sign)
+
+        def make_h(b, t):
+            h_pass(b, t, 0)
+            h_pass(b, t, 1)
+            fetch_h(b, t)
 
         departure = {}
         weight = {}
 
-        def influence(b, t):
+        def influence(b, t, first, end, fused):
+            width = end - first
             if t == 0:
-                departure[b] = keep.tile([P, PACK, PAIRS], F32, name=f"departure{b}")
-                weight[b] = keep.tile([P, PACK, PAIRS], F32, name=f"weight{b}")
-            picks = []
+                departure[b, first] = keep.tile([P, PACK, width], F32, name=f"departure{b}_{first}")
+                weight[b, first] = keep.tile([P, PACK, width], F32, name=f"weight{b}_{first}")
+            work = []
             for side in range(2):
-                name = f"pick{b}{t}{side}"
-                if b == 0 and t >= 2:
-                    offset = STAGE_BYTES * (t - 2) + STAGE_BYTES // 2 * side
-                    picks.append(stage.tile([P, PAIRS], F32, name=name, align_bytes=64, offset=offset))
+                name = f"work{b}{t}{side}_{first}"
+                if (b, t) == (0, PACK - 1):
+                    offset = STAGE_BYTES * side
+                    work.append(stage.tile([P, width], F32, name=name, align_bytes=64, offset=offset))
                 else:
-                    picks.append(keep.tile([P, PAIRS], F32, name=name))
-            nc.vector.tensor_copy(out=picks[0][:], in_=h[b, t][:].indirect(p1_list[:]))
-            nc.vector.tensor_copy(out=picks[1][:], in_=h[b, t][:].indirect(p2_list[:]))
-            d = departure[b][:, t, :]
-            subtractor = nc.vector if (b, t) == (1, PACK - 1) else nc.gpsimd
-            subtractor.tensor_tensor(d, picks[0][:], picks[1][:], ALU.subtract)
-            squared, shrink = picks
+                    work.append(keep.tile([P, width], F32, name=name))
+            entries = slice(first // 16, end // 16)
+            d = departure[b, first][:, t, :]
+            nc.vector.tensor_copy(out=work[1][:], in_=h[b, t][:].indirect(p2_list[:, entries]))
+            if fused:
+                nc.vector.tensor_tensor(d, h[b, t][:].indirect(p1_list[:, entries]), work[1][:], ALU.subtract)
+            else:
+                nc.vector.tensor_copy(out=work[0][:], in_=h[b, t][:].indirect(p1_list[:, entries]))
+                nc.gpsimd.tensor_tensor(d, work[0][:], work[1][:], ALU.subtract)
+            squared, shrink = work
             col = slice(PACK * b + t, PACK * b + t + 1)
             nc.scalar.activation(squared[:], d, ACT.Square)
             nc.scalar.activation(shrink[:], squared[:], ACT.Abs_reciprocal_sqrt, bias=fix[:, col], scale=fix[:, col])
-            nc.scalar.activation(weight[b][:, t, :], shrink[:], ACT.Square, scale=root[:, col])
+            nc.scalar.activation(weight[b, first][:, t, :], shrink[:], ACT.Square, scale=root[:, col])
 
-        z_words = [keep.tile([P, PAIRS], U32, name=f"z_words{b}", align_bytes=64) for b in range(2)]
-        z_scales = [keep.tile([P, PAIRS], U8, name=f"z_scales{b}", align_bytes=64) for b in range(2)]
+        z_words = {}
+        z_scales = {}
 
-        def multiply(b, cols, rounded):
+        def make_z(b, base, first, end):
+            width = end - first
+            cols = slice(first - base, end - base)
+            if b == 0:
+                rounded = stage.tile([P, PACK * width], BF16, name="z_rounded0", align_bytes=64, offset=2 * STAGE_BYTES)
+            else:
+                rounded = keep.tile([P, PACK * width], BF16, name=f"z_rounded{b}_{first}", align_bytes=64)
+            words = keep.tile([P, width], U32, name=f"z_words{b}_{first}", align_bytes=64)
+            scales = keep.tile([P, width], U8, name=f"z_scales{b}_{first}", align_bytes=64)
             nc.vector.tensor_tensor(
-                rounded.rearrange("p (c i t) -> p c t i", i=4, t=PACK),
-                departure[b][:, :, cols].rearrange("p t (c i) -> p c t i", i=4),
-                weight[b][:, :, cols].rearrange("p t (c i) -> p c t i", i=4),
+                rounded[:].rearrange("p (c i t) -> p c t i", i=4, t=PACK),
+                departure[b, base][:, :, cols].rearrange("p t (c i) -> p c t i", i=4),
+                weight[b, base][:, :, cols].rearrange("p t (c i) -> p c t i", i=4),
                 ALU.mult,
             )
-
-        def quantise_z(b, cols, rounded):
-            nc.vector.quantize_mx(out=z_words[b][:, cols].bitcast(FP8X4), scales=z_scales[b][:, cols], in_=rounded)
+            nc.vector.quantize_mx(out=words[:].bitcast(FP8X4), scales=scales[:], in_=rounded[:])
+            for start in range(0, width, CHUNK):
+                z_words[b, (first + start) // CHUNK] = words[:, start : start + CHUNK]
+                z_scales[b, (first + start) // CHUNK] = scales[:, start : start + CHUNK]
 
         w4_word_bytes = w4_word_tile[:].bitcast(U8)
         w4_scale_bytes = w4_scale_tile[:].bitcast(U8)
         out_by_tile = out.rearrange("(i q) c -> q i c", q=P)
         out_tiles = N // P
+        out_acc = {}
 
-        def out_pass(acc, i, cols, b):
-            nc.tensor.matmul_mx(
-                out=acc,
-                lhsT=w4_word_bytes[:, b, 2 * P * i : 2 * P * (i + 1)].bitcast(FP4X4),
-                lhsT_scale=w4_scale_bytes[:, b, P * i : P * (i + 1)],
-                rhs=z_words[b][:, cols].bitcast(FP8X4),
-                rhs_scale=z_scales[b][:, cols],
-                start=(b == 0),
-                stop=(b == 1),
-            )
+        def out_passes(b, chunk, first_tile, end_tile):
+            if b == 0:
+                out_acc[chunk, first_tile] = psum.tile([P, end_tile - first_tile, CHUNK], F32, name="acc")
+            for i in range(first_tile, end_tile):
+                nc.tensor.matmul_mx(
+                    out=out_acc[chunk, first_tile][:, i - first_tile, :],
+                    lhsT=w4_word_bytes[:, b, 2 * P * i : 2 * P * (i + 1)].bitcast(FP4X4),
+                    lhsT_scale=w4_scale_bytes[:, b, P * i : P * (i + 1)],
+                    rhs=z_words[b, chunk].bitcast(FP8X4),
+                    rhs_scale=z_scales[b, chunk],
+                    start=(b == 0 and i == first_tile),
+                    stop=(b == 1 and i == end_tile - 1),
+                )
 
+        def finish(chunk, first_tile, end_tile, copy):
+            out_passes(1, chunk, first_tile, end_tile)
+            result = keep.tile([P, end_tile - first_tile, CHUNK], F32, name=f"result{chunk}{first_tile}")
+            copy(out=result[:], in_=out_acc[chunk, first_tile][:])
+            cols = slice(CHUNK * chunk, CHUNK * (chunk + 1))
+            nc.sync.dma_start(out=out_by_tile[:, first_tile:end_tile, cols], in_=result[:])
+
+        def gather_words(a):
+            nc.vector.tensor_copy(out=v_words[a][:], in_=table_words[a][:].bitcast(U32).indirect(idx_list[:]))
+
+        gather_words(0)
+        nc.vector.tensor_copy(out=v_scales[:], in_=table_scales[:].bitcast(U8).indirect(idx_list[:]))
         round_w1(0, 0, 0, nc.scalar.copy)
         round_w1(0, 0, 1, copy_on_gpsimd)
         quantise_w1(0, 0, 0, PACK)
+        gather_words(1)
+        for t in range(2):
+            h_pass(0, t, 0)
         round_w1(0, 1, 0, nc.scalar.copy)
-        round_w1(0, 1, 1, nc.vector.tensor_copy)
+        round_w1(0, 1, 1, nc.scalar.copy, 0, 32)
+        round_w1(0, 1, 1, nc.vector.tensor_copy, 32, 64)
         quantise_w1(0, 1, 0, 1)
-        make_h(0, 0)
+        h_pass(0, 0, 1)
+        fetch_h(0, 0)
         quantise_w1(0, 1, 1, 2)
         quantise_w1(0, 1, 2, PACK)
-        make_h(0, 1)
+        h_pass(0, 1, 1)
+        fetch_h(0, 1)
         make_h(0, 2)
         round_w1(1, 0, 0, copy_on_gpsimd)
         round_w1(1, 0, 1, copy_on_gpsimd)
+        round_w1(1, 1, 0, nc.scalar.copy)
         make_h(0, 3)
-        influence(0, 0)
-        round_w1(1, 1, 0, copy_on_gpsimd)
         round_w1(1, 1, 1, nc.scalar.copy)
+        influence(0, 0, 0, PAIRS, False)
+        influence(0, 1, 0, PAIRS, False)
         for a in range(2):
             quantise_w1(1, a, 0, PACK)
         for t in range(PACK):
             make_h(1, t)
-        for slot in range(1, 2 * PACK):
-            influence(*divmod(slot, PACK))
+        influence(0, 2, 0, PAIRS, False)
+        influence(0, 3, 0, PAIRS, False)
+        for first, end in GROUP1_RANGES:
+            for t in range(PACK):
+                influence(1, t, first, end, end == PAIRS and t == PACK - 1)
 
-        z0_rounded = keep.tile([P, PACK * PAIRS], BF16, name="z0_rounded", align_bytes=64)
-        all_pairs = slice(0, PAIRS)
-        multiply(0, all_pairs, z0_rounded[:])
-        quantise_z(0, all_pairs, z0_rounded[:])
-
-        last_cols = slice(PAIRS - CHUNK, PAIRS)
-        last_accs = []
-        for i in range(out_tiles):
-            last_accs.append(out_psum.tile([P, CHUNK], F32, name="out_acc"))
-            out_pass(last_accs[i][:], i, last_cols, 0)
-
-        for chunk in range(CHUNKS):
-            cols = slice(CHUNK * chunk, CHUNK * (chunk + 1))
-            z1_rounded = keep.tile([P, PACK * CHUNK], BF16, name="z1_rounded", align_bytes=64, bufs=2)
-            multiply(1, cols, z1_rounded[:])
-            quantise_z(1, cols, z1_rounded[:])
-            result = keep.tile([P, out_tiles, CHUNK], F32, name=f"result{chunk}")
-            if chunk < CHUNKS - 1:
-                acc = out_psum.tile([P, out_tiles, CHUNK], F32, name="out_acc")
-                for i in range(out_tiles):
-                    for b in range(2):
-                        out_pass(acc[:, i, :], i, cols, b)
-                nc.scalar.copy(out=result[:], in_=acc[:])
-                nc.sync.dma_start(out=out_by_tile[:, :, cols], in_=result[:])
-            else:
-                for i in range(out_tiles):
-                    out_pass(last_accs[i][:], i, cols, 1)
-                    nc.vector.tensor_copy(out=result[:, i, :], in_=last_accs[i][:])
-                    if i % 2 == 1:
-                        nc.sync.dma_start(out=out_by_tile[:, i - 1 : i + 1, cols], in_=result[:, i - 1 : i + 1, :])
+        banks = [(chunk, 0, out_tiles) for chunk in range(CHUNKS - 1)]
+        banks.extend([(CHUNKS - 1, 0, out_tiles // 2), (CHUNKS - 1, out_tiles // 2, out_tiles)])
+        make_z(0, 0, 0, PAIRS)
+        for bank in banks:
+            out_passes(0, *bank)
+        for base, end in GROUP1_RANGES:
+            for first in range(base, end, CHUNK):
+                make_z(1, base, first, first + CHUNK)
+                for bank in banks:
+                    if first == CHUNK * bank[0]:
+                        finish(*bank, nc.vector.tensor_copy if bank == banks[-1] else nc.scalar.copy)

@@ -279,17 +279,17 @@ def tile_list_robust_station_increments_kernel(
         round_w1(1, 1, 0, nc.scalar.copy)
         make_h(0, 3)
         round_w1(1, 1, 1, nc.scalar.copy)
-        influence(0, 0, 0, PAIRS, False)
-        influence(0, 1, 0, PAIRS, False)
+        influence(0, 0, 0, PAIRS, True)
+        influence(0, 1, 0, PAIRS, True)
         for a in range(2):
             quantise_w1(1, a, 0, PACK)
         for t in range(PACK):
             make_h(1, t)
-        influence(0, 2, 0, PAIRS, False)
-        influence(0, 3, 0, PAIRS, False)
+        influence(0, 2, 0, PAIRS, True)
+        influence(0, 3, 0, PAIRS, True)
         for first, end in GROUP1_RANGES:
             for t in range(PACK):
-                influence(1, t, first, end, end == PAIRS and t == PACK - 1)
+                influence(1, t, first, end, True)
 
         banks = [(chunk, 0, out_tiles) for chunk in range(CHUNKS - 1)]
         banks.extend([(CHUNKS - 1, 0, out_tiles // 2), (CHUNKS - 1, out_tiles // 2, out_tiles)])

@@ -25,7 +25,7 @@ CHUNK = 128
 CHUNKS = PAIRS // CHUNK
 SMALLEST = 2.0**-126
 STAGE_BYTES = 2 * PACK * PASS
-GROUP1_RANGES = ((0, 512),)
+LAST_RAW = 3 * STAGE_BYTES
 
 
 def tile_list_robust_station_increments_kernel(
@@ -54,7 +54,10 @@ def tile_list_robust_station_increments_kernel(
         w1_raw = {}
 
         def load_w1(b, a, first, width):
-            raw = keep.tile([P, PACK, width], F32, name=f"w1_raw{b}{a}{first}")
+            if (b, a) == (1, 1):
+                raw = stage.tile([P, PACK, width], F32, name="w1_raw11", align_bytes=64, offset=LAST_RAW)
+            else:
+                raw = keep.tile([P, PACK, width], F32, name=f"w1_raw{b}{a}{first}")
             rows = w1[PASS * a : PASS * (a + 1), PASS * b + first : PASS * b + first + width]
             nc.sync.dma_start(out=raw[:], in_=rows.rearrange("(p j) c -> p j c", j=PACK))
             for start in range(0, width, HALF):
@@ -108,7 +111,10 @@ def tile_list_robust_station_increments_kernel(
         w1_scales = {}
         for b in range(2):
             for a in range(2):
-                w1_words[b, a] = keep.tile([P, PASS], U32, name=f"w1_words{b}{a}", align_bytes=64)
+                if (b, a) == (1, 0):
+                    w1_words[b, a] = stage.tile([P, PASS], U32, name="w1_words10", align_bytes=64, offset=LAST_RAW)
+                else:
+                    w1_words[b, a] = keep.tile([P, PASS], U32, name=f"w1_words{b}{a}", align_bytes=64)
                 w1_scales[b, a] = keep.tile([P, PASS], U8, name=f"w1_scales{b}{a}", align_bytes=64)
 
         def copy_on_gpsimd(dst, src):
@@ -175,49 +181,47 @@ def tile_list_robust_station_increments_kernel(
         departure = {}
         weight = {}
 
-        def influence(b, t, first, end, fused):
-            width = end - first
+        picked = {}
+
+        def pick(b, t):
+            picked[b, t] = keep.tile([P, PAIRS], F32, name=f"picked{b}{t}")
+            nc.vector.tensor_copy(out=picked[b, t][:], in_=h[b, t][:].indirect(p2_list[:]))
+
+        def influence(b, t):
+            if (b, t) == (0, 0):
+                departure[b] = stage.tile(
+                    [P, PACK, PAIRS], F32, name="departure0", align_bytes=64, offset=LAST_RAW + STAGE_BYTES
+                )
+            elif t == 0:
+                departure[b] = keep.tile([P, PACK, PAIRS], F32, name=f"departure{b}")
             if t == 0:
-                departure[b, first] = keep.tile([P, PACK, width], F32, name=f"departure{b}_{first}")
-                weight[b, first] = keep.tile([P, PACK, width], F32, name=f"weight{b}_{first}")
-            work = []
-            for side in range(2):
-                name = f"work{b}{t}{side}_{first}"
-                if (b, t) == (0, PACK - 1):
-                    offset = STAGE_BYTES * side
-                    work.append(stage.tile([P, width], F32, name=name, align_bytes=64, offset=offset))
-                else:
-                    work.append(keep.tile([P, width], F32, name=name))
-            entries = slice(first // 16, end // 16)
-            d = departure[b, first][:, t, :]
-            nc.vector.tensor_copy(out=work[1][:], in_=h[b, t][:].indirect(p2_list[:, entries]))
-            if fused:
-                nc.vector.tensor_tensor(d, h[b, t][:].indirect(p1_list[:, entries]), work[1][:], ALU.subtract)
-            else:
-                nc.vector.tensor_copy(out=work[0][:], in_=h[b, t][:].indirect(p1_list[:, entries]))
-                nc.gpsimd.tensor_tensor(d, work[0][:], work[1][:], ALU.subtract)
-            squared, shrink = work
+                weight[b] = keep.tile([P, PACK, PAIRS], F32, name=f"weight{b}")
+            d = departure[b][:, t, :]
+            nc.vector.tensor_tensor(d, h[b, t][:].indirect(p1_list[:]), picked[b, t][:], ALU.subtract)
+            squared = keep.tile([P, PAIRS], F32, name=f"squared{b}{t}")
+            shrink = picked[b, t]
             col = slice(PACK * b + t, PACK * b + t + 1)
             nc.scalar.activation(squared[:], d, ACT.Square)
             nc.scalar.activation(shrink[:], squared[:], ACT.Abs_reciprocal_sqrt, bias=fix[:, col], scale=fix[:, col])
-            nc.scalar.activation(weight[b, first][:, t, :], shrink[:], ACT.Square, scale=root[:, col])
+            nc.scalar.activation(weight[b][:, t, :], shrink[:], ACT.Square, scale=root[:, col])
 
         z_words = {}
         z_scales = {}
 
-        def make_z(b, base, first, end):
+        def make_z(b, first, end):
             width = end - first
-            cols = slice(first - base, end - base)
+            cols = slice(first, end)
             if b == 0:
-                rounded = stage.tile([P, PACK * width], BF16, name="z_rounded0", align_bytes=64, offset=2 * STAGE_BYTES)
+                offset = 2 * STAGE_BYTES + 2 * PACK * first
+                rounded = stage.tile([P, PACK * width], BF16, name=f"z_rounded0_{first}", align_bytes=64, offset=offset)
             else:
                 rounded = keep.tile([P, PACK * width], BF16, name=f"z_rounded{b}_{first}", align_bytes=64)
             words = keep.tile([P, width], U32, name=f"z_words{b}_{first}", align_bytes=64)
             scales = keep.tile([P, width], U8, name=f"z_scales{b}_{first}", align_bytes=64)
             nc.vector.tensor_tensor(
                 rounded[:].rearrange("p (c i t) -> p c t i", i=4, t=PACK),
-                departure[b, base][:, :, cols].rearrange("p t (c i) -> p c t i", i=4),
-                weight[b, base][:, :, cols].rearrange("p t (c i) -> p c t i", i=4),
+                departure[b][:, :, cols].rearrange("p t (c i) -> p c t i", i=4),
+                weight[b][:, :, cols].rearrange("p t (c i) -> p c t i", i=4),
                 ALU.mult,
             )
             nc.vector.quantize_mx(out=words[:].bitcast(FP8X4), scales=scales[:], in_=rounded[:])
@@ -265,7 +269,7 @@ def tile_list_robust_station_increments_kernel(
             h_pass(0, t, 0)
         round_w1(0, 1, 0, nc.scalar.copy)
         round_w1(0, 1, 1, nc.scalar.copy, 0, 32)
-        round_w1(0, 1, 1, nc.vector.tensor_copy, 32, 64)
+        round_w1(0, 1, 1, copy_on_gpsimd, 32, 64)
         quantise_w1(0, 1, 0, 1)
         h_pass(0, 0, 1)
         fetch_h(0, 0)
@@ -274,31 +278,34 @@ def tile_list_robust_station_increments_kernel(
         h_pass(0, 1, 1)
         fetch_h(0, 1)
         make_h(0, 2)
+        make_h(0, 3)
         round_w1(1, 0, 0, copy_on_gpsimd)
         round_w1(1, 0, 1, copy_on_gpsimd)
-        round_w1(1, 1, 0, nc.scalar.copy)
-        make_h(0, 3)
+        round_w1(1, 1, 0, copy_on_gpsimd)
         round_w1(1, 1, 1, nc.scalar.copy)
-        influence(0, 0, 0, PAIRS, True)
-        influence(0, 1, 0, PAIRS, True)
-        for a in range(2):
-            quantise_w1(1, a, 0, PACK)
+        for t in range(PACK):
+            pick(0, t)
+        influence(0, 0)
+        quantise_w1(1, 0, 0, PACK)
+        influence(0, 1)
+        quantise_w1(1, 1, 0, PACK)
         for t in range(PACK):
             make_h(1, t)
-        influence(0, 2, 0, PAIRS, True)
-        influence(0, 3, 0, PAIRS, True)
-        for first, end in GROUP1_RANGES:
-            for t in range(PACK):
-                influence(1, t, first, end, True)
+        influence(0, 2)
+        influence(0, 3)
+        for t in range(PACK):
+            pick(1, t)
+            influence(1, t)
 
         banks = [(chunk, 0, out_tiles) for chunk in range(CHUNKS - 1)]
         banks.extend([(CHUNKS - 1, 0, out_tiles // 2), (CHUNKS - 1, out_tiles // 2, out_tiles)])
-        make_z(0, 0, 0, PAIRS)
-        for bank in banks:
-            out_passes(0, *bank)
-        for base, end in GROUP1_RANGES:
-            for first in range(base, end, CHUNK):
-                make_z(1, base, first, first + CHUNK)
-                for bank in banks:
-                    if first == CHUNK * bank[0]:
-                        finish(*bank, nc.vector.tensor_copy if bank == banks[-1] else nc.scalar.copy)
+        for first in range(0, PAIRS, 2 * CHUNK):
+            make_z(0, first, first + 2 * CHUNK)
+            for bank in banks:
+                if first <= CHUNK * bank[0] < first + 2 * CHUNK:
+                    out_passes(0, *bank)
+        for first in range(0, PAIRS, CHUNK):
+            make_z(1, first, first + CHUNK)
+            for bank in banks:
+                if first == CHUNK * bank[0]:
+                    finish(*bank, nc.vector.tensor_copy if bank[0] == CHUNKS - 1 else nc.scalar.copy)

@@ -25,6 +25,9 @@ CHUNK = 128
 CHUNKS = PAIRS // CHUNK
 SMALLEST = 2.0**-126
 STAGE_BYTES = 2 * PACK * PASS
+SCALAR_SHARE = 38
+LATE = 6 * STAGE_BYTES
+RAW11 = 8 * STAGE_BYTES
 LAST_RAW = 3 * STAGE_BYTES
 
 
@@ -54,8 +57,10 @@ def tile_list_robust_station_increments_kernel(
         w1_raw = {}
 
         def load_w1(b, a, first, width):
-            if (b, a) == (1, 1):
-                raw = stage.tile([P, PACK, width], F32, name="w1_raw11", align_bytes=64, offset=LAST_RAW)
+            if (b, a) == (1, 0):
+                raw = stage.tile([P, PACK, width], F32, name="w1_raw10", align_bytes=64, offset=LAST_RAW)
+            elif (b, a) == (1, 1):
+                raw = stage.tile([P, PACK, width], F32, name="w1_raw11", align_bytes=64, offset=RAW11)
             else:
                 raw = keep.tile([P, PACK, width], F32, name=f"w1_raw{b}{a}{first}")
             rows = w1[PASS * a : PASS * (a + 1), PASS * b + first : PASS * b + first + width]
@@ -111,10 +116,7 @@ def tile_list_robust_station_increments_kernel(
         w1_scales = {}
         for b in range(2):
             for a in range(2):
-                if (b, a) == (1, 0):
-                    w1_words[b, a] = stage.tile([P, PASS], U32, name="w1_words10", align_bytes=64, offset=LAST_RAW)
-                else:
-                    w1_words[b, a] = keep.tile([P, PASS], U32, name=f"w1_words{b}{a}", align_bytes=64)
+                w1_words[b, a] = keep.tile([P, PASS], U32, name=f"w1_words{b}{a}", align_bytes=64)
                 w1_scales[b, a] = keep.tile([P, PASS], U8, name=f"w1_scales{b}{a}", align_bytes=64)
 
         def copy_on_gpsimd(dst, src):
@@ -146,10 +148,11 @@ def tile_list_robust_station_increments_kernel(
 
         def h_pass(b, t, a):
             slot_cols = slice(P * t, P * (t + 1))
-            for bank in range(S // BANK):
-                cols = slice(BANK * bank, BANK * (bank + 1))
+            width = BANK // 2 if (b, t) == (0, 0) else BANK
+            for bank in range(S // width):
+                cols = slice(width * bank, width * (bank + 1))
                 if a == 0:
-                    h_acc[b, t, bank] = psum.tile([P, BANK], F32, name="acc")
+                    h_acc[b, t, bank] = psum.tile([P, width], F32, name="acc")
                 nc.tensor.matmul_mx(
                     out=h_acc[b, t, bank][:],
                     lhsT=w1_words[b, a][:, slot_cols].bitcast(FP8X4),
@@ -166,9 +169,10 @@ def tile_list_robust_station_increments_kernel(
             else:
                 h[b, t] = keep.tile([P, S], F32, name=f"h{b}{t}")
             row_sign = sign[:, PACK * b + t : PACK * b + t + 1]
-            for bank in range(S // BANK):
-                cols = slice(BANK * bank, BANK * (bank + 1))
-                if (b, t, bank) == (0, 0, 1):
+            width = BANK // 2 if (b, t) == (0, 0) else BANK
+            for bank in range(S // width):
+                cols = slice(width * bank, width * (bank + 1))
+                if (b, t) == (0, 0) and bank % 2 == 1:
                     nc.vector.tensor_scalar(h[b, t][:, cols], h_acc[b, t, bank][:], row_sign, None, ALU.mult)
                 else:
                     nc.scalar.activation(h[b, t][:, cols], h_acc[b, t, bank][:], ACT.Copy, scale=row_sign)
@@ -184,26 +188,39 @@ def tile_list_robust_station_increments_kernel(
         picked = {}
 
         def pick(b, t):
-            picked[b, t] = keep.tile([P, PAIRS], F32, name=f"picked{b}{t}")
+            if (b, t) == (0, PACK - 1):
+                picked[b, t] = stage.tile([P, PAIRS], F32, name="picked03", align_bytes=64, offset=RAW11)
+            else:
+                picked[b, t] = keep.tile([P, PAIRS], F32, name=f"picked{b}{t}")
             nc.vector.tensor_copy(out=picked[b, t][:], in_=h[b, t][:].indirect(p2_list[:]))
 
-        def influence(b, t):
+        def depart(b, t):
             if (b, t) == (0, 0):
                 departure[b] = stage.tile(
                     [P, PACK, PAIRS], F32, name="departure0", align_bytes=64, offset=LAST_RAW + STAGE_BYTES
                 )
             elif t == 0:
-                departure[b] = keep.tile([P, PACK, PAIRS], F32, name=f"departure{b}")
+                departure[b] = stage.tile([P, PACK, PAIRS], F32, name="departure1", align_bytes=64, offset=LATE)
             if t == 0:
                 weight[b] = keep.tile([P, PACK, PAIRS], F32, name=f"weight{b}")
             d = departure[b][:, t, :]
             nc.vector.tensor_tensor(d, h[b, t][:].indirect(p1_list[:]), picked[b, t][:], ALU.subtract)
-            squared = keep.tile([P, PAIRS], F32, name=f"squared{b}{t}")
-            shrink = picked[b, t]
+
+        def weigh(b, t, squared):
+            shrink = keep.tile([P, PAIRS], F32, name=f"shrink{b}{t}")
             col = slice(PACK * b + t, PACK * b + t + 1)
-            nc.scalar.activation(squared[:], d, ACT.Square)
-            nc.scalar.activation(shrink[:], squared[:], ACT.Abs_reciprocal_sqrt, bias=fix[:, col], scale=fix[:, col])
+            nc.scalar.activation(shrink[:], squared, ACT.Abs_reciprocal_sqrt, bias=fix[:, col], scale=fix[:, col])
             nc.scalar.activation(weight[b][:, t, :], shrink[:], ACT.Square, scale=root[:, col])
+
+        def influence(b, t):
+            depart(b, t)
+            if b == 0:
+                offset = RAW11 + STAGE_BYTES // 2 * (t + 1)
+                squared = stage.tile([P, PAIRS], F32, name=f"squared{b}{t}", align_bytes=64, offset=offset)
+            else:
+                squared = keep.tile([P, PAIRS], F32, name=f"squared{b}{t}")
+            nc.scalar.activation(squared[:], departure[b][:, t, :], ACT.Square)
+            weigh(b, t, squared[:])
 
         z_words = {}
         z_scales = {}
@@ -267,9 +284,9 @@ def tile_list_robust_station_increments_kernel(
         gather_words(1)
         for t in range(2):
             h_pass(0, t, 0)
-        round_w1(0, 1, 0, nc.scalar.copy)
-        round_w1(0, 1, 1, nc.scalar.copy, 0, 32)
-        round_w1(0, 1, 1, copy_on_gpsimd, 32, 64)
+        for half in range(2):
+            round_w1(0, 1, half, nc.scalar.copy, 0, SCALAR_SHARE)
+            round_w1(0, 1, half, copy_on_gpsimd, SCALAR_SHARE, HALF // PACK)
         quantise_w1(0, 1, 0, 1)
         h_pass(0, 0, 1)
         fetch_h(0, 0)
@@ -281,20 +298,30 @@ def tile_list_robust_station_increments_kernel(
         make_h(0, 3)
         round_w1(1, 0, 0, copy_on_gpsimd)
         round_w1(1, 0, 1, copy_on_gpsimd)
-        round_w1(1, 1, 0, copy_on_gpsimd)
+        round_w1(1, 1, 0, nc.scalar.copy)
         round_w1(1, 1, 1, nc.scalar.copy)
-        for t in range(PACK):
-            pick(0, t)
+        pick(0, 0)
+        pick(0, 1)
         influence(0, 0)
         quantise_w1(1, 0, 0, PACK)
+        for t in range(PACK):
+            h_pass(1, t, 0)
+        pick(0, 2)
         influence(0, 1)
         quantise_w1(1, 1, 0, PACK)
         for t in range(PACK):
-            make_h(1, t)
-        influence(0, 2)
-        influence(0, 3)
+            h_pass(1, t, 1)
+            fetch_h(1, t)
+        pick(0, 3)
+        depart(0, 2)
+        depart(0, 3)
+        last_squares = stage.tile([P, 2, PAIRS], F32, name="last_squares", align_bytes=64, offset=LATE)
+        nc.gpsimd.tensor_tensor(last_squares[:], departure[0][:, 2:, :], departure[0][:, 2:, :], ALU.mult)
+        weigh(0, 2, last_squares[:, 0, :])
+        weigh(0, 3, last_squares[:, 1, :])
         for t in range(PACK):
             pick(1, t)
+        for t in range(PACK):
             influence(1, t)
 
         banks = [(chunk, 0, out_tiles) for chunk in range(CHUNKS - 1)]
@@ -308,4 +335,4 @@ def tile_list_robust_station_increments_kernel(
             make_z(1, first, first + CHUNK)
             for bank in banks:
                 if first == CHUNK * bank[0]:
-                    finish(*bank, nc.vector.tensor_copy if bank[0] == CHUNKS - 1 else nc.scalar.copy)
+                    finish(*bank, nc.vector.tensor_copy if bank == banks[-2] else nc.scalar.copy)

@@ -23,12 +23,17 @@ BANK = 512
 HALF = PASS // 2
 CHUNK = 128
 CHUNKS = PAIRS // CHUNK
+RANGE = PAIRS // 2
 SMALLEST = 2.0**-126
-STAGE_BYTES = 2 * PACK * PASS
 SCALAR_SHARE = 38
-LATE = 6 * STAGE_BYTES
-RAW11 = 8 * STAGE_BYTES
-LAST_RAW = 3 * STAGE_BYTES
+
+KIB = 1024
+ROUNDED = 0
+RAW10 = 8 * KIB
+RAW11 = 16 * KIB
+SIGN11 = 24 * KIB
+LAST_H = 32 * KIB
+FIX13 = 36 * KIB
 
 
 def tile_list_robust_station_increments_kernel(
@@ -37,32 +42,32 @@ def tile_list_robust_station_increments_kernel(
     nc = tc.nc
     with ExitStack() as ctx:
         keep = ctx.enter_context(tc.tile_pool(name="keep", bufs=1))
-        stage = ctx.enter_context(tc.tile_pool(name="stage", bufs=1))
+        shared = ctx.enter_context(tc.tile_pool(name="shared", bufs=1))
         psum = ctx.enter_context(tc.psum_pool(name="psum", bufs=8))
+
+        def sbuf(name, shape, dtype, offset=None):
+            if offset is None:
+                return keep.tile(shape, dtype, name=name, align_bytes=64)
+            return shared.tile(shape, dtype, name=name, align_bytes=64, offset=offset)
 
         idx_list = keep.tile([P, S // 16], U16, name="idx_list")
         p1_list = keep.tile([P, PAIRS // 16], U16, name="p1_list")
         p2_list = keep.tile([P, PAIRS // 16], U16, name="p2_list")
-        table_words = [keep.tile([P, T], I32, name=f"table_words{a}", align_bytes=64) for a in range(2)]
-        table_scales = keep.tile([P, T // 4], I32, name="table_scales", align_bytes=64)
-        v_words = [keep.tile([P, S], U32, name=f"v_words{a}", align_bytes=64) for a in range(2)]
-        v_scales = keep.tile([P, S], U8, name="v_scales", align_bytes=64)
-        w4_word_tile = keep.tile([P, 2, 2 * N // 4], I32, name="w4_word_tile", align_bytes=64)
-        w4_scale_tile = keep.tile([P, 2, N // 4], I32, name="w4_scale_tile", align_bytes=64)
-        gain_tile = keep.tile([P, 2, PACK], F32, name="gain_tile")
+        table_words = [sbuf(f"table_words{a}", [P, T], I32) for a in range(2)]
+        table_scales = sbuf("table_scales", [P, T // 4], I32)
+        v_words = [sbuf(f"v_words{a}", [P, S], U32) for a in range(2)]
+        v_scales = sbuf("v_scales", [P, S], U8)
+        w4_word_tile = sbuf("w4_word_tile", [P, 2, 2 * N // 4], I32)
+        w4_scale_tile = sbuf("w4_scale_tile", [P, 2, N // 4], I32)
+        gain_tile = sbuf("gain_tile", [P, 2, PACK], F32)
 
         nc.vector.memset(table_scales[:], 0)
         nc.vector.memset(w4_scale_tile[:], 0)
 
         w1_raw = {}
 
-        def load_w1(b, a, first, width):
-            if (b, a) == (1, 0):
-                raw = stage.tile([P, PACK, width], F32, name="w1_raw10", align_bytes=64, offset=LAST_RAW)
-            elif (b, a) == (1, 1):
-                raw = stage.tile([P, PACK, width], F32, name="w1_raw11", align_bytes=64, offset=RAW11)
-            else:
-                raw = keep.tile([P, PACK, width], F32, name=f"w1_raw{b}{a}{first}")
+        def load_w1(b, a, first, width, offset=None):
+            raw = sbuf(f"w1_raw{b}{a}{first}", [P, PACK, width], F32, offset)
             rows = w1[PASS * a : PASS * (a + 1), PASS * b + first : PASS * b + first + width]
             nc.sync.dma_start(out=raw[:], in_=rows.rearrange("(p j) c -> p j c", j=PACK))
             for start in range(0, width, HALF):
@@ -83,10 +88,10 @@ def tile_list_robust_station_increments_kernel(
         load_table_words(1)
         load_w1(0, 1, 0, HALF)
         load_w1(0, 1, HALF, HALF)
-        load_w1(1, 0, 0, PASS)
-        nc.sync.dma_start(p1_list[:], pos1)
         nc.sync.dma_start(p2_list[:], pos2)
-        load_w1(1, 1, 0, PASS)
+        nc.sync.dma_start(p1_list[:], pos1)
+        load_w1(1, 0, 0, PASS, RAW10)
+        load_w1(1, 1, 0, PASS, RAW11)
         nc.sync.dma_start(out=w4_word_tile[:], in_=w4_words.bitcast(I32).rearrange("b p c -> p b c"))
         for quad in range(4):
             nc.sync.dma_start(
@@ -94,30 +99,32 @@ def tile_list_robust_station_increments_kernel(
                 in_=w4_scales.bitcast(I32)[:, 4 * quad : 4 * quad + 4, :].rearrange("b i c -> i b c"),
             )
 
-        slots = 2 * PACK
-        gains = gain_tile[:].rearrange("p b t -> p (b t)")
         twice_positive, sign, size, root_squared, fix = (
-            keep.tile([P, slots], F32, name=f"gain_{name}") for name in ("twice", "sign", "size", "root_squared", "fix")
+            sbuf(f"gain_{name}", [P, 2, PACK], F32) for name in ("twice", "sign", "size", "root_squared", "fix")
         )
-        to_invert = keep.tile([P, 2, slots], F32, name="gain_to_invert")
-        inverted = keep.tile([P, 2, slots], F32, name="gain_inverted")
-        floored, inverse, root = to_invert[:, 0, :], inverted[:, 0, :], inverted[:, 1, :]
-        nc.gpsimd.tensor_scalar(twice_positive[:], gains, 0.0, 2.0, ALU.is_ge, ALU.mult)
+        sign11 = sbuf("sign11", [P, 1], F32, SIGN11)
+        fix13 = sbuf("fix13", [P, 1], F32, FIX13)
+        to_invert = sbuf("gain_to_invert", [P, 2, 2, PACK], F32)
+        inverted = sbuf("gain_inverted", [P, 2, 2, PACK], F32)
+        floored, inverse, root = to_invert[:, 0, :, :], inverted[:, 0, :, :], inverted[:, 1, :, :]
+        nc.gpsimd.tensor_scalar(twice_positive[:], gain_tile[:], 0.0, 2.0, ALU.is_ge, ALU.mult)
         nc.gpsimd.tensor_scalar(sign[:], twice_positive[:], 1.0, -1.0, ALU.mult, ALU.add)
-        nc.gpsimd.tensor_tensor(size[:], gains, sign[:], ALU.mult)
+        nc.gpsimd.tensor_tensor(size[:], gain_tile[:], sign[:], ALU.mult)
         nc.gpsimd.tensor_scalar(floored, size[:], SMALLEST, None, ALU.max)
-        nc.scalar.activation(to_invert[:, 1, :], floored, ACT.Abs_reciprocal_sqrt)
+        nc.scalar.activation(to_invert[:, 1, :, :], floored, ACT.Abs_reciprocal_sqrt)
+        nc.gpsimd.tensor_scalar(sign11[:], twice_positive[:, 1, 1:2], 1.0, -1.0, ALU.mult, ALU.add)
         nc.vector.reciprocal(inverted[:], to_invert[:])
         nc.gpsimd.tensor_tensor(root_squared[:], root, root, ALU.mult)
         nc.gpsimd.tensor_tensor(fix[:], root_squared[:], inverse, ALU.mult)
+        nc.gpsimd.tensor_tensor(fix13[:], root_squared[:, 1, 3:4], inverse[:, 1, 3:4], ALU.mult)
 
         w1_rounded = {}
         w1_words = {}
         w1_scales = {}
         for b in range(2):
             for a in range(2):
-                w1_words[b, a] = keep.tile([P, PASS], U32, name=f"w1_words{b}{a}", align_bytes=64)
-                w1_scales[b, a] = keep.tile([P, PASS], U8, name=f"w1_scales{b}{a}", align_bytes=64)
+                w1_words[b, a] = sbuf(f"w1_words{b}{a}", [P, PASS], U32)
+                w1_scales[b, a] = sbuf(f"w1_scales{b}{a}", [P, PASS], U8)
 
         def copy_on_gpsimd(dst, src):
             nc.gpsimd.tensor_scalar(dst, src, 1.0, 0.0, ALU.mult, ALU.add)
@@ -125,9 +132,7 @@ def tile_list_robust_station_increments_kernel(
         def round_w1(b, a, half, copy, first=0, end=HALF // PACK):
             if (b, a) not in w1_rounded:
                 area = (a + b + 1) % 2
-                w1_rounded[b, a] = stage.tile(
-                    [P, PACK * PASS], BF16, name=f"w1_rounded{b}{a}", align_bytes=64, offset=STAGE_BYTES * area
-                )
+                w1_rounded[b, a] = sbuf(f"w1_rounded{b}{a}", [P, PACK * PASS], BF16, ROUNDED + 4 * KIB * area)
             by_column = w1_rounded[b, a][:].rearrange("p (t m j) -> p m t j", t=PACK, j=PACK)
             base = HALF // PACK * half
             copy(
@@ -146,9 +151,12 @@ def tile_list_robust_station_increments_kernel(
         h = {}
         h_acc = {}
 
+        def h_width(b, t):
+            return BANK // 2 if (b, t) == (0, 0) else BANK
+
         def h_pass(b, t, a):
             slot_cols = slice(P * t, P * (t + 1))
-            width = BANK // 2 if (b, t) == (0, 0) else BANK
+            width = h_width(b, t)
             for bank in range(S // width):
                 cols = slice(width * bank, width * (bank + 1))
                 if a == 0:
@@ -164,12 +172,9 @@ def tile_list_robust_station_increments_kernel(
                 )
 
         def fetch_h(b, t):
-            if (b, t) == (1, PACK - 1):
-                h[b, t] = stage.tile([P, S], F32, name=f"h{b}{t}", align_bytes=64, offset=2 * STAGE_BYTES)
-            else:
-                h[b, t] = keep.tile([P, S], F32, name=f"h{b}{t}")
-            row_sign = sign[:, PACK * b + t : PACK * b + t + 1]
-            width = BANK // 2 if (b, t) == (0, 0) else BANK
+            h[b, t] = sbuf(f"h{b}{t}", [P, S], F32, LAST_H if (b, t) == (1, PACK - 1) else None)
+            row_sign = sign11[:] if (b, t) == (1, 1) else sign[:, b, t : t + 1]
+            width = h_width(b, t)
             for bank in range(S // width):
                 cols = slice(width * bank, width * (bank + 1))
                 if (b, t) == (0, 0) and bank % 2 == 1:
@@ -177,72 +182,46 @@ def tile_list_robust_station_increments_kernel(
                 else:
                     nc.scalar.activation(h[b, t][:, cols], h_acc[b, t, bank][:], ACT.Copy, scale=row_sign)
 
-        def make_h(b, t):
-            h_pass(b, t, 0)
-            h_pass(b, t, 1)
-            fetch_h(b, t)
-
-        departure = {}
-        weight = {}
-
+        departure = [sbuf(f"departure{b}", [P, PACK, PAIRS], F32, (RAW10, SIGN11)[b]) for b in range(2)]
+        weight = [sbuf(f"weight{b}", [P, PACK, PAIRS], F32) for b in range(2)]
         picked = {}
 
         def pick(b, t):
-            if (b, t) == (0, PACK - 1):
-                picked[b, t] = stage.tile([P, PAIRS], F32, name="picked03", align_bytes=64, offset=RAW11)
-            else:
-                picked[b, t] = keep.tile([P, PAIRS], F32, name=f"picked{b}{t}")
+            picked[b, t] = sbuf(f"picked{b}{t}", [P, PAIRS], F32, RAW11 if (b, t) == (0, PACK - 1) else None)
             nc.vector.tensor_copy(out=picked[b, t][:], in_=h[b, t][:].indirect(p2_list[:]))
 
-        def depart(b, t):
-            if (b, t) == (0, 0):
-                departure[b] = stage.tile(
-                    [P, PACK, PAIRS], F32, name="departure0", align_bytes=64, offset=LAST_RAW + STAGE_BYTES
-                )
-            elif t == 0:
-                departure[b] = stage.tile([P, PACK, PAIRS], F32, name="departure1", align_bytes=64, offset=LATE)
-            if t == 0:
-                weight[b] = keep.tile([P, PACK, PAIRS], F32, name=f"weight{b}")
-            d = departure[b][:, t, :]
-            nc.vector.tensor_tensor(d, h[b, t][:].indirect(p1_list[:]), picked[b, t][:], ALU.subtract)
+        def depart(b, t, first=0, end=PAIRS):
+            stations = h[b, t][:].indirect(p1_list[:, first // 16 : end // 16])
+            nc.vector.tensor_tensor(departure[b][:, t, first:end], stations, picked[b, t][:, first:end], ALU.subtract)
 
-        def weigh(b, t, squared):
-            shrink = keep.tile([P, PAIRS], F32, name=f"shrink{b}{t}")
-            col = slice(PACK * b + t, PACK * b + t + 1)
-            nc.scalar.activation(shrink[:], squared, ACT.Abs_reciprocal_sqrt, bias=fix[:, col], scale=fix[:, col])
-            nc.scalar.activation(weight[b][:, t, :], shrink[:], ACT.Square, scale=root[:, col])
+        def weigh(b, t, squared, first=0, end=PAIRS):
+            shrink = sbuf(f"shrink{b}{t}_{first}", [P, end - first], F32)
+            row_fix = fix13[:] if (b, t) == (1, PACK - 1) else fix[:, b, t : t + 1]
+            nc.scalar.activation(shrink[:], squared, ACT.Abs_reciprocal_sqrt, bias=row_fix, scale=row_fix)
+            nc.scalar.activation(weight[b][:, t, first:end], shrink[:], ACT.Square, scale=root[:, b, t : t + 1])
 
-        def influence(b, t):
-            depart(b, t)
-            if b == 0:
-                offset = RAW11 + STAGE_BYTES // 2 * (t + 1)
-                squared = stage.tile([P, PAIRS], F32, name=f"squared{b}{t}", align_bytes=64, offset=offset)
-            else:
-                squared = keep.tile([P, PAIRS], F32, name=f"squared{b}{t}")
-            nc.scalar.activation(squared[:], departure[b][:, t, :], ACT.Square)
-            weigh(b, t, squared[:])
+        def influence(b, t, first=0, end=PAIRS):
+            depart(b, t, first, end)
+            offset = RAW11 + 2 * KIB * (t + 1) if b == 0 else None
+            squared = sbuf(f"squared{b}{t}_{first}", [P, end - first], F32, offset)
+            nc.scalar.activation(squared[:], departure[b][:, t, first:end], ACT.Square)
+            weigh(b, t, squared[:], first, end)
 
         z_words = {}
         z_scales = {}
 
-        def make_z(b, first, end):
-            width = end - first
-            cols = slice(first, end)
-            if b == 0:
-                offset = 2 * STAGE_BYTES + 2 * PACK * first
-                rounded = stage.tile([P, PACK * width], BF16, name=f"z_rounded0_{first}", align_bytes=64, offset=offset)
-            else:
-                rounded = keep.tile([P, PACK * width], BF16, name=f"z_rounded{b}_{first}", align_bytes=64)
-            words = keep.tile([P, width], U32, name=f"z_words{b}_{first}", align_bytes=64)
-            scales = keep.tile([P, width], U8, name=f"z_scales{b}_{first}", align_bytes=64)
+        def make_z(b, first, end, offset=None):
+            rounded = sbuf(f"z_rounded{b}_{first}", [P, PACK * (end - first)], BF16, offset)
+            words = sbuf(f"z_words{b}_{first}", [P, end - first], U32)
+            scales = sbuf(f"z_scales{b}_{first}", [P, end - first], U8)
             nc.vector.tensor_tensor(
                 rounded[:].rearrange("p (c i t) -> p c t i", i=4, t=PACK),
-                departure[b][:, :, cols].rearrange("p t (c i) -> p c t i", i=4),
-                weight[b][:, :, cols].rearrange("p t (c i) -> p c t i", i=4),
+                departure[b][:, :, first:end].rearrange("p t (c i) -> p c t i", i=4),
+                weight[b][:, :, first:end].rearrange("p t (c i) -> p c t i", i=4),
                 ALU.mult,
             )
             nc.vector.quantize_mx(out=words[:].bitcast(FP8X4), scales=scales[:], in_=rounded[:])
-            for start in range(0, width, CHUNK):
+            for start in range(0, end - first, CHUNK):
                 z_words[b, (first + start) // CHUNK] = words[:, start : start + CHUNK]
                 z_scales[b, (first + start) // CHUNK] = scales[:, start : start + CHUNK]
 
@@ -268,7 +247,7 @@ def tile_list_robust_station_increments_kernel(
 
         def finish(chunk, first_tile, end_tile, copy):
             out_passes(1, chunk, first_tile, end_tile)
-            result = keep.tile([P, end_tile - first_tile, CHUNK], F32, name=f"result{chunk}{first_tile}")
+            result = sbuf(f"result{chunk}{first_tile}", [P, end_tile - first_tile, CHUNK], F32)
             copy(out=result[:], in_=out_acc[chunk, first_tile][:])
             cols = slice(CHUNK * chunk, CHUNK * (chunk + 1))
             nc.sync.dma_start(out=out_by_tile[:, first_tile:end_tile, cols], in_=result[:])
@@ -294,12 +273,14 @@ def tile_list_robust_station_increments_kernel(
         quantise_w1(0, 1, 2, PACK)
         h_pass(0, 1, 1)
         fetch_h(0, 1)
-        make_h(0, 2)
-        make_h(0, 3)
-        round_w1(1, 0, 0, copy_on_gpsimd)
-        round_w1(1, 0, 1, copy_on_gpsimd)
-        round_w1(1, 1, 0, nc.scalar.copy)
-        round_w1(1, 1, 1, nc.scalar.copy)
+        for t in range(2, PACK):
+            h_pass(0, t, 0)
+            h_pass(0, t, 1)
+            fetch_h(0, t)
+        for half in range(2):
+            round_w1(1, 0, half, copy_on_gpsimd)
+        for half in range(2):
+            round_w1(1, 1, half, nc.scalar.copy)
         pick(0, 0)
         pick(0, 1)
         influence(0, 0)
@@ -311,28 +292,36 @@ def tile_list_robust_station_increments_kernel(
         quantise_w1(1, 1, 0, PACK)
         for t in range(PACK):
             h_pass(1, t, 1)
-            fetch_h(1, t)
+        fetch_h(1, 0)
+        fetch_h(1, 1)
         pick(0, 3)
         depart(0, 2)
         depart(0, 3)
-        last_squares = stage.tile([P, 2, PAIRS], F32, name="last_squares", align_bytes=64, offset=LATE)
+        last_squares = sbuf("last_squares", [P, 2, PAIRS], F32)
         nc.gpsimd.tensor_tensor(last_squares[:], departure[0][:, 2:, :], departure[0][:, 2:, :], ALU.mult)
-        weigh(0, 2, last_squares[:, 0, :])
-        weigh(0, 3, last_squares[:, 1, :])
-        for t in range(PACK):
-            pick(1, t)
-        for t in range(PACK):
-            influence(1, t)
+        fetch_h(1, 2)
+        for t in range(2, PACK):
+            weigh(0, t, last_squares[:, t - 2, :])
+        fetch_h(1, 3)
+        pick(1, 0)
+        pick(1, 1)
+        influence(1, 0)
+        pick(1, 2)
+        influence(1, 1)
+        pick(1, 3)
+        influence(1, 2)
+        for first in range(0, PAIRS, RANGE):
+            influence(1, 3, first, first + RANGE)
 
         banks = [(chunk, 0, out_tiles) for chunk in range(CHUNKS - 1)]
         banks.extend([(CHUNKS - 1, 0, out_tiles // 2), (CHUNKS - 1, out_tiles // 2, out_tiles)])
-        for first in range(0, PAIRS, 2 * CHUNK):
-            make_z(0, first, first + 2 * CHUNK)
+        for base in range(0, PAIRS, RANGE):
+            make_z(0, base, base + RANGE, FIX13 if base else LAST_H)
             for bank in banks:
-                if first <= CHUNK * bank[0] < first + 2 * CHUNK:
+                if base <= CHUNK * bank[0] < base + RANGE:
                     out_passes(0, *bank)
-        for first in range(0, PAIRS, CHUNK):
-            make_z(1, first, first + CHUNK)
-            for bank in banks:
-                if first == CHUNK * bank[0]:
-                    finish(*bank, nc.vector.tensor_copy if bank == banks[-2] else nc.scalar.copy)
+            for first in range(base, base + RANGE, CHUNK):
+                make_z(1, first, first + CHUNK)
+                for bank in banks:
+                    if first == CHUNK * bank[0]:
+                        finish(*bank, nc.vector.tensor_copy if bank == banks[-2] else nc.scalar.copy)

@@ -25,15 +25,15 @@ CHUNK = 128
 CHUNKS = PAIRS // CHUNK
 RANGE = PAIRS // 2
 SMALLEST = 2.0**-126
-SCALAR_SHARE = 38
+SCALAR_SHARE = 32
 
 KIB = 1024
 ROUNDED = 0
-RAW10 = 8 * KIB
-RAW11 = 16 * KIB
-SIGN11 = 24 * KIB
+RAW110 = 8 * KIB
+RAW111 = 20 * KIB
+SIGN11 = 40 * KIB
 LAST_H = 32 * KIB
-FIX13 = 36 * KIB
+ROOT13 = 36 * KIB
 
 
 def tile_list_robust_station_increments_kernel(
@@ -90,8 +90,10 @@ def tile_list_robust_station_increments_kernel(
         load_w1(0, 1, HALF, HALF)
         nc.sync.dma_start(p2_list[:], pos2)
         nc.sync.dma_start(p1_list[:], pos1)
-        load_w1(1, 0, 0, PASS, RAW10)
-        load_w1(1, 1, 0, PASS, RAW11)
+        load_w1(1, 0, 0, HALF)
+        load_w1(1, 0, HALF, HALF)
+        load_w1(1, 1, 0, HALF, RAW110)
+        load_w1(1, 1, HALF, HALF, RAW111)
         nc.sync.dma_start(out=w4_word_tile[:], in_=w4_words.bitcast(I32).rearrange("b p c -> p b c"))
         for quad in range(4):
             nc.sync.dma_start(
@@ -103,7 +105,7 @@ def tile_list_robust_station_increments_kernel(
             sbuf(f"gain_{name}", [P, 2, PACK], F32) for name in ("twice", "sign", "size", "root_squared", "fix")
         )
         sign11 = sbuf("sign11", [P, 1], F32, SIGN11)
-        fix13 = sbuf("fix13", [P, 1], F32, FIX13)
+        root13 = sbuf("root13", [P, 1], F32, ROOT13)
         to_invert = sbuf("gain_to_invert", [P, 2, 2, PACK], F32)
         inverted = sbuf("gain_inverted", [P, 2, 2, PACK], F32)
         floored, inverse, root = to_invert[:, 0, :, :], inverted[:, 0, :, :], inverted[:, 1, :, :]
@@ -116,14 +118,14 @@ def tile_list_robust_station_increments_kernel(
         nc.vector.reciprocal(inverted[:], to_invert[:])
         nc.gpsimd.tensor_tensor(root_squared[:], root, root, ALU.mult)
         nc.gpsimd.tensor_tensor(fix[:], root_squared[:], inverse, ALU.mult)
-        nc.gpsimd.tensor_tensor(fix13[:], root_squared[:, 1, 3:4], inverse[:, 1, 3:4], ALU.mult)
+        nc.gpsimd.tensor_copy(out=root13[:], in_=root[:, 1, 3:4])
 
         w1_rounded = {}
         w1_words = {}
         w1_scales = {}
         for b in range(2):
             for a in range(2):
-                w1_words[b, a] = sbuf(f"w1_words{b}{a}", [P, PASS], U32)
+                w1_words[b, a] = sbuf(f"w1_words{b}{a}", [P, PASS], U32, RAW110 if (b, a) == (1, 0) else None)
                 w1_scales[b, a] = sbuf(f"w1_scales{b}{a}", [P, PASS], U8)
 
         def copy_on_gpsimd(dst, src):
@@ -182,12 +184,12 @@ def tile_list_robust_station_increments_kernel(
                 else:
                     nc.scalar.activation(h[b, t][:, cols], h_acc[b, t, bank][:], ACT.Copy, scale=row_sign)
 
-        departure = [sbuf(f"departure{b}", [P, PACK, PAIRS], F32, (RAW10, SIGN11)[b]) for b in range(2)]
+        departure = [sbuf(f"departure{b}", [P, PACK, PAIRS], F32, (RAW110 + 2 * KIB, SIGN11)[b]) for b in range(2)]
         weight = [sbuf(f"weight{b}", [P, PACK, PAIRS], F32) for b in range(2)]
         picked = {}
 
         def pick(b, t):
-            picked[b, t] = sbuf(f"picked{b}{t}", [P, PAIRS], F32, RAW11 if (b, t) == (0, PACK - 1) else None)
+            picked[b, t] = sbuf(f"picked{b}{t}", [P, PAIRS], F32, RAW111 - KIB if (b, t) == (0, PACK - 1) else None)
             nc.vector.tensor_copy(out=picked[b, t][:], in_=h[b, t][:].indirect(p2_list[:]))
 
         def depart(b, t, first=0, end=PAIRS):
@@ -196,13 +198,14 @@ def tile_list_robust_station_increments_kernel(
 
         def weigh(b, t, squared, first=0, end=PAIRS):
             shrink = sbuf(f"shrink{b}{t}_{first}", [P, end - first], F32)
-            row_fix = fix13[:] if (b, t) == (1, PACK - 1) else fix[:, b, t : t + 1]
+            row_fix = fix[:, b, t : t + 1]
+            row_root = root13[:] if (b, t) == (1, PACK - 1) else root[:, b, t : t + 1]
             nc.scalar.activation(shrink[:], squared, ACT.Abs_reciprocal_sqrt, bias=row_fix, scale=row_fix)
-            nc.scalar.activation(weight[b][:, t, first:end], shrink[:], ACT.Square, scale=root[:, b, t : t + 1])
+            nc.scalar.activation(weight[b][:, t, first:end], shrink[:], ACT.Square, scale=row_root)
 
         def influence(b, t, first=0, end=PAIRS):
             depart(b, t, first, end)
-            offset = RAW11 + 2 * KIB * (t + 1) if b == 0 else None
+            offset = RAW111 + KIB + 2 * KIB * t if b == 0 else None
             squared = sbuf(f"squared{b}{t}_{first}", [P, end - first], F32, offset)
             nc.scalar.activation(squared[:], departure[b][:, t, first:end], ACT.Square)
             weigh(b, t, squared[:], first, end)
@@ -279,15 +282,14 @@ def tile_list_robust_station_increments_kernel(
             fetch_h(0, t)
         for half in range(2):
             round_w1(1, 0, half, copy_on_gpsimd)
-        for half in range(2):
-            round_w1(1, 1, half, nc.scalar.copy)
-        pick(0, 0)
-        pick(0, 1)
+        round_w1(1, 1, 0, copy_on_gpsimd)
+        round_w1(1, 1, 1, nc.scalar.copy)
+        for t in range(PACK - 1):
+            pick(0, t)
         influence(0, 0)
         quantise_w1(1, 0, 0, PACK)
         for t in range(PACK):
             h_pass(1, t, 0)
-        pick(0, 2)
         influence(0, 1)
         quantise_w1(1, 1, 0, PACK)
         for t in range(PACK):
@@ -316,7 +318,7 @@ def tile_list_robust_station_increments_kernel(
         banks = [(chunk, 0, out_tiles) for chunk in range(CHUNKS - 1)]
         banks.extend([(CHUNKS - 1, 0, out_tiles // 2), (CHUNKS - 1, out_tiles // 2, out_tiles)])
         for base in range(0, PAIRS, RANGE):
-            make_z(0, base, base + RANGE, FIX13 if base else LAST_H)
+            make_z(0, base, base + RANGE, ROOT13 if base else LAST_H)
             for bank in banks:
                 if base <= CHUNK * bank[0] < base + RANGE:
                     out_passes(0, *bank)

@@ -31,9 +31,8 @@ KIB = 1024
 ROUNDED = 0
 RAW110 = 8 * KIB
 RAW111 = 20 * KIB
-SIGN11 = 40 * KIB
 LAST_H = 32 * KIB
-ROOT13 = 36 * KIB
+LAST_ROOT = 36 * KIB
 
 
 def tile_list_robust_station_increments_kernel(
@@ -76,6 +75,7 @@ def tile_list_robust_station_increments_kernel(
         def load_table_words(a):
             nc.sync.dma_start(out=table_words[a][:], in_=tab_words[a].rearrange("p t i -> p (t i)").bitcast(I32))
 
+        nc.scalar.dma_start(out=gain_tile[:], in_=gain.rearrange("(b p t) -> p b t", b=2, t=PACK))
         nc.sync.dma_start(idx_list[:], offs)
         load_table_words(0)
         for quad in range(4):
@@ -83,7 +83,6 @@ def tile_list_robust_station_increments_kernel(
                 out=table_scales[32 * quad : 32 * quad + 8, :],
                 in_=tab_scales.bitcast(I32)[:, 4 * quad : 4 * quad + 4, :],
             )
-        nc.sync.dma_start(out=gain_tile[:], in_=gain.rearrange("(b p t) -> p b t", b=2, t=PACK))
         load_w1(0, 0, 0, PASS)
         load_table_words(1)
         load_w1(0, 1, 0, HALF)
@@ -101,24 +100,28 @@ def tile_list_robust_station_increments_kernel(
                 in_=w4_scales.bitcast(I32)[:, 4 * quad : 4 * quad + 4, :].rearrange("b i c -> i b c"),
             )
 
+        departure = [sbuf(f"departure{b}", [P, PACK, PAIRS], F32, (RAW110 + 2 * KIB, None)[b]) for b in range(2)]
+
         twice_positive, sign, size, root_squared, fix = (
             sbuf(f"gain_{name}", [P, 2, PACK], F32) for name in ("twice", "sign", "size", "root_squared", "fix")
         )
-        sign11 = sbuf("sign11", [P, 1], F32, SIGN11)
-        root13 = sbuf("root13", [P, 1], F32, ROOT13)
+        last_root = [sbuf(f"last_root{r}", [P, 1], F32, LAST_ROOT + 2 * KIB * r) for r in range(2)]
         to_invert = sbuf("gain_to_invert", [P, 2, 2, PACK], F32)
         inverted = sbuf("gain_inverted", [P, 2, 2, PACK], F32)
         floored, inverse, root = to_invert[:, 0, :, :], inverted[:, 0, :, :], inverted[:, 1, :, :]
         nc.gpsimd.tensor_scalar(twice_positive[:], gain_tile[:], 0.0, 2.0, ALU.is_ge, ALU.mult)
         nc.gpsimd.tensor_scalar(sign[:], twice_positive[:], 1.0, -1.0, ALU.mult, ALU.add)
-        nc.gpsimd.tensor_tensor(size[:], gain_tile[:], sign[:], ALU.mult)
-        nc.gpsimd.tensor_scalar(floored, size[:], SMALLEST, None, ALU.max)
+        nc.vector.scalar_tensor_tensor(size[:], gain_tile[:], -1.0, gain_tile[:], ALU.mult, ALU.max)
+        nc.vector.tensor_scalar(floored, size[:], SMALLEST, None, ALU.max)
         nc.scalar.activation(to_invert[:, 1, :, :], floored, ACT.Abs_reciprocal_sqrt)
-        nc.gpsimd.tensor_scalar(sign11[:], twice_positive[:, 1, 1:2], 1.0, -1.0, ALU.mult, ALU.add)
+        for t in (1, 3):
+            column = departure[1][:, t - 1, 0:1]
+            nc.gpsimd.tensor_scalar(column, twice_positive[:, 1, t : t + 1], 1.0, -1.0, ALU.mult, ALU.add)
         nc.vector.reciprocal(inverted[:], to_invert[:])
         nc.gpsimd.tensor_tensor(root_squared[:], root, root, ALU.mult)
         nc.gpsimd.tensor_tensor(fix[:], root_squared[:], inverse, ALU.mult)
-        nc.gpsimd.tensor_copy(out=root13[:], in_=root[:, 1, 3:4])
+        for column in last_root:
+            nc.gpsimd.tensor_copy(out=column[:], in_=root[:, 1, 3:4])
 
         w1_rounded = {}
         w1_words = {}
@@ -175,7 +178,7 @@ def tile_list_robust_station_increments_kernel(
 
         def fetch_h(b, t):
             h[b, t] = sbuf(f"h{b}{t}", [P, S], F32, LAST_H if (b, t) == (1, PACK - 1) else None)
-            row_sign = sign11[:] if (b, t) == (1, 1) else sign[:, b, t : t + 1]
+            row_sign = departure[1][:, t - 1, 0:1] if b == 1 and t % 2 else sign[:, b, t : t + 1]
             width = h_width(b, t)
             for bank in range(S // width):
                 cols = slice(width * bank, width * (bank + 1))
@@ -184,7 +187,6 @@ def tile_list_robust_station_increments_kernel(
                 else:
                     nc.scalar.activation(h[b, t][:, cols], h_acc[b, t, bank][:], ACT.Copy, scale=row_sign)
 
-        departure = [sbuf(f"departure{b}", [P, PACK, PAIRS], F32, (RAW110 + 2 * KIB, SIGN11)[b]) for b in range(2)]
         weight = [sbuf(f"weight{b}", [P, PACK, PAIRS], F32) for b in range(2)]
         picked = {}
 
@@ -199,7 +201,7 @@ def tile_list_robust_station_increments_kernel(
         def weigh(b, t, squared, first=0, end=PAIRS):
             shrink = sbuf(f"shrink{b}{t}_{first}", [P, end - first], F32)
             row_fix = fix[:, b, t : t + 1]
-            row_root = root13[:] if (b, t) == (1, PACK - 1) else root[:, b, t : t + 1]
+            row_root = last_root[first // RANGE][:] if (b, t) == (1, PACK - 1) else root[:, b, t : t + 1]
             nc.scalar.activation(shrink[:], squared, ACT.Abs_reciprocal_sqrt, bias=row_fix, scale=row_fix)
             nc.scalar.activation(weight[b][:, t, first:end], shrink[:], ACT.Square, scale=row_root)
 
@@ -308,21 +310,21 @@ def tile_list_robust_station_increments_kernel(
         pick(1, 0)
         pick(1, 1)
         influence(1, 0)
-        pick(1, 2)
         influence(1, 1)
+        pick(1, 2)
         pick(1, 3)
-        influence(1, 2)
         for first in range(0, PAIRS, RANGE):
-            influence(1, 3, first, first + RANGE)
+            for t in range(2, PACK):
+                influence(1, t, first, first + RANGE)
 
         banks = [(chunk, 0, out_tiles) for chunk in range(CHUNKS - 1)]
         banks.extend([(CHUNKS - 1, 0, out_tiles // 2), (CHUNKS - 1, out_tiles // 2, out_tiles)])
-        for base in range(0, PAIRS, RANGE):
-            make_z(0, base, base + RANGE, ROOT13 if base else LAST_H)
+        for base, end, offset in ((0, RANGE, LAST_H), (RANGE, RANGE + CHUNK, LAST_ROOT), (RANGE + CHUNK, PAIRS, LAST_ROOT + 2 * KIB)):
+            make_z(0, base, end, offset)
             for bank in banks:
-                if base <= CHUNK * bank[0] < base + RANGE:
+                if base <= CHUNK * bank[0] < end:
                     out_passes(0, *bank)
-            for first in range(base, base + RANGE, CHUNK):
+            for first in range(base, end, CHUNK):
                 make_z(1, first, first + CHUNK)
                 for bank in banks:
                     if first == CHUNK * bank[0]:

@@ -76,18 +76,20 @@ def tile_list_robust_station_increments_kernel(
             nc.sync.dma_start(out=table_words[a][:], in_=tab_words[a].rearrange("p t i -> p (t i)").bitcast(I32))
 
         nc.scalar.dma_start(out=gain_tile[:], in_=gain.rearrange("(b p t) -> p b t", b=2, t=PACK))
+        def load_table_scales(first, end):
+            for r in range(first, end):
+                for a in range(2):
+                    nc.sync.dma_start(out=table_scales[4 * a + r : P : 32, :], in_=tab_scales.bitcast(I32)[a, r:16:4, :])
+
         nc.sync.dma_start(idx_list[:], offs)
+        nc.sync.dma_start(p2_list[:], pos2)
+        load_table_scales(0, 1)
         load_table_words(0)
-        for quad in range(4):
-            nc.sync.dma_start(
-                out=table_scales[32 * quad : 32 * quad + 8, :],
-                in_=tab_scales.bitcast(I32)[:, 4 * quad : 4 * quad + 4, :],
-            )
+        load_table_scales(1, 4)
         load_w1(0, 0, 0, PASS)
         load_table_words(1)
         load_w1(0, 1, 0, HALF)
         load_w1(0, 1, HALF, HALF)
-        nc.sync.dma_start(p2_list[:], pos2)
         nc.sync.dma_start(p1_list[:], pos1)
         load_w1(1, 0, 0, HALF)
         load_w1(1, 0, HALF, HALF)

@@ -25,12 +25,11 @@ CHUNK = 128
 CHUNKS = PAIRS // CHUNK
 RANGE = PAIRS // 2
 SMALLEST = 2.0**-126
-SCALAR_SHARE = 32
+SCALAR_SHARE = 22
 
 KIB = 1024
 ROUNDED = 0
-RAW110 = 8 * KIB
-RAW111 = 20 * KIB
+RAW11 = 20 * KIB
 LAST_H = 32 * KIB
 LAST_ROOT = 36 * KIB
 
@@ -55,18 +54,26 @@ def tile_list_robust_station_increments_kernel(
         table_words = [sbuf(f"table_words{a}", [P, T], I32) for a in range(2)]
         table_scales = sbuf("table_scales", [P, T // 4], I32)
         v_words = [sbuf(f"v_words{a}", [P, S], U32) for a in range(2)]
-        v_scales = sbuf("v_scales", [P, S], U8)
+        picked_scales = sbuf("picked_scales", [P, S], U8)
+        carried_scales = sbuf("carried_scales", [P, S // 4], I32)
+        v_scales = (picked_scales[:], carried_scales[:].bitcast(U8))
         w4_word_tile = sbuf("w4_word_tile", [P, 2, 2 * N // 4], I32)
         w4_scale_tile = sbuf("w4_scale_tile", [P, 2, N // 4], I32)
         gain_tile = sbuf("gain_tile", [P, 2, PACK], F32)
 
         nc.vector.memset(table_scales[:], 0)
+        nc.vector.memset(carried_scales[:], 0)
         nc.vector.memset(w4_scale_tile[:], 0)
 
         w1_raw = {}
+        departure = [sbuf(f"departure{b}", [P, PACK, PAIRS], F32) for b in range(2)]
+        picked = {(1, 2): sbuf("picked12", [P, PAIRS], F32)}
 
         def load_w1(b, a, first, width, offset=None):
-            raw = sbuf(f"w1_raw{b}{a}{first}", [P, PACK, width], F32, offset)
+            if (b, a, first) == (1, 0, HALF):
+                raw = departure[0][:, :2, :].rearrange("p t (j c) -> p (t j) c", c=HALF)
+            else:
+                raw = sbuf(f"w1_raw{b}{a}{first}", [P, PACK, width], F32, offset)
             rows = w1[PASS * a : PASS * (a + 1), PASS * b + first : PASS * b + first + width]
             nc.sync.dma_start(out=raw[:], in_=rows.rearrange("(p j) c -> p j c", j=PACK))
             for start in range(0, width, HALF):
@@ -76,16 +83,12 @@ def tile_list_robust_station_increments_kernel(
             nc.sync.dma_start(out=table_words[a][:], in_=tab_words[a].rearrange("p t i -> p (t i)").bitcast(I32))
 
         nc.scalar.dma_start(out=gain_tile[:], in_=gain.rearrange("(b p t) -> p b t", b=2, t=PACK))
-        def load_table_scales(first, end):
-            for r in range(first, end):
-                for a in range(2):
-                    nc.sync.dma_start(out=table_scales[4 * a + r : P : 32, :], in_=tab_scales.bitcast(I32)[a, r:16:4, :])
-
         nc.sync.dma_start(idx_list[:], offs)
         nc.sync.dma_start(p2_list[:], pos2)
-        load_table_scales(0, 1)
+        scale_rows = tab_scales.bitcast(I32).rearrange("a (q r) c -> r q a c", r=4)
+        for r in range(4):
+            nc.sync.dma_start(out=table_scales[r:P:16, :], in_=scale_rows[r])
         load_table_words(0)
-        load_table_scales(1, 4)
         load_w1(0, 0, 0, PASS)
         load_table_words(1)
         load_w1(0, 1, 0, HALF)
@@ -93,8 +96,7 @@ def tile_list_robust_station_increments_kernel(
         nc.sync.dma_start(p1_list[:], pos1)
         load_w1(1, 0, 0, HALF)
         load_w1(1, 0, HALF, HALF)
-        load_w1(1, 1, 0, HALF, RAW110)
-        load_w1(1, 1, HALF, HALF, RAW111)
+        load_w1(1, 1, 0, PASS, RAW11)
         nc.sync.dma_start(out=w4_word_tile[:], in_=w4_words.bitcast(I32).rearrange("b p c -> p b c"))
         for quad in range(4):
             nc.sync.dma_start(
@@ -102,36 +104,36 @@ def tile_list_robust_station_increments_kernel(
                 in_=w4_scales.bitcast(I32)[:, 4 * quad : 4 * quad + 4, :].rearrange("b i c -> i b c"),
             )
 
-        departure = [sbuf(f"departure{b}", [P, PACK, PAIRS], F32, (RAW110 + 2 * KIB, None)[b]) for b in range(2)]
 
-        twice_positive, sign, size, root_squared, fix = (
-            sbuf(f"gain_{name}", [P, 2, PACK], F32) for name in ("twice", "sign", "size", "root_squared", "fix")
+        size, inverse_root, inverse, sign = (
+            sbuf(f"gain_{name}", [P, 2, PACK], F32) for name in ("size", "inverse_root", "inverse", "sign")
         )
-        last_root = [sbuf(f"last_root{r}", [P, 1], F32, LAST_ROOT + 2 * KIB * r) for r in range(2)]
-        to_invert = sbuf("gain_to_invert", [P, 2, 2, PACK], F32)
-        inverted = sbuf("gain_inverted", [P, 2, 2, PACK], F32)
-        floored, inverse, root = to_invert[:, 0, :, :], inverted[:, 0, :, :], inverted[:, 1, :, :]
-        nc.gpsimd.tensor_scalar(twice_positive[:], gain_tile[:], 0.0, 2.0, ALU.is_ge, ALU.mult)
-        nc.gpsimd.tensor_scalar(sign[:], twice_positive[:], 1.0, -1.0, ALU.mult, ALU.add)
+        last_inverse = [sbuf(f"last_inverse{r}", [P, 1], F32, LAST_ROOT + 2 * KIB * r) for r in range(2)]
         nc.vector.scalar_tensor_tensor(size[:], gain_tile[:], -1.0, gain_tile[:], ALU.mult, ALU.max)
-        nc.vector.tensor_scalar(floored, size[:], SMALLEST, None, ALU.max)
-        nc.scalar.activation(to_invert[:, 1, :, :], floored, ACT.Abs_reciprocal_sqrt)
-        for t in (1, 3):
-            column = departure[1][:, t - 1, 0:1]
-            nc.gpsimd.tensor_scalar(column, twice_positive[:, 1, t : t + 1], 1.0, -1.0, ALU.mult, ALU.add)
-        nc.vector.reciprocal(inverted[:], to_invert[:])
-        nc.gpsimd.tensor_tensor(root_squared[:], root, root, ALU.mult)
-        nc.gpsimd.tensor_tensor(fix[:], root_squared[:], inverse, ALU.mult)
-        for column in last_root:
-            nc.gpsimd.tensor_copy(out=column[:], in_=root[:, 1, 3:4])
+        nc.scalar.activation(inverse_root[:], size[:], ACT.Abs_reciprocal_sqrt, bias=SMALLEST)
+        nc.scalar.activation(inverse[:], inverse_root[:], ACT.Square)
+        for column in last_inverse:
+            nc.gpsimd.tensor_tensor(column[:], inverse_root[:, 1, 3:4], inverse_root[:, 1, 3:4], ALU.mult)
+        early_inverse = {(0, t): departure[0][:, 2 + t, 0:1] for t in range(2)}
+        for (b, t), column in early_inverse.items():
+            nc.scalar.activation(column, inverse_root[:, b, t : t + 1], ACT.Square)
+        late_sign = {1: departure[1][:, 0, 0:1], 3: picked[1, 2][:, 0:1]}
+        for t, column in late_sign.items():
+            nc.scalar.activation(column, gain_tile[:, 1, t : t + 1], ACT.Sign, scale=inverse_root[:, 1, t : t + 1])
+        for b, t in ((0, 0), (0, 1), (0, 2), (0, 3), (1, 0), (1, 2)):
+            column = sign[:, b, t : t + 1]
+            nc.scalar.activation(column, gain_tile[:, b, t : t + 1], ACT.Sign, scale=inverse_root[:, b, t : t + 1])
 
         w1_rounded = {}
         w1_words = {}
         w1_scales = {}
         for b in range(2):
             for a in range(2):
-                w1_words[b, a] = sbuf(f"w1_words{b}{a}", [P, PASS], U32, RAW110 if (b, a) == (1, 0) else None)
-                w1_scales[b, a] = sbuf(f"w1_scales{b}{a}", [P, PASS], U8)
+                for pair in range(2):
+                    late = RAW11 + 6 * KIB + KIB * a if (b, pair) == (1, 1) else None
+                    words = sbuf(f"w1_words{b}{a}{pair}", [P, HALF], U32, late)
+                    scales = sbuf(f"w1_scales{b}{a}{pair}", [P, HALF], U8)
+                    w1_words[b, a, pair], w1_scales[b, a, pair] = words, scales
 
         def copy_on_gpsimd(dst, src):
             nc.gpsimd.tensor_scalar(dst, src, 1.0, 0.0, ALU.mult, ALU.add)
@@ -148,10 +150,11 @@ def tile_list_robust_station_increments_kernel(
             )
 
         def quantise_w1(b, a, first_slot, end_slot):
-            cols = slice(P * first_slot, P * end_slot)
+            pair = first_slot // 2
+            cols = slice(P * (first_slot - 2 * pair), P * (end_slot - 2 * pair))
             nc.vector.quantize_mx(
-                out=w1_words[b, a][:, cols].bitcast(FP8X4),
-                scales=w1_scales[b, a][:, cols],
+                out=w1_words[b, a, pair][:, cols].bitcast(FP8X4),
+                scales=w1_scales[b, a, pair][:, cols],
                 in_=w1_rounded[b, a][:, PASS * first_slot : PASS * end_slot],
             )
 
@@ -162,7 +165,7 @@ def tile_list_robust_station_increments_kernel(
             return BANK // 2 if (b, t) == (0, 0) else BANK
 
         def h_pass(b, t, a):
-            slot_cols = slice(P * t, P * (t + 1))
+            slot_cols = slice(P * (t % 2), P * (t % 2 + 1))
             width = h_width(b, t)
             for bank in range(S // width):
                 cols = slice(width * bank, width * (bank + 1))
@@ -170,17 +173,17 @@ def tile_list_robust_station_increments_kernel(
                     h_acc[b, t, bank] = psum.tile([P, width], F32, name="acc")
                 nc.tensor.matmul_mx(
                     out=h_acc[b, t, bank][:],
-                    lhsT=w1_words[b, a][:, slot_cols].bitcast(FP8X4),
-                    lhsT_scale=w1_scales[b, a][:, slot_cols],
+                    lhsT=w1_words[b, a, t // 2][:, slot_cols].bitcast(FP8X4),
+                    lhsT_scale=w1_scales[b, a, t // 2][:, slot_cols],
                     rhs=v_words[a][:, cols].bitcast(FP8X4),
-                    rhs_scale=v_scales[4 * a :, cols],
+                    rhs_scale=v_scales[a][:, cols],
                     start=(a == 0),
                     stop=(a == 1),
                 )
 
         def fetch_h(b, t):
             h[b, t] = sbuf(f"h{b}{t}", [P, S], F32, LAST_H if (b, t) == (1, PACK - 1) else None)
-            row_sign = departure[1][:, t - 1, 0:1] if b == 1 and t % 2 else sign[:, b, t : t + 1]
+            row_sign = late_sign[t] if b == 1 and t % 2 else sign[:, b, t : t + 1]
             width = h_width(b, t)
             for bank in range(S // width):
                 cols = slice(width * bank, width * (bank + 1))
@@ -190,29 +193,38 @@ def tile_list_robust_station_increments_kernel(
                     nc.scalar.activation(h[b, t][:, cols], h_acc[b, t, bank][:], ACT.Copy, scale=row_sign)
 
         weight = [sbuf(f"weight{b}", [P, PACK, PAIRS], F32) for b in range(2)]
-        picked = {}
 
         def pick(b, t):
-            picked[b, t] = sbuf(f"picked{b}{t}", [P, PAIRS], F32, RAW111 - KIB if (b, t) == (0, PACK - 1) else None)
+            if (b, t) not in picked:
+                picked[b, t] = sbuf(f"picked{b}{t}", [P, PAIRS], F32, RAW11 if (b, t) == (0, PACK - 1) else None)
             nc.vector.tensor_copy(out=picked[b, t][:], in_=h[b, t][:].indirect(p2_list[:]))
 
         def depart(b, t, first=0, end=PAIRS):
             stations = h[b, t][:].indirect(p1_list[:, first // 16 : end // 16])
             nc.vector.tensor_tensor(departure[b][:, t, first:end], stations, picked[b, t][:, first:end], ALU.subtract)
 
-        def weigh(b, t, squared, first=0, end=PAIRS):
-            shrink = sbuf(f"shrink{b}{t}_{first}", [P, end - first], F32)
-            row_fix = fix[:, b, t : t + 1]
-            row_root = last_root[first // RANGE][:] if (b, t) == (1, PACK - 1) else root[:, b, t : t + 1]
-            nc.scalar.activation(shrink[:], squared, ACT.Abs_reciprocal_sqrt, bias=row_fix, scale=row_fix)
-            nc.scalar.activation(weight[b][:, t, first:end], shrink[:], ACT.Square, scale=row_root)
+        shrunk = {}
 
-        def influence(b, t, first=0, end=PAIRS):
+        def shrink_step(b, t, squared, first=0, end=PAIRS):
+            shrink = sbuf(f"shrink{b}{t}_{first}", [P, end - first], F32)
+            row = last_inverse[first // RANGE][:] if (b, t) == (1, PACK - 1) else inverse[:, b, t : t + 1]
+            row = early_inverse.get((b, t), row)
+            nc.scalar.activation(shrink[:], squared, ACT.Abs_reciprocal_sqrt, bias=row, scale=row)
+            shrunk[b, t] = shrink
+
+        def weight_step(b, t, first=0, end=PAIRS):
+            nc.scalar.activation(weight[b][:, t, first:end], shrunk[b, t][:], ACT.Square)
+
+        def weigh(b, t, squared, first=0, end=PAIRS):
+            shrink_step(b, t, squared, first, end)
+            weight_step(b, t, first, end)
+
+        def influence(b, t, first=0, end=PAIRS, then=weigh):
             depart(b, t, first, end)
-            offset = RAW111 + KIB + 2 * KIB * t if b == 0 else None
+            offset = RAW11 + 2 * KIB * (t + 1) if b == 0 else None
             squared = sbuf(f"squared{b}{t}_{first}", [P, end - first], F32, offset)
             nc.scalar.activation(squared[:], departure[b][:, t, first:end], ACT.Square)
-            weigh(b, t, squared[:], first, end)
+            then(b, t, squared[:], first, end)
 
         z_words = {}
         z_scales = {}
@@ -262,17 +274,21 @@ def tile_list_robust_station_increments_kernel(
         def gather_words(a):
             nc.vector.tensor_copy(out=v_words[a][:], in_=table_words[a][:].bitcast(U32).indirect(idx_list[:]))
 
+        nc.vector.tensor_copy(out=picked_scales[:], in_=table_scales[:].bitcast(U8).indirect(idx_list[:]))
+        for quad in range(4):
+            rows = picked_scales[32 * quad + 16 : 32 * quad + 20, :].bitcast(I32)
+            nc.scalar.dma_start(out=carried_scales[32 * quad : 32 * quad + 4, :], in_=rows)
         gather_words(0)
-        nc.vector.tensor_copy(out=v_scales[:], in_=table_scales[:].bitcast(U8).indirect(idx_list[:]))
         round_w1(0, 0, 0, nc.scalar.copy)
-        round_w1(0, 0, 1, copy_on_gpsimd)
-        quantise_w1(0, 0, 0, PACK)
+        round_w1(0, 0, 1, nc.vector.tensor_copy)
+        quantise_w1(0, 0, 0, 2)
+        quantise_w1(0, 0, 2, PACK)
         gather_words(1)
         for t in range(2):
             h_pass(0, t, 0)
-        for half in range(2):
-            round_w1(0, 1, half, nc.scalar.copy, 0, SCALAR_SHARE)
-            round_w1(0, 1, half, copy_on_gpsimd, SCALAR_SHARE, HALF // PACK)
+        round_w1(0, 1, 0, nc.scalar.copy)
+        round_w1(0, 1, 1, nc.scalar.copy, 0, SCALAR_SHARE)
+        round_w1(0, 1, 1, nc.vector.tensor_copy, SCALAR_SHARE, HALF // PACK)
         quantise_w1(0, 1, 0, 1)
         h_pass(0, 0, 1)
         fetch_h(0, 0)
@@ -286,29 +302,36 @@ def tile_list_robust_station_increments_kernel(
             fetch_h(0, t)
         for half in range(2):
             round_w1(1, 0, half, copy_on_gpsimd)
-        round_w1(1, 1, 0, copy_on_gpsimd)
+        round_w1(1, 1, 0, nc.scalar.copy)
         round_w1(1, 1, 1, nc.scalar.copy)
         for t in range(PACK - 1):
             pick(0, t)
-        influence(0, 0)
-        quantise_w1(1, 0, 0, PACK)
-        for t in range(PACK):
+        influence(0, 0, then=shrink_step)
+        quantise_w1(1, 0, 0, 2)
+        for t in range(2):
             h_pass(1, t, 0)
-        influence(0, 1)
-        quantise_w1(1, 1, 0, PACK)
-        for t in range(PACK):
+        influence(0, 1, then=shrink_step)
+        quantise_w1(1, 1, 0, 2)
+        for t in range(2):
             h_pass(1, t, 1)
         fetch_h(1, 0)
         fetch_h(1, 1)
+        weight_step(0, 0)
+        weight_step(0, 1)
         pick(0, 3)
+        for a in range(2):
+            quantise_w1(1, a, 2, PACK)
+        for t in range(2, PACK):
+            h_pass(1, t, 0)
+            h_pass(1, t, 1)
         depart(0, 2)
         depart(0, 3)
         last_squares = sbuf("last_squares", [P, 2, PAIRS], F32)
         nc.gpsimd.tensor_tensor(last_squares[:], departure[0][:, 2:, :], departure[0][:, 2:, :], ALU.mult)
         fetch_h(1, 2)
+        fetch_h(1, 3)
         for t in range(2, PACK):
             weigh(0, t, last_squares[:, t - 2, :])
-        fetch_h(1, 3)
         pick(1, 0)
         pick(1, 1)
         influence(1, 0)

@@ -108,12 +108,12 @@ def tile_list_robust_station_increments_kernel(
         size, inverse_root, inverse, sign = (
             sbuf(f"gain_{name}", [P, 2, PACK], F32) for name in ("size", "inverse_root", "inverse", "sign")
         )
-        last_inverse = [sbuf(f"last_inverse{r}", [P, 1], F32, LAST_ROOT + 2 * KIB * r) for r in range(2)]
+        last_step = sbuf("last_step", [P, RANGE + 1], F32, LAST_ROOT)
+        last_inverse = last_step[:, RANGE:]
         nc.vector.scalar_tensor_tensor(size[:], gain_tile[:], -1.0, gain_tile[:], ALU.mult, ALU.max)
         nc.scalar.activation(inverse_root[:], size[:], ACT.Abs_reciprocal_sqrt, bias=SMALLEST)
         nc.scalar.activation(inverse[:], inverse_root[:], ACT.Square)
-        for column in last_inverse:
-            nc.gpsimd.tensor_tensor(column[:], inverse_root[:, 1, 3:4], inverse_root[:, 1, 3:4], ALU.mult)
+        nc.gpsimd.tensor_tensor(last_inverse, inverse_root[:, 1, 3:4], inverse_root[:, 1, 3:4], ALU.mult)
         early_inverse = {(0, t): departure[0][:, 2 + t, 0:1] for t in range(2)}
         for (b, t), column in early_inverse.items():
             nc.scalar.activation(column, inverse_root[:, b, t : t + 1], ACT.Square)
@@ -182,7 +182,7 @@ def tile_list_robust_station_increments_kernel(
                 )
 
         def fetch_h(b, t):
-            h[b, t] = sbuf(f"h{b}{t}", [P, S], F32, LAST_H if (b, t) == (1, PACK - 1) else None)
+            h[b, t] = sbuf(f"h{b}{t}", [P, S], F32, {(1, 2): LAST_H + 20 * KIB, (1, 3): LAST_H}.get((b, t)))
             row_sign = late_sign[t] if b == 1 and t % 2 else sign[:, b, t : t + 1]
             width = h_width(b, t)
             for bank in range(S // width):
@@ -206,8 +206,9 @@ def tile_list_robust_station_increments_kernel(
         shrunk = {}
 
         def shrink_step(b, t, squared, first=0, end=PAIRS):
-            shrink = sbuf(f"shrink{b}{t}_{first}", [P, end - first], F32)
-            row = last_inverse[first // RANGE][:] if (b, t) == (1, PACK - 1) else inverse[:, b, t : t + 1]
+            last = (b, t, first) == (1, PACK - 1, RANGE)
+            shrink = last_step[:, :RANGE] if last else sbuf(f"shrink{b}{t}_{first}", [P, end - first], F32)
+            row = last_inverse if last else inverse[:, b, t : t + 1]
             row = early_inverse.get((b, t), row)
             nc.scalar.activation(shrink[:], squared, ACT.Abs_reciprocal_sqrt, bias=row, scale=row)
             shrunk[b, t] = shrink
@@ -219,27 +220,35 @@ def tile_list_robust_station_increments_kernel(
             shrink_step(b, t, squared, first, end)
             weight_step(b, t, first, end)
 
-        def influence(b, t, first=0, end=PAIRS, then=weigh):
+        def influence(b, t, first=0, end=PAIRS, then=weigh, on_gpsimd=False):
             depart(b, t, first, end)
             offset = RAW11 + 2 * KIB * (t + 1) if b == 0 else None
             squared = sbuf(f"squared{b}{t}_{first}", [P, end - first], F32, offset)
-            nc.scalar.activation(squared[:], departure[b][:, t, first:end], ACT.Square)
+            if on_gpsimd:
+                nc.gpsimd.tensor_tensor(squared[:], departure[b][:, t, :], departure[b][:, t, :], ALU.mult)
+            else:
+                nc.scalar.activation(squared[:], departure[b][:, t, first:end], ACT.Square)
             then(b, t, squared[:], first, end)
 
         z_words = {}
         z_scales = {}
 
-        def make_z(b, first, end, offset=None):
+        z_rounded = {}
+
+        def product(b, first, end, offset=None):
             rounded = sbuf(f"z_rounded{b}_{first}", [P, PACK * (end - first)], BF16, offset)
-            words = sbuf(f"z_words{b}_{first}", [P, end - first], U32)
-            scales = sbuf(f"z_scales{b}_{first}", [P, end - first], U8)
+            z_rounded[b, first] = rounded
             nc.vector.tensor_tensor(
                 rounded[:].rearrange("p (c i t) -> p c t i", i=4, t=PACK),
                 departure[b][:, :, first:end].rearrange("p t (c i) -> p c t i", i=4),
                 weight[b][:, :, first:end].rearrange("p t (c i) -> p c t i", i=4),
                 ALU.mult,
             )
-            nc.vector.quantize_mx(out=words[:].bitcast(FP8X4), scales=scales[:], in_=rounded[:])
+
+        def quantise_z(b, first, end):
+            words = sbuf(f"z_words{b}_{first}", [P, end - first], U32)
+            scales = sbuf(f"z_scales{b}_{first}", [P, end - first], U8)
+            nc.vector.quantize_mx(out=words[:].bitcast(FP8X4), scales=scales[:], in_=z_rounded[b, first][:])
             for start in range(0, end - first, CHUNK):
                 z_words[b, (first + start) // CHUNK] = words[:, start : start + CHUNK]
                 z_scales[b, (first + start) // CHUNK] = scales[:, start : start + CHUNK]
@@ -327,15 +336,18 @@ def tile_list_robust_station_increments_kernel(
         depart(0, 2)
         depart(0, 3)
         last_squares = sbuf("last_squares", [P, 2, PAIRS], F32)
-        nc.gpsimd.tensor_tensor(last_squares[:], departure[0][:, 2:, :], departure[0][:, 2:, :], ALU.mult)
+        flat_squares = last_squares[:].rearrange("p t c -> p (t c)")
+        flat_departure = departure[0][:, 2:, :].rearrange("p t c -> p (t c)")
+        nc.gpsimd.tensor_tensor(flat_squares[:, RANGE:], flat_departure[:, RANGE:], flat_departure[:, RANGE:], ALU.mult)
         fetch_h(1, 2)
+        nc.scalar.activation(flat_squares[:, :RANGE], flat_departure[:, :RANGE], ACT.Square)
         fetch_h(1, 3)
         for t in range(2, PACK):
             weigh(0, t, last_squares[:, t - 2, :])
         pick(1, 0)
         pick(1, 1)
         influence(1, 0)
-        influence(1, 1)
+        influence(1, 1, on_gpsimd=True)
         pick(1, 2)
         pick(1, 3)
         for first in range(0, PAIRS, RANGE):
@@ -344,13 +356,31 @@ def tile_list_robust_station_increments_kernel(
 
         banks = [(chunk, 0, out_tiles) for chunk in range(CHUNKS - 1)]
         banks.extend([(CHUNKS - 1, 0, out_tiles // 2), (CHUNKS - 1, out_tiles // 2, out_tiles)])
-        for base, end, offset in ((0, RANGE, LAST_H), (RANGE, RANGE + CHUNK, LAST_ROOT), (RANGE + CHUNK, PAIRS, LAST_ROOT + 2 * KIB)):
-            make_z(0, base, end, offset)
+
+        def open_sums(first, end):
+            quantise_z(0, first, end)
             for bank in banks:
-                if base <= CHUNK * bank[0] < end:
+                if first <= CHUNK * bank[0] < end:
                     out_passes(0, *bank)
-            for first in range(base, end, CHUNK):
-                make_z(1, first, first + CHUNK)
-                for bank in banks:
-                    if first == CHUNK * bank[0]:
-                        finish(*bank, nc.vector.tensor_copy if bank == banks[-2] else nc.scalar.copy)
+
+        def close_sums(first):
+            quantise_z(1, first, first + CHUNK)
+            for bank in banks:
+                if first == CHUNK * bank[0]:
+                    finish(*bank, nc.vector.tensor_copy if bank == banks[-2] else nc.scalar.copy)
+
+        last = PAIRS - CHUNK
+        product(0, 0, RANGE, LAST_H + 20 * KIB)
+        product(0, RANGE, last, LAST_H)
+        open_sums(0, RANGE)
+        open_sums(RANGE, last)
+        for first in (0, CHUNK):
+            product(1, first, first + CHUNK)
+        for first in (0, CHUNK):
+            close_sums(first)
+        product(1, RANGE, last)
+        product(0, last, PAIRS, LAST_ROOT)
+        close_sums(RANGE)
+        product(1, last, PAIRS)
+        open_sums(last, PAIRS)
+        close_sums(last)

@@ -61,7 +61,7 @@ def tile_list_robust_station_increments_kernel(
         w4_scale_tile = sbuf("w4_scale_tile", [P, 2, N // 4], I32)
         gain_tile = sbuf("gain_tile", [P, 2, PACK], F32)
 
-        nc.vector.memset(table_scales[:], 0)
+        nc.gpsimd.memset(table_scales[:], 0)
         nc.vector.memset(carried_scales[:], 0)
         nc.vector.memset(w4_scale_tile[:], 0)
 
@@ -278,7 +278,8 @@ def tile_list_robust_station_increments_kernel(
             result = sbuf(f"result{chunk}{first_tile}", [P, end_tile - first_tile, CHUNK], F32)
             copy(out=result[:], in_=out_acc[chunk, first_tile][:])
             cols = slice(CHUNK * chunk, CHUNK * (chunk + 1))
-            nc.sync.dma_start(out=out_by_tile[:, first_tile:end_tile, cols], in_=result[:])
+            queue = nc.scalar if first_tile > 0 else nc.sync
+            queue.dma_start(out=out_by_tile[:, first_tile:end_tile, cols], in_=result[:])
 
         def gather_words(a):
             nc.vector.tensor_copy(out=v_words[a][:], in_=table_words[a][:].bitcast(U32).indirect(idx_list[:]))

@@ -66,7 +66,11 @@ def tile_list_robust_station_increments_kernel(
         nc.vector.memset(w4_scale_tile[:], 0)
 
         w1_raw = {}
-        departure = [sbuf(f"departure{b}", [P, PACK, PAIRS], F32) for b in range(2)]
+        departure1_weight0 = sbuf("departure1_weight0", [P, 2 * PACK * PAIRS - CHUNK], F32)
+        departure = [
+            sbuf("departure0", [P, PACK, PAIRS], F32),
+            departure1_weight0[:, : PACK * PAIRS].rearrange("p (t c) -> p t c", t=PACK),
+        ]
         picked = {(1, 2): sbuf("picked12", [P, PAIRS], F32)}
 
         def load_w1(b, a, first, width, offset=None):
@@ -192,7 +196,10 @@ def tile_list_robust_station_increments_kernel(
                 else:
                     nc.scalar.activation(h[b, t][:, cols], h_acc[b, t, bank][:], ACT.Copy, scale=row_sign)
 
-        weight = [sbuf(f"weight{b}", [P, PACK, PAIRS], F32) for b in range(2)]
+        weight = [
+            departure1_weight0[:, PACK * PAIRS - CHUNK :].rearrange("p (t c) -> p t c", t=PACK),
+            sbuf("weight1", [P, PACK, PAIRS], F32),
+        ]
 
         def pick(b, t):
             if (b, t) not in picked:
@@ -236,14 +243,19 @@ def tile_list_robust_station_increments_kernel(
         z_rounded = {}
 
         def product(b, first, end, offset=None):
-            rounded = sbuf(f"z_rounded{b}_{first}", [P, PACK * (end - first)], BF16, offset)
+            if (b, first) == (0, RANGE):
+                rounded = weight[1][:, 0, :RANGE].bitcast(BF16)
+            else:
+                rounded = sbuf(f"z_rounded{b}_{first}", [P, PACK * (end - first)], BF16, offset)
             z_rounded[b, first] = rounded
-            nc.vector.tensor_tensor(
-                rounded[:].rearrange("p (c i t) -> p c t i", i=4, t=PACK),
-                departure[b][:, :, first:end].rearrange("p t (c i) -> p c t i", i=4),
-                weight[b][:, :, first:end].rearrange("p t (c i) -> p c t i", i=4),
-                ALU.mult,
-            )
+            for start in range(first, end, CHUNK):
+                cols = slice(PACK * (start - first), PACK * (start - first + CHUNK))
+                nc.vector.tensor_tensor(
+                    rounded[:, cols].rearrange("p (c i t) -> p c t i", i=4, t=PACK),
+                    departure[b][:, :, start : start + CHUNK].rearrange("p t (c i) -> p c t i", i=4),
+                    weight[b][:, :, start : start + CHUNK].rearrange("p t (c i) -> p c t i", i=4),
+                    ALU.mult,
+                )
 
         def quantise_z(b, first, end):
             words = sbuf(f"z_words{b}_{first}", [P, end - first], U32)
@@ -278,7 +290,7 @@ def tile_list_robust_station_increments_kernel(
             result = sbuf(f"result{chunk}{first_tile}", [P, end_tile - first_tile, CHUNK], F32)
             copy(out=result[:], in_=out_acc[chunk, first_tile][:])
             cols = slice(CHUNK * chunk, CHUNK * (chunk + 1))
-            queue = nc.scalar if first_tile > 0 else nc.sync
+            queue = nc.scalar if (chunk, end_tile) == (CHUNKS - 1, out_tiles) else nc.sync
             queue.dma_start(out=out_by_tile[:, first_tile:end_tile, cols], in_=result[:])
 
         def gather_words(a):
@@ -351,12 +363,15 @@ def tile_list_robust_station_increments_kernel(
         influence(1, 1, on_gpsimd=True)
         pick(1, 2)
         pick(1, 3)
-        for first in range(0, PAIRS, RANGE):
-            for t in range(2, PACK):
-                influence(1, t, first, first + RANGE)
+        for t in range(2, PACK):
+            influence(1, t, 0, RANGE)
+        influence(1, 2, RANGE, PAIRS)
+        product(0, 0, RANGE)
+        influence(1, 3, RANGE, PAIRS)
 
-        banks = [(chunk, 0, out_tiles) for chunk in range(CHUNKS - 1)]
-        banks.extend([(CHUNKS - 1, 0, out_tiles // 2), (CHUNKS - 1, out_tiles // 2, out_tiles)])
+        banks = [(chunk, 0, out_tiles) for chunk in range(CHUNKS // 2)]
+        for chunk in range(CHUNKS // 2, CHUNKS):
+            banks.extend([(chunk, 0, out_tiles // 2), (chunk, out_tiles // 2, out_tiles)])
 
         def open_sums(first, end):
             quantise_z(0, first, end)
@@ -371,15 +386,14 @@ def tile_list_robust_station_increments_kernel(
                     finish(*bank, nc.vector.tensor_copy if bank == banks[-2] else nc.scalar.copy)
 
         last = PAIRS - CHUNK
-        product(0, 0, RANGE, LAST_H + 20 * KIB)
-        product(0, RANGE, last, LAST_H)
         open_sums(0, RANGE)
-        open_sums(RANGE, last)
         for first in (0, CHUNK):
             product(1, first, first + CHUNK)
         for first in (0, CHUNK):
             close_sums(first)
+        product(0, RANGE, last)
         product(1, RANGE, last)
+        open_sums(RANGE, last)
         product(0, last, PAIRS, LAST_ROOT)
         close_sums(RANGE)
         product(1, last, PAIRS)

from contextlib import ExitStack

import concourse.mybir as mybir

K, T, S, PAIRS, H, N = 1024, 2048, 1024, 512, 1024, 512
FLOPS = 2 * K * H * S + 2 * H * N * PAIRS

F32 = mybir.dt.float32
BF16 = mybir.dt.bfloat16
I32 = mybir.dt.int32
U32 = mybir.dt.uint32
U16 = mybir.dt.uint16
U8 = mybir.dt.uint8
FP8X4 = mybir.dt.float8_e4m3fn_x4
FP4X4 = mybir.dt.float4_e2m1fn_x4
ALU = mybir.AluOpType
ACT = mybir.ActivationFunctionType

P = 128
PACK = 4
PASS = P * PACK
BANK = 512
HALF = PASS // 2
CHUNK = 128
CHUNKS = PAIRS // CHUNK
RANGE = PAIRS // 2
SMALLEST = 2.0**-126
SCALAR_SHARE = 22

KIB = 1024
ROUNDED = 0
RAW11 = 20 * KIB
LAST_H = 32 * KIB
LAST_ROOT = 36 * KIB


def tile_list_robust_station_increments_kernel(
    tc, tab_words, tab_scales, offs, pos1, pos2, w1, gain, w4_words, w4_scales, out
):
    nc = tc.nc
    with ExitStack() as ctx:
        keep = ctx.enter_context(tc.tile_pool(name="keep", bufs=1))
        shared = ctx.enter_context(tc.tile_pool(name="shared", bufs=1))
        psum = ctx.enter_context(tc.psum_pool(name="psum", bufs=8))

        def sbuf(name, shape, dtype, offset=None):
            if offset is None:
                return keep.tile(shape, dtype, name=name, align_bytes=64)
            return shared.tile(shape, dtype, name=name, align_bytes=64, offset=offset)

        idx_list = keep.tile([P, S // 16], U16, name="idx_list")
        p1_list = keep.tile([P, PAIRS // 16], U16, name="p1_list")
        p2_list = keep.tile([P, PAIRS // 16], U16, name="p2_list")
        table_words = [sbuf(f"table_words{a}", [P, T], I32) for a in range(2)]
        table_scales = sbuf("table_scales", [P, T // 4], I32)
        v_words = [sbuf(f"v_words{a}", [P, S], U32) for a in range(2)]
        picked_scales = sbuf("picked_scales", [P, S], U8)
        carried_scales = sbuf("carried_scales", [P, S // 4], I32)
        v_scales = (picked_scales[:], carried_scales[:].bitcast(U8))
        w4_word_tile = sbuf("w4_word_tile", [P, 2, 2 * N // 4], I32)
        w4_scale_tile = sbuf("w4_scale_tile", [P, 2, N // 4], I32)
        gain_tile = sbuf("gain_tile", [P, 2, PACK], F32)

        nc.gpsimd.memset(table_scales[:], 0)
        nc.vector.memset(carried_scales[:], 0)
        nc.vector.memset(w4_scale_tile[:], 0)

        w1_raw = {}
        departure1_weight0 = sbuf("departure1_weight0", [P, 2 * PACK * PAIRS - CHUNK], F32)
        departure = [
            sbuf("departure0", [P, PACK, PAIRS], F32),
            departure1_weight0[:, : PACK * PAIRS].rearrange("p (t c) -> p t c", t=PACK),
        ]
        picked = {(1, 2): sbuf("picked12", [P, PAIRS], F32)}

        def load_w1(b, a, first, width, offset=None):
            if (b, a, first) == (1, 0, HALF):
                raw = departure[0][:, :2, :].rearrange("p t (j c) -> p (t j) c", c=HALF)
            else:
                raw = sbuf(f"w1_raw{b}{a}{first}", [P, PACK, width], F32, offset)
            rows = w1[PASS * a : PASS * (a + 1), PASS * b + first : PASS * b + first + width]
            nc.sync.dma_start(out=raw[:], in_=rows.rearrange("(p j) c -> p j c", j=PACK))
            for start in range(0, width, HALF):
                w1_raw[b, a, (first + start) // HALF] = raw[:, :, start : start + HALF]

        def load_table_words(a):
            nc.sync.dma_start(out=table_words[a][:], in_=tab_words[a].rearrange("p t i -> p (t i)").bitcast(I32))

        nc.scalar.dma_start(out=gain_tile[:], in_=gain.rearrange("(b p t) -> p b t", b=2, t=PACK))
        nc.sync.dma_start(idx_list[:], offs)
        nc.sync.dma_start(p2_list[:], pos2)
        scale_rows = tab_scales.bitcast(I32).rearrange("a (q r) c -> r q a c", r=4)
        for r in range(4):
            nc.sync.dma_start(out=table_scales[r:P:16, :], in_=scale_rows[r])
        load_table_words(0)
        load_w1(0, 0, 0, PASS)
        load_table_words(1)
        load_w1(0, 1, 0, HALF)
        load_w1(0, 1, HALF, HALF)
        nc.sync.dma_start(p1_list[:], pos1)
        load_w1(1, 0, 0, HALF)
        load_w1(1, 0, HALF, HALF)
        load_w1(1, 1, 0, PASS, RAW11)
        nc.sync.dma_start(out=w4_word_tile[:], in_=w4_words.bitcast(I32).rearrange("b p c -> p b c"))
        for quad in range(4):
            nc.sync.dma_start(
                out=w4_scale_tile[32 * quad : 32 * quad + 4, :, :],
                in_=w4_scales.bitcast(I32)[:, 4 * quad : 4 * quad + 4, :].rearrange("b i c -> i b c"),
            )


        size, inverse_root, inverse, sign = (
            sbuf(f"gain_{name}", [P, 2, PACK], F32) for name in ("size", "inverse_root", "inverse", "sign")
        )
        last_step = sbuf("last_step", [P, RANGE + 1], F32, LAST_ROOT)
        last_inverse = last_step[:, RANGE:]
        nc.vector.scalar_tensor_tensor(size[:], gain_tile[:], -1.0, gain_tile[:], ALU.mult, ALU.max)
        nc.scalar.activation(inverse_root[:], size[:], ACT.Abs_reciprocal_sqrt, bias=SMALLEST)
        nc.scalar.activation(inverse[:], inverse_root[:], ACT.Square)
        nc.gpsimd.tensor_tensor(last_inverse, inverse_root[:, 1, 3:4], inverse_root[:, 1, 3:4], ALU.mult)
        early_inverse = {(0, t): departure[0][:, 2 + t, 0:1] for t in range(2)}
        for (b, t), column in early_inverse.items():
            nc.scalar.activation(column, inverse_root[:, b, t : t + 1], ACT.Square)
        late_sign = {1: departure[1][:, 0, 0:1], 3: picked[1, 2][:, 0:1]}
        for t, column in late_sign.items():
            nc.scalar.activation(column, gain_tile[:, 1, t : t + 1], ACT.Sign, scale=inverse_root[:, 1, t : t + 1])
        for b, t in ((0, 0), (0, 1), (0, 2), (0, 3), (1, 0), (1, 2)):
            column = sign[:, b, t : t + 1]
            nc.scalar.activation(column, gain_tile[:, b, t : t + 1], ACT.Sign, scale=inverse_root[:, b, t : t + 1])

        w1_rounded = {}
        w1_words = {}
        w1_scales = {}
        for b in range(2):
            for a in range(2):
                for pair in range(2):
                    late = RAW11 + 6 * KIB + KIB * a if (b, pair) == (1, 1) else None
                    words = sbuf(f"w1_words{b}{a}{pair}", [P, HALF], U32, late)
                    scales = sbuf(f"w1_scales{b}{a}{pair}", [P, HALF], U8)
                    w1_words[b, a, pair], w1_scales[b, a, pair] = words, scales

        def copy_on_gpsimd(dst, src):
            nc.gpsimd.tensor_scalar(dst, src, 1.0, 0.0, ALU.mult, ALU.add)

        def round_w1(b, a, half, copy, first=0, end=HALF // PACK):
            if (b, a) not in w1_rounded:
                area = (a + b + 1) % 2
                w1_rounded[b, a] = sbuf(f"w1_rounded{b}{a}", [P, PACK * PASS], BF16, ROUNDED + 4 * KIB * area)
            by_column = w1_rounded[b, a][:].rearrange("p (t m j) -> p m t j", t=PACK, j=PACK)
            base = HALF // PACK * half
            copy(
                by_column[:, base + first : base + end, :, :],
                w1_raw[b, a, half].rearrange("p j (m t) -> p m t j", t=PACK)[:, first:end, :, :],
            )

        def quantise_w1(b, a, first_slot, end_slot):
            pair = first_slot // 2
            cols = slice(P * (first_slot - 2 * pair), P * (end_slot - 2 * pair))
            nc.vector.quantize_mx(
                out=w1_words[b, a, pair][:, cols].bitcast(FP8X4),
                scales=w1_scales[b, a, pair][:, cols],
                in_=w1_rounded[b, a][:, PASS * first_slot : PASS * end_slot],
            )

        h = {}
        h_acc = {}

        def h_width(b, t):
            return BANK // 2 if (b, t) == (0, 0) else BANK

        def h_pass(b, t, a):
            slot_cols = slice(P * (t % 2), P * (t % 2 + 1))
            width = h_width(b, t)
            for bank in range(S // width):
                cols = slice(width * bank, width * (bank + 1))
                if a == 0:
                    h_acc[b, t, bank] = psum.tile([P, width], F32, name="acc")
                nc.tensor.matmul_mx(
                    out=h_acc[b, t, bank][:],
                    lhsT=w1_words[b, a, t // 2][:, slot_cols].bitcast(FP8X4),
                    lhsT_scale=w1_scales[b, a, t // 2][:, slot_cols],
                    rhs=v_words[a][:, cols].bitcast(FP8X4),
                    rhs_scale=v_scales[a][:, cols],
                    start=(a == 0),
                    stop=(a == 1),
                )

        def fetch_h(b, t):
            h[b, t] = sbuf(f"h{b}{t}", [P, S], F32, {(1, 2): LAST_H + 20 * KIB, (1, 3): LAST_H}.get((b, t)))
            row_sign = late_sign[t] if b == 1 and t % 2 else sign[:, b, t : t + 1]
            width = h_width(b, t)
            for bank in range(S // width):
                cols = slice(width * bank, width * (bank + 1))
                if (b, t) == (0, 0) and bank % 2 == 1:
                    nc.vector.tensor_scalar(h[b, t][:, cols], h_acc[b, t, bank][:], row_sign, None, ALU.mult)
                else:
                    nc.scalar.activation(h[b, t][:, cols], h_acc[b, t, bank][:], ACT.Copy, scale=row_sign)

        weight = [
            departure1_weight0[:, PACK * PAIRS - CHUNK :].rearrange("p (t c) -> p t c", t=PACK),
            sbuf("weight1", [P, PACK, PAIRS], F32),
        ]

        def pick(b, t):
            if (b, t) not in picked:
                picked[b, t] = sbuf(f"picked{b}{t}", [P, PAIRS], F32, RAW11 if (b, t) == (0, PACK - 1) else None)
            nc.vector.tensor_copy(out=picked[b, t][:], in_=h[b, t][:].indirect(p2_list[:]))

        def depart(b, t, first=0, end=PAIRS):
            stations = h[b, t][:].indirect(p1_list[:, first // 16 : end // 16])
            nc.vector.tensor_tensor(departure[b][:, t, first:end], stations, picked[b, t][:, first:end], ALU.subtract)

        shrunk = {}

        def shrink_step(b, t, squared, first=0, end=PAIRS):
            last = (b, t, first) == (1, PACK - 1, RANGE)
            shrink = last_step[:, :RANGE] if last else sbuf(f"shrink{b}{t}_{first}", [P, end - first], F32)
            row = last_inverse if last else inverse[:, b, t : t + 1]
            row = early_inverse.get((b, t), row)
            nc.scalar.activation(shrink[:], squared, ACT.Abs_reciprocal_sqrt, bias=row, scale=row)
            shrunk[b, t] = shrink

        def weight_step(b, t, first=0, end=PAIRS):
            nc.scalar.activation(weight[b][:, t, first:end], shrunk[b, t][:], ACT.Square)

        def weigh(b, t, squared, first=0, end=PAIRS):
            shrink_step(b, t, squared, first, end)
            weight_step(b, t, first, end)

        def influence(b, t, first=0, end=PAIRS, then=weigh, on_gpsimd=False):
            depart(b, t, first, end)
            offset = RAW11 + 2 * KIB * (t + 1) if b == 0 else None
            squared = sbuf(f"squared{b}{t}_{first}", [P, end - first], F32, offset)
            if on_gpsimd:
                nc.gpsimd.tensor_tensor(squared[:], departure[b][:, t, :], departure[b][:, t, :], ALU.mult)
            else:
                nc.scalar.activation(squared[:], departure[b][:, t, first:end], ACT.Square)
            then(b, t, squared[:], first, end)

        z_words = {}
        z_scales = {}

        z_rounded = {}

        def product(b, first, end, offset=None):
            if (b, first) == (0, RANGE):
                rounded = weight[1][:, 0, :RANGE].bitcast(BF16)
            else:
                rounded = sbuf(f"z_rounded{b}_{first}", [P, PACK * (end - first)], BF16, offset)
            z_rounded[b, first] = rounded
            for start in range(first, end, CHUNK):
                cols = slice(PACK * (start - first), PACK * (start - first + CHUNK))
                nc.vector.tensor_tensor(
                    rounded[:, cols].rearrange("p (c i t) -> p c t i", i=4, t=PACK),
                    departure[b][:, :, start : start + CHUNK].rearrange("p t (c i) -> p c t i", i=4),
                    weight[b][:, :, start : start + CHUNK].rearrange("p t (c i) -> p c t i", i=4),
                    ALU.mult,
                )

        def quantise_z(b, first, end):
            words = sbuf(f"z_words{b}_{first}", [P, end - first], U32)
            scales = sbuf(f"z_scales{b}_{first}", [P, end - first], U8)
            nc.vector.quantize_mx(out=words[:].bitcast(FP8X4), scales=scales[:], in_=z_rounded[b, first][:])
            for start in range(0, end - first, CHUNK):
                z_words[b, (first + start) // CHUNK] = words[:, start : start + CHUNK]
                z_scales[b, (first + start) // CHUNK] = scales[:, start : start + CHUNK]

        w4_word_bytes = w4_word_tile[:].bitcast(U8)
        w4_scale_bytes = w4_scale_tile[:].bitcast(U8)
        out_by_tile = out.rearrange("(i q) c -> q i c", q=P)
        out_tiles = N // P
        out_acc = {}

        def out_passes(b, chunk, first_tile, end_tile):
            if b == 0:
                out_acc[chunk, first_tile] = psum.tile([P, end_tile - first_tile, CHUNK], F32, name="acc")
            for i in range(first_tile, end_tile):
                nc.tensor.matmul_mx(
                    out=out_acc[chunk, first_tile][:, i - first_tile, :],
                    lhsT=w4_word_bytes[:, b, 2 * P * i : 2 * P * (i + 1)].bitcast(FP4X4),
                    lhsT_scale=w4_scale_bytes[:, b, P * i : P * (i + 1)],
                    rhs=z_words[b, chunk].bitcast(FP8X4),
                    rhs_scale=z_scales[b, chunk],
                    start=(b == 0 and i == first_tile),
                    stop=(b == 1 and i == end_tile - 1),
                )

        def finish(chunk, first_tile, end_tile, copy):
            out_passes(1, chunk, first_tile, end_tile)
            result = sbuf(f"result{chunk}{first_tile}", [P, end_tile - first_tile, CHUNK], F32)
            copy(out=result[:], in_=out_acc[chunk, first_tile][:])
            cols = slice(CHUNK * chunk, CHUNK * (chunk + 1))
            queue = nc.scalar if (chunk, end_tile) == (CHUNKS - 1, out_tiles) else nc.sync
            queue.dma_start(out=out_by_tile[:, first_tile:end_tile, cols], in_=result[:])

        def gather_words(a):
            nc.vector.tensor_copy(out=v_words[a][:], in_=table_words[a][:].bitcast(U32).indirect(idx_list[:]))

        nc.vector.tensor_copy(out=picked_scales[:], in_=table_scales[:].bitcast(U8).indirect(idx_list[:]))
        for quad in range(4):
            rows = picked_scales[32 * quad + 16 : 32 * quad + 20, :].bitcast(I32)
            nc.scalar.dma_start(out=carried_scales[32 * quad : 32 * quad + 4, :], in_=rows)
        gather_words(0)
        round_w1(0, 0, 0, nc.scalar.copy)
        round_w1(0, 0, 1, nc.vector.tensor_copy)
        quantise_w1(0, 0, 0, 2)
        quantise_w1(0, 0, 2, PACK)
        gather_words(1)
        for t in range(2):
            h_pass(0, t, 0)
        round_w1(0, 1, 0, nc.scalar.copy)
        round_w1(0, 1, 1, nc.scalar.copy, 0, SCALAR_SHARE)
        round_w1(0, 1, 1, nc.vector.tensor_copy, SCALAR_SHARE, HALF // PACK)
        quantise_w1(0, 1, 0, 1)
        h_pass(0, 0, 1)
        fetch_h(0, 0)
        quantise_w1(0, 1, 1, 2)
        quantise_w1(0, 1, 2, PACK)
        h_pass(0, 1, 1)
        fetch_h(0, 1)
        for t in range(2, PACK):
            h_pass(0, t, 0)
            h_pass(0, t, 1)
            fetch_h(0, t)
        for half in range(2):
            round_w1(1, 0, half, copy_on_gpsimd)
        round_w1(1, 1, 0, nc.scalar.copy)
        round_w1(1, 1, 1, nc.scalar.copy)
        for t in range(PACK - 1):
            pick(0, t)
        influence(0, 0, then=shrink_step)
        quantise_w1(1, 0, 0, 2)
        for t in range(2):
            h_pass(1, t, 0)
        influence(0, 1, then=shrink_step)
        quantise_w1(1, 1, 0, 2)
        for t in range(2):
            h_pass(1, t, 1)
        fetch_h(1, 0)
        fetch_h(1, 1)
        weight_step(0, 0)
        weight_step(0, 1)
        pick(0, 3)
        for a in range(2):
            quantise_w1(1, a, 2, PACK)
        for t in range(2, PACK):
            h_pass(1, t, 0)
            h_pass(1, t, 1)
        depart(0, 2)
        depart(0, 3)
        last_squares = sbuf("last_squares", [P, 2, PAIRS], F32)
        flat_squares = last_squares[:].rearrange("p t c -> p (t c)")
        flat_departure = departure[0][:, 2:, :].rearrange("p t c -> p (t c)")
        nc.gpsimd.tensor_tensor(flat_squares[:, RANGE:], flat_departure[:, RANGE:], flat_departure[:, RANGE:], ALU.mult)
        fetch_h(1, 2)
        nc.scalar.activation(flat_squares[:, :RANGE], flat_departure[:, :RANGE], ACT.Square)
        fetch_h(1, 3)
        for t in range(2, PACK):
            weigh(0, t, last_squares[:, t - 2, :])
        pick(1, 0)
        pick(1, 1)
        influence(1, 0)
        influence(1, 1, on_gpsimd=True)
        pick(1, 2)
        pick(1, 3)
        for t in range(2, PACK):
            influence(1, t, 0, RANGE)
        influence(1, 2, RANGE, PAIRS)
        product(0, 0, RANGE)
        influence(1, 3, RANGE, PAIRS)

        banks = [(chunk, 0, out_tiles) for chunk in range(CHUNKS // 2)]
        for chunk in range(CHUNKS // 2, CHUNKS):
            banks.extend([(chunk, 0, out_tiles // 2), (chunk, out_tiles // 2, out_tiles)])

        def open_sums(first, end):
            quantise_z(0, first, end)
            for bank in banks:
                if first <= CHUNK * bank[0] < end:
                    out_passes(0, *bank)

        def close_sums(first):
            quantise_z(1, first, first + CHUNK)
            for bank in banks:
                if first == CHUNK * bank[0]:
                    finish(*bank, nc.vector.tensor_copy if bank == banks[-2] else nc.scalar.copy)

        last = PAIRS - CHUNK
        open_sums(0, RANGE)
        for first in (0, CHUNK):
            product(1, first, first + CHUNK)
        for first in (0, CHUNK):
            close_sums(first)
        product(0, RANGE, last)
        product(1, RANGE, last)
        open_sums(RANGE, last)
        product(0, last, PAIRS, LAST_ROOT)
        close_sums(RANGE)
        product(1, last, PAIRS)
        open_sums(last, PAIRS)
        close_sums(last)
